import numpy as np
import ml_dtypes


def mxq(x, axis, fmt="e4m3"):
    dtype, down = {"e4m3": (ml_dtypes.float8_e4m3fn, 7), "e5m2": (ml_dtypes.float8_e5m2, 14)}[fmt]
    v = np.moveaxis(np.asarray(x, np.float32).astype(ml_dtypes.bfloat16).astype(np.float64), axis, -1)
    blocks = v.reshape(v.shape[:-1] + (-1, 32))
    amax = np.abs(blocks).max(-1, keepdims=True)
    byte = np.maximum(np.where(amax > 0, np.frexp(amax)[1] - 1 + 127, 0) - down, 1)
    scale = np.exp2(byte - 127.0)
    codes = (blocks / scale).astype(np.float32).astype(dtype).astype(np.float64)
    return np.moveaxis((codes * scale).reshape(v.shape), -1, axis)


WIDE = False


def mx_kscale(k):
    if not WIDE:
        return np.ones(k)
    levels = np.array([10, -10, 5, -5, 0])
    if k % 512:
        return np.exp2(np.random.permutation(np.resize(levels, k // 32))).repeat(32)
    a = np.empty((k // 512, 16))
    for p in range(k // 512):
        a[p, :8] = np.random.permutation(np.resize(levels, 8))
        for g in range(8):
            far = levels[np.abs(levels - a[p, g]) >= 10]
            a[p, g + 8] = far[np.random.randint(len(far))]
    return np.exp2(a.ravel()).repeat(32)


def f64(x):
    return np.asarray(x).astype(np.float64)


def striped(idx):
    return np.tile(idx.reshape(-1, 16).T, (8, 1)).astype(np.uint16)


def unstriped(offs):
    return offs[:16].T.reshape(-1).astype(np.int64)


E2M1 = np.array([0.0, 0.5, 1.0, 1.5, 2.0, 3.0, 4.0, 6.0, -0.0, -0.5, -1.0, -1.5, -2.0, -3.0, -4.0, -6.0])


def pack_weight(w, fmt):
    k, n = w.shape
    w = f64(np.asarray(w, np.float32).astype(ml_dtypes.bfloat16)).reshape(k // 32, 32, n)
    amax = np.abs(w).max(1)
    if fmt == "e4m3":
        byte = np.frexp(amax)[1] - 1 + 127 - 7
    else:
        mant, ex = np.frexp(amax / 6.0)
        byte = np.where(mant > 0.5, ex, ex - 1) + 127
    byte = np.clip(np.where(amax > 0, byte, 1), 1, 254)
    scaled = (w * np.exp2(127.0 - byte)[:, None, :]).reshape(k, n).astype(np.float32)
    by_word = np.ascontiguousarray(scaled.reshape(k // 512, 128, 4, n).transpose(0, 1, 3, 2))
    if fmt == "e4m3":
        words = by_word.astype(ml_dtypes.float8_e4m3fn).view(np.uint8)
    else:
        c = by_word.astype(ml_dtypes.float4_e2m1fn).view(np.uint8) & 0xF
        words = (c[..., 0::2] | (c[..., 1::2] << 4)).reshape(k // 512, 128, 2 * n)
    return np.ascontiguousarray(words), np.ascontiguousarray(byte.astype(np.uint8).reshape(k // 512, 16, n))


def unpack_weight(words, scales, fmt):
    g, _, n = scales.shape
    words = np.ascontiguousarray(words).reshape(g, 128, n, -1)
    if fmt == "e4m3":
        vals = words.view(ml_dtypes.float8_e4m3fn).astype(np.float64)
    else:
        nib = np.empty((g, 128, n, 4), np.uint8)
        nib[..., 0::2] = words & 0xF
        nib[..., 1::2] = words >> 4
        vals = E2M1[nib]
    vals = vals * np.repeat(np.exp2(scales.astype(np.float64) - 127.0), 8, axis=1)[..., None]
    return vals.transpose(0, 1, 3, 2).reshape(g * 512, n)


def gelu(v):
    return 0.5 * v * (1.0 + np.tanh(np.sqrt(2.0 / np.pi) * (v + 0.044715 * v**3)))


def bf(x):
    return np.asarray(x, np.float32).astype(ml_dtypes.bfloat16)

def planes(Y):
    n, m = Y.shape
    b = f64(bf(Y)).reshape(n // 32, 32, m)
    amax = np.abs(b).max(1)
    byte = np.clip(np.where(amax > 0, np.frexp(amax)[1] - 1 + 127 - 7, 1), 1, 254)
    codes = (b * np.exp2(127.0 - byte)[:, None, :]).reshape(n, m).astype(np.float32).astype(ml_dtypes.float8_e4m3fn).view(np.uint8)
    words = codes.reshape(n // 512, 128, 4, m).transpose(0, 1, 3, 2)
    return np.ascontiguousarray(words), np.ascontiguousarray(byte.astype(np.uint8).reshape(n // 512, 16, m))


K, T, S, T2, S2, N = 1024, 2048, 1024, 4096, 1024, 512


def setup_inputs():
    n = np.random.standard_normal
    s = mx_kscale(K)[:, None]
    u = mx_kscale(S)[:, None]
    tab_words, tab_scales = pack_weight(n((K, T)) * s, "e4m3")
    tab2_words, tab2_scales = pack_weight(n((K, T2)) / s / np.sqrt(K), "e4m3")
    gain = np.exp(0.8 * n(N))[None, :]
    wa = n((S, N)) * gain / np.sqrt(S) / u
    wb_words, wb_scales = pack_weight(n((S, N)) * gain / np.sqrt(S) / u, "e2m1")
    return {
        "tab_words": tab_words, "tab_scales": tab_scales,
        "tab2_words": tab2_words, "tab2_scales": tab2_scales,
        "offs": striped(np.random.permutation(T)[:S]),
        "offs2": striped(np.random.permutation(T2)[:S2]),
        "tw": (np.exp(0.3 * n(S)) * u[:, 0]).astype(np.float32),
        "wa": wa.astype(np.float32),
        "wb_words": wb_words, "wb_scales": wb_scales,
    }


def reference(tab_words, tab_scales, tab2_words, tab2_scales, offs, offs2, tw, wa, wb_words, wb_scales):
    v = unpack_weight(tab_words, tab_scales, "e4m3")[:, unstriped(offs)]
    v2 = unpack_weight(tab2_words, tab2_scales, "e4m3")[:, unstriped(offs2)]
    a = v.T @ v2
    h = np.tanh(a) * f64(tw)[:, None]
    hq = mxq(h, 0, "e4m3")
    ya = mxq(f64(wa), 0, "e4m3").T @ hq
    yb = unpack_weight(wb_words, wb_scales, "e2m1").T @ hq
    y = np.maximum(ya, yb)
    words, scales = planes(y)
    return y, words, scales

@@ -1,0 +1,232 @@
+from contextlib import ExitStack
+
+import concourse.mybir as mybir
+
+K, T, S, T2, S2, N = 1024, 2048, 1024, 4096, 1024, 512
+FLOPS = 2 * K * S * S2 + 2 * 2 * S * N * S2
+
+F32 = mybir.dt.float32
+BF16 = mybir.dt.bfloat16
+I32 = mybir.dt.int32
+U32 = mybir.dt.uint32
+U16 = mybir.dt.uint16
+U8 = mybir.dt.uint8
+FP8X4 = mybir.dt.float8_e4m3fn_x4
+FP4X4 = mybir.dt.float4_e2m1fn_x4
+TANH = mybir.ActivationFunctionType.Tanh
+MULT = mybir.AluOpType.mult
+MAX = mybir.AluOpType.max
+
+P = 128
+PACK = 4
+PASS = P * PACK
+PASSES = 2
+BANK = 512
+HALF = S2 // 2
+FP4_N = 128
+CHUNKS = (256, 256, 256, 128, 128)
+
+
+def tile_list_repurposing_mechanism_max_kernel(
+    tc, tab_words, tab_scales, tab2_words, tab2_scales, offs, offs2, tw, wa, wb_words, wb_scales, out_0, out_1, out_2
+):
+    nc = tc.nc
+    with ExitStack() as ctx:
+        keep = ctx.enter_context(tc.tile_pool(name="keep", bufs=1))
+        ring = ctx.enter_context(tc.tile_pool(name="ring", bufs=3))
+        psum_a = ctx.enter_context(tc.psum_pool(name="psum_a", bufs=4))
+        psum_y = ctx.enter_context(tc.psum_pool(name="psum_y", bufs=2))
+
+        def held(name, shape, dtype, tag=None):
+            return keep.tile(shape, dtype, name=name, tag=tag or name, align_bytes=64)
+
+        def as_words(packed):
+            return packed.rearrange("p t i -> p (t i)").bitcast(I32)
+
+        list_v = held("list_v", [P, S // 16], U16)
+        list_x = held("list_x", [P, S2 // 16], U16)
+        v_table = [held("v_table%d" % k, [P, T], U32) for k in range(PASSES)]
+        x_table = [held("x_table0", [P, T2], U32)]
+        v_table_sc = held("v_table_sc", [P, T], U8)
+        x_table_sc = held("x_table_sc", [P, T2], U8)
+        wb_raw = held("wb_raw", [P, PASSES, 2 * N], U8)
+        wb_raw_sc = held("wb_raw_sc", [P, PASSES, N], U8)
+        tw_sb = held("tw_sb", [P, PASSES, PACK], F32)
+
+        nc.vector.memset(v_table_sc[:].bitcast(I32), 0)
+        nc.vector.memset(x_table_sc[:].bitcast(I32), 0)
+        nc.vector.memset(wb_raw_sc[:].rearrange("p a n -> p (a n)").bitcast(I32), 0)
+
+        nc.sync.dma_start(list_v[:], offs)
+        nc.sync.dma_start(v_table[0][:].bitcast(I32), as_words(tab_words[0]))
+        nc.sync.dma_start(list_x[:], offs2)
+        nc.sync.dma_start(v_table[1][:].bitcast(I32), as_words(tab_words[1]))
+        nc.sync.dma_start(x_table[0][:].bitcast(I32), as_words(tab2_words[0]))
+        nc.sync.dma_start(wb_raw[:].bitcast(I32), wb_words.rearrange("a p b -> p a b").bitcast(I32))
+        for queue, plane, scales in ((nc.scalar, v_table_sc, tab_scales), (nc.gpsimd, x_table_sc, tab2_scales)):
+            for q in range(4):
+                queue.dma_start(
+                    plane[32 * q : 32 * q + 8, :].bitcast(I32), scales[:, 4 * q : 4 * q + 4, :].bitcast(I32)
+                )
+        nc.scalar.dma_start(tw_sb[:], tw.rearrange("(a p t) -> p a t", a=PASSES, t=PACK))
+        for q in range(4):
+            nc.scalar.dma_start(
+                wb_raw_sc[32 * q : 32 * q + 4, :, :].bitcast(I32),
+                wb_scales[:, 4 * q : 4 * q + 4, :].rearrange("a r n -> r a n").bitcast(I32),
+            )
+
+        v_words = [held("v_words%d" % k, [P, S], U32) for k in range(PASSES)]
+        v_picked_sc = held("v_picked_sc", [P, S], U8)
+        v_sc = held("v_sc", [P, S], U8)
+        x_words = [[held("x_words%d_%d" % (k, u), [P, HALF], U32) for u in range(2)] for k in range(PASSES)]
+        x_sc = [held("x_sc%d" % u, [P, HALF], U8) for u in range(2)]
+
+        def gather_v(k):
+            nc.vector.tensor_copy(
+                v_words[k][:].rearrange("p (a t m) -> p a m t", a=PASSES, t=PACK), v_table[k][:].indirect(list_v[:])
+            )
+
+        def half_list(u):
+            return list_x[:, u * (HALF // 16) : (u + 1) * (HALF // 16)]
+
+        gather_v(0)
+        nc.vector.tensor_copy(v_picked_sc[:], v_table_sc[:].indirect(list_v[:]))
+        x_table.append(held("x_table1", [P, T2], U32, tag="v_table_sc"))
+        nc.sync.dma_start(x_table[1][:].bitcast(I32), as_words(tab2_words[1]))
+        gather_v(1)
+        wa_raw = [held("wa_raw%d" % a, [P, PACK, N], F32, tag="v_table%d" % a) for a in range(PASSES)]
+        for a in range(PASSES):
+            nc.sync.dma_start(wa_raw[a][:], wa[a * PASS : (a + 1) * PASS, :].rearrange("(p i) n -> p i n", i=PACK))
+        nc.vector.tensor_copy(
+            v_sc[:].rearrange("p (a t m) -> p a t m", a=PASSES, t=PACK),
+            v_picked_sc[:].rearrange("p (a m t) -> p a t m", a=PASSES, t=PACK),
+        )
+
+        def gather_x(u):
+            nc.vector.tensor_copy(x_sc[u][:], x_table_sc[:].indirect(half_list(u)))
+            for k in range(PASSES):
+                nc.vector.tensor_copy(x_words[k][u][:], x_table[k][:].indirect(half_list(u)))
+
+        gather_x(0)
+        gather_x(1)
+
+        wb_codes = held("wb_codes", [P, PASSES, 2 * N], U8)
+        wb_sc = held("wb_sc", [P, PASSES, N], U8)
+        nc.vector.tensor_copy(
+            wb_codes[:].bitcast(U16).rearrange("p a (t m) -> p a t m", t=PACK),
+            wb_raw[:].bitcast(U16).rearrange("p a (m t) -> p a t m", t=PACK),
+        )
+        nc.vector.tensor_copy(
+            wb_sc[:].rearrange("p a (t m) -> p a t m", t=PACK), wb_raw_sc[:].rearrange("p a (m t) -> p a t m", t=PACK)
+        )
+
+        wa_codes = [held("wa_codes%d" % a, [P, N], U32) for a in range(PASSES)]
+        wa_sc = [held("wa_sc%d" % a, [P, N], U8) for a in range(PASSES)]
+
+        def quantise_wa(a, copy):
+            grouped = held("wa_grouped%d" % a, [P, N * PACK], BF16)
+            dealt = grouped[:].rearrange("p (t m i) -> p m i t", t=PACK, i=PACK)
+            raw = wa_raw[a][:].rearrange("p i (m t) -> p m i t", t=PACK)
+            for m0 in (0, P // 2):
+                copy(dealt[:, m0 : m0 + P // 2], raw[:, m0 : m0 + P // 2])
+            nc.vector.quantize_mx(out=wa_codes[a][:].bitcast(FP8X4), scales=wa_sc[a][:], in_=grouped[:])
+
+        y_codes = held("y_codes", [P, S2], U32)
+        y_sc = held("y_sc", [P, S2], U8)
+        y_rows = out_0.rearrange("(p t) j -> p t j", t=PACK)
+        y_words = as_words(out_1[0])
+
+        def effects(j0, w):
+            per_bank = BANK // w
+            banks = PACK // per_bank
+            u, c0 = divmod(j0, HALF)
+            cols = slice(c0, c0 + w)
+            made = []
+            for a in range(PASSES):
+                th = ring.tile([P, banks, w, per_bank], F32, name="th", align_bytes=64)
+                for b in range(banks):
+                    acc = psum_a.tile([P, per_bank, w], F32, name="acc")
+                    for e in range(per_bank):
+                        i0 = a * PASS + (b * per_bank + e) * P
+                        for k in range(PASSES):
+                            nc.tensor.matmul_mx(
+                                out=acc[:, e, :],
+                                lhsT=v_words[k][:, i0 : i0 + P].bitcast(FP8X4),
+                                lhsT_scale=v_sc[4 * k : P, i0 : i0 + P],
+                                rhs=x_words[k][u][:, cols].bitcast(FP8X4),
+                                rhs_scale=x_sc[u][4 * k : P, cols],
+                                start=(k == 0),
+                                stop=(k == PASSES - 1),
+                            )
+                    nc.scalar.activation(th[:, b], acc[:].rearrange("p e n -> p n e"), TANH)
+                h = ring.tile([P, w * PACK], BF16, name="h", align_bytes=64)
+                weight = tw_sb[:, a : a + 1, :].rearrange("p o (b e) -> p o b e", b=banks)
+                nc.vector.tensor_tensor(
+                    h[:].rearrange("p (n b e) -> p n b e", b=banks, e=per_bank),
+                    th[:].rearrange("p b n e -> p n b e"),
+                    weight.broadcast_to([P, w, banks, per_bank]),
+                    MULT,
+                )
+                h_codes = ring.tile([P, w], U32, name="h_codes%d" % a, align_bytes=64)
+                h_sc = ring.tile([P, w], U8, name="h_sc%d" % a, align_bytes=64)
+                nc.vector.quantize_mx(out=h_codes[:].bitcast(FP8X4), scales=h_sc[:], in_=h[:])
+                made.append((h_codes, h_sc))
+            return made
+
+        def scores(j0, w, made, copy):
+            per_bank = BANK // w
+            banks = PACK // per_bank
+            y = ring.tile([P, PACK, w], F32, name="y", align_bytes=64)
+            for b in range(banks):
+                acc_b = psum_y.tile([P, per_bank, w], F32, name="acc_b")
+                acc_a = psum_y.tile([P, per_bank, w], F32, name="acc_a")
+                for e in range(per_bank):
+                    n0 = (b * per_bank + e) * P
+                    for a in range(PASSES):
+                        nc.tensor.matmul_mx(
+                            out=acc_a[:, e, :],
+                            lhsT=wa_codes[a][:, n0 : n0 + P].bitcast(FP8X4),
+                            lhsT_scale=wa_sc[a][:, n0 : n0 + P],
+                            rhs=made[a][0][:].bitcast(FP8X4),
+                            rhs_scale=made[a][1][:],
+                            start=(a == 0),
+                            stop=(a == PASSES - 1),
+                        )
+                for e in range(per_bank):
+                    n0 = (b * per_bank + e) * P
+                    for c0 in range(0, w, FP4_N):
+                        for a in range(PASSES):
+                            nc.tensor.matmul_mx(
+                                out=acc_b[:, e, c0 : c0 + FP4_N],
+                                lhsT=wb_codes[:, a, 2 * n0 : 2 * (n0 + P)].bitcast(FP4X4),
+                                lhsT_scale=wb_sc[:, a, n0 : n0 + P],
+                                rhs=made[a][0][:, c0 : c0 + FP4_N].bitcast(FP8X4),
+                                rhs_scale=made[a][1][:, c0 : c0 + FP4_N],
+                                start=(a == 0),
+                                stop=(a == PASSES - 1),
+                            )
+                ya = ring.tile([P, per_bank, w], F32, name="ya", align_bytes=64)
+                nc.scalar.copy(ya[:], acc_a[:])
+                nc.vector.tensor_tensor(y[:, b * per_bank : (b + 1) * per_bank, :], acc_b[:], ya[:], MAX)
+            nc.sync.dma_start(y_rows[:, :, j0 : j0 + w], y[:])
+            y16 = ring.tile([P, w * PACK], BF16, name="y16", align_bytes=64)
+            copy(
+                y16[:].rearrange("p (c i t) -> p c t i", i=4, t=PACK),
+                y[:].rearrange("p t (c i) -> p c t i", i=4),
+            )
+            cols = slice(j0, j0 + w)
+            nc.vector.quantize_mx(out=y_codes[:, cols].bitcast(FP8X4), scales=y_sc[:, cols], in_=y16[:])
+            nc.sync.dma_start(y_words[:, cols], y_codes[:, cols].bitcast(I32))
+
+        starts = [sum(CHUNKS[:c]) for c in range(len(CHUNKS))]
+        made = effects(starts[0], CHUNKS[0])
+        quantise_wa(0, nc.scalar.copy)
+        quantise_wa(1, nc.scalar.copy)
+        for c in range(1, len(CHUNKS)):
+            ahead = effects(starts[c], CHUNKS[c])
+            scores(starts[c - 1], CHUNKS[c - 1], made, nc.scalar.copy)
+            made = ahead
+        scores(starts[-1], CHUNKS[-1], made, nc.vector.tensor_copy)
+        for q in range(4):
+            queue = nc.sync if q % 2 == 0 else nc.scalar
+            queue.dma_start(out_2[0, 4 * q : 4 * q + 4, :].bitcast(I32), y_sc[32 * q : 32 * q + 4, :].bitcast(I32))

@@ -46,28 +46,35 @@ def tile_list_repurposing_mechanism_max_kernel(
         list_v = held("list_v", [P, S // 16], U16)
         list_x = held("list_x", [P, S2 // 16], U16)
         v_table = [held("v_table%d" % k, [P, T], U32) for k in range(PASSES)]
-        x_table = [held("x_table0", [P, T2], U32)]
+        x_table = [held("x_table%d" % k, [P, T2], U32) for k in range(PASSES)]
+        wb_raw = held("wb_raw", [P, PASSES, 2 * N], U8)
+        wa_raw = [held("wa_raw%d" % a, [P, PACK, N], F32) for a in range(PASSES)]
         v_table_sc = held("v_table_sc", [P, T], U8)
         x_table_sc = held("x_table_sc", [P, T2], U8)
-        wb_raw = held("wb_raw", [P, PASSES, 2 * N], U8)
         wb_raw_sc = held("wb_raw_sc", [P, PASSES, N], U8)
         tw_sb = held("tw_sb", [P, PASSES, PACK], F32)
 
-        nc.vector.memset(v_table_sc[:].bitcast(I32), 0)
         nc.vector.memset(x_table_sc[:].bitcast(I32), 0)
+        nc.vector.memset(v_table_sc[:].bitcast(I32), 0)
         nc.vector.memset(wb_raw_sc[:].rearrange("p a n -> p (a n)").bitcast(I32), 0)
 
-        nc.sync.dma_start(list_v[:], offs)
-        nc.sync.dma_start(v_table[0][:].bitcast(I32), as_words(tab_words[0]))
-        nc.sync.dma_start(list_x[:], offs2)
-        nc.sync.dma_start(v_table[1][:].bitcast(I32), as_words(tab_words[1]))
-        nc.sync.dma_start(x_table[0][:].bitcast(I32), as_words(tab2_words[0]))
-        nc.sync.dma_start(wb_raw[:].bitcast(I32), wb_words.rearrange("a p b -> p a b").bitcast(I32))
-        for queue, plane, scales in ((nc.scalar, v_table_sc, tab_scales), (nc.gpsimd, x_table_sc, tab2_scales)):
+        def load_scale_rows(queue, plane, scales):
             for q in range(4):
                 queue.dma_start(
                     plane[32 * q : 32 * q + 8, :].bitcast(I32), scales[:, 4 * q : 4 * q + 4, :].bitcast(I32)
                 )
+
+        load_scale_rows(nc.gpsimd, x_table_sc, tab2_scales)
+        load_scale_rows(nc.scalar, v_table_sc, tab_scales)
+        nc.sync.dma_start(list_v[:], offs)
+        nc.sync.dma_start(v_table[0][:].bitcast(I32), as_words(tab_words[0]))
+        nc.sync.dma_start(list_x[:], offs2)
+        nc.sync.dma_start(x_table[0][:].bitcast(I32), as_words(tab2_words[0]))
+        nc.sync.dma_start(v_table[1][:].bitcast(I32), as_words(tab_words[1]))
+        nc.sync.dma_start(x_table[1][:].bitcast(I32), as_words(tab2_words[1]))
+        nc.sync.dma_start(wb_raw[:].bitcast(I32), wb_words.rearrange("a p b -> p a b").bitcast(I32))
+        for a in range(PASSES):
+            nc.sync.dma_start(wa_raw[a][:], wa[a * PASS : (a + 1) * PASS, :].rearrange("(p i) n -> p i n", i=PACK))
         nc.scalar.dma_start(tw_sb[:], tw.rearrange("(a p t) -> p a t", a=PASSES, t=PACK))
         for q in range(4):
             nc.scalar.dma_start(
@@ -78,8 +85,8 @@ def tile_list_repurposing_mechanism_max_kernel(
         v_words = [held("v_words%d" % k, [P, S], U32) for k in range(PASSES)]
         v_picked_sc = held("v_picked_sc", [P, S], U8)
         v_sc = held("v_sc", [P, S], U8)
-        x_words = [[held("x_words%d_%d" % (k, u), [P, HALF], U32) for u in range(2)] for k in range(PASSES)]
-        x_sc = [held("x_sc%d" % u, [P, HALF], U8) for u in range(2)]
+        x_sc = held("x_sc", [P, S2], U8)
+        x_words = {}
 
         def gather_v(k):
             nc.vector.tensor_copy(
@@ -91,34 +98,33 @@ def tile_list_repurposing_mechanism_max_kernel(
 
         gather_v(0)
         nc.vector.tensor_copy(v_picked_sc[:], v_table_sc[:].indirect(list_v[:]))
-        x_table.append(held("x_table1", [P, T2], U32, tag="v_table_sc"))
-        nc.sync.dma_start(x_table[1][:].bitcast(I32), as_words(tab2_words[1]))
-        gather_v(1)
-        wa_raw = [held("wa_raw%d" % a, [P, PACK, N], F32, tag="v_table%d" % a) for a in range(PASSES)]
-        for a in range(PASSES):
-            nc.sync.dma_start(wa_raw[a][:], wa[a * PASS : (a + 1) * PASS, :].rearrange("(p i) n -> p i n", i=PACK))
         nc.vector.tensor_copy(
             v_sc[:].rearrange("p (a t m) -> p a t m", a=PASSES, t=PACK),
             v_picked_sc[:].rearrange("p (a m t) -> p a t m", a=PASSES, t=PACK),
         )
 
-        def gather_x(u):
-            nc.vector.tensor_copy(x_sc[u][:], x_table_sc[:].indirect(half_list(u)))
-            for k in range(PASSES):
-                nc.vector.tensor_copy(x_words[k][u][:], x_table[k][:].indirect(half_list(u)))
 
-        gather_x(0)
-        gather_x(1)
+        def gather_x(k, u, tag=None):
+            x_words[k, u] = held("x_words%d_%d" % (k, u), [P, HALF], U32, tag=tag)
+            nc.vector.tensor_copy(x_words[k, u][:], x_table[k][:].indirect(half_list(u)))
 
-        wb_codes = held("wb_codes", [P, PASSES, 2 * N], U8)
-        wb_sc = held("wb_sc", [P, PASSES, N], U8)
+        nc.vector.tensor_copy(x_sc[:], x_table_sc[:].indirect(list_x[:]))
+        gather_x(0, 0)
+        gather_v(1)
+        gather_x(1, 0)
+        gather_x(1, 1)
+
+        wb_codes = held("wb_codes", [P, PASSES, 2 * N], U8, tag="x_table1")
         nc.vector.tensor_copy(
             wb_codes[:].bitcast(U16).rearrange("p a (t m) -> p a t m", t=PACK),
             wb_raw[:].bitcast(U16).rearrange("p a (m t) -> p a t m", t=PACK),
         )
+        gather_x(0, 1, tag="wb_raw")
+        wb_sc = held("wb_sc", [P, PASSES, N], U8, tag="x_table0")
         nc.vector.tensor_copy(
             wb_sc[:].rearrange("p a (t m) -> p a t m", t=PACK), wb_raw_sc[:].rearrange("p a (m t) -> p a t m", t=PACK)
         )
+
 
         wa_codes = [held("wa_codes%d" % a, [P, N], U32) for a in range(PASSES)]
         wa_sc = [held("wa_sc%d" % a, [P, N], U8) for a in range(PASSES)]
@@ -141,25 +147,25 @@ def tile_list_repurposing_mechanism_max_kernel(
             banks = PACK // per_bank
             u, c0 = divmod(j0, HALF)
             cols = slice(c0, c0 + w)
-            made = []
+            rounded = []
             for a in range(PASSES):
-                th = ring.tile([P, banks, w, per_bank], F32, name="th", align_bytes=64)
+                th = ring.tile([P, banks, w, per_bank], F32, name="th", align_bytes=64, bufs=4)
                 for b in range(banks):
                     acc = psum_a.tile([P, per_bank, w], F32, name="acc")
-                    for e in range(per_bank):
-                        i0 = a * PASS + (b * per_bank + e) * P
-                        for k in range(PASSES):
+                    for k in range(PASSES):
+                        for e in range(per_bank):
+                            i0 = a * PASS + (b * per_bank + e) * P
                             nc.tensor.matmul_mx(
                                 out=acc[:, e, :],
                                 lhsT=v_words[k][:, i0 : i0 + P].bitcast(FP8X4),
                                 lhsT_scale=v_sc[4 * k : P, i0 : i0 + P],
-                                rhs=x_words[k][u][:, cols].bitcast(FP8X4),
-                                rhs_scale=x_sc[u][4 * k : P, cols],
-                                start=(k == 0),
-                                stop=(k == PASSES - 1),
+                                rhs=x_words[k, u][:, cols].bitcast(FP8X4),
+                                rhs_scale=x_sc[4 * k : P, j0 : j0 + w],
+                                start=(k == 0 and e == 0),
+                                stop=(k == PASSES - 1 and e == per_bank - 1),
                             )
                     nc.scalar.activation(th[:, b], acc[:].rearrange("p e n -> p n e"), TANH)
-                h = ring.tile([P, w * PACK], BF16, name="h", align_bytes=64)
+                h = ring.tile([P, w * PACK], BF16, name="h", align_bytes=64, bufs=4)
                 weight = tw_sb[:, a : a + 1, :].rearrange("p o (b e) -> p o b e", b=banks)
                 nc.vector.tensor_tensor(
                     h[:].rearrange("p (n b e) -> p n b e", b=banks, e=per_bank),
@@ -167,6 +173,9 @@ def tile_list_repurposing_mechanism_max_kernel(
                     weight.broadcast_to([P, w, banks, per_bank]),
                     MULT,
                 )
+                rounded.append(h)
+            made = []
+            for a, h in enumerate(rounded):
                 h_codes = ring.tile([P, w], U32, name="h_codes%d" % a, align_bytes=64)
                 h_sc = ring.tile([P, w], U8, name="h_sc%d" % a, align_bytes=64)
                 nc.vector.quantize_mx(out=h_codes[:].bitcast(FP8X4), scales=h_sc[:], in_=h[:])

@@ -54,8 +54,8 @@ def tile_list_repurposing_mechanism_max_kernel(
         wb_raw_sc = held("wb_raw_sc", [P, PASSES, N], U8)
         tw_sb = held("tw_sb", [P, PASSES, PACK], F32)
 
-        nc.vector.memset(x_table_sc[:].bitcast(I32), 0)
         nc.vector.memset(v_table_sc[:].bitcast(I32), 0)
+        nc.vector.memset(x_table_sc[:].bitcast(I32), 0)
         nc.vector.memset(wb_raw_sc[:].rearrange("p a n -> p (a n)").bitcast(I32), 0)
 
         def load_scale_rows(queue, plane, scales):
@@ -64,17 +64,20 @@ def tile_list_repurposing_mechanism_max_kernel(
                     plane[32 * q : 32 * q + 8, :].bitcast(I32), scales[:, 4 * q : 4 * q + 4, :].bitcast(I32)
                 )
 
+        def load_wa(a):
+            nc.sync.dma_start(wa_raw[a][:], wa[a * PASS : (a + 1) * PASS, :].rearrange("(p i) n -> p i n", i=PACK))
+
         load_scale_rows(nc.gpsimd, x_table_sc, tab2_scales)
         load_scale_rows(nc.scalar, v_table_sc, tab_scales)
         nc.sync.dma_start(list_v[:], offs)
         nc.sync.dma_start(v_table[0][:].bitcast(I32), as_words(tab_words[0]))
         nc.sync.dma_start(list_x[:], offs2)
         nc.sync.dma_start(x_table[0][:].bitcast(I32), as_words(tab2_words[0]))
+        nc.sync.dma_start(wb_raw[:].bitcast(I32), wb_words.rearrange("a p b -> p a b").bitcast(I32))
+        load_wa(0)
         nc.sync.dma_start(v_table[1][:].bitcast(I32), as_words(tab_words[1]))
         nc.sync.dma_start(x_table[1][:].bitcast(I32), as_words(tab2_words[1]))
-        nc.sync.dma_start(wb_raw[:].bitcast(I32), wb_words.rearrange("a p b -> p a b").bitcast(I32))
-        for a in range(PASSES):
-            nc.sync.dma_start(wa_raw[a][:], wa[a * PASS : (a + 1) * PASS, :].rearrange("(p i) n -> p i n", i=PACK))
+        load_wa(1)
         nc.scalar.dma_start(tw_sb[:], tw.rearrange("(a p t) -> p a t", a=PASSES, t=PACK))
         for q in range(4):
             nc.scalar.dma_start(
@@ -104,38 +107,39 @@ def tile_list_repurposing_mechanism_max_kernel(
         )
 
 
-        def gather_x(k, u, tag=None):
-            x_words[k, u] = held("x_words%d_%d" % (k, u), [P, HALF], U32, tag=tag)
+        def gather_x(k, u):
+            x_words[k, u] = held("x_words%d_%d" % (k, u), [P, HALF], U32)
             nc.vector.tensor_copy(x_words[k, u][:], x_table[k][:].indirect(half_list(u)))
 
         nc.vector.tensor_copy(x_sc[:], x_table_sc[:].indirect(list_x[:]))
         gather_x(0, 0)
-        gather_v(1)
-        gather_x(1, 0)
-        gather_x(1, 1)
+        gather_x(0, 1)
 
-        wb_codes = held("wb_codes", [P, PASSES, 2 * N], U8, tag="x_table1")
+        wb_codes = held("wb_codes", [P, PASSES, 2 * N], U8)
         nc.vector.tensor_copy(
             wb_codes[:].bitcast(U16).rearrange("p a (t m) -> p a t m", t=PACK),
             wb_raw[:].bitcast(U16).rearrange("p a (m t) -> p a t m", t=PACK),
         )
-        gather_x(0, 1, tag="wb_raw")
-        wb_sc = held("wb_sc", [P, PASSES, N], U8, tag="x_table0")
+        wb_sc = held("wb_sc", [P, PASSES, N], U8)
         nc.vector.tensor_copy(
             wb_sc[:].rearrange("p a (t m) -> p a t m", t=PACK), wb_raw_sc[:].rearrange("p a (m t) -> p a t m", t=PACK)
         )
 
-
         wa_codes = [held("wa_codes%d" % a, [P, N], U32) for a in range(PASSES)]
         wa_sc = [held("wa_sc%d" % a, [P, N], U8) for a in range(PASSES)]
 
-        def quantise_wa(a, copy):
+        def quantise_wa(a):
             grouped = held("wa_grouped%d" % a, [P, N * PACK], BF16)
             dealt = grouped[:].rearrange("p (t m i) -> p m i t", t=PACK, i=PACK)
             raw = wa_raw[a][:].rearrange("p i (m t) -> p m i t", t=PACK)
             for m0 in (0, P // 2):
-                copy(dealt[:, m0 : m0 + P // 2], raw[:, m0 : m0 + P // 2])
+                nc.scalar.copy(dealt[:, m0 : m0 + P // 2], raw[:, m0 : m0 + P // 2])
             nc.vector.quantize_mx(out=wa_codes[a][:].bitcast(FP8X4), scales=wa_sc[a][:], in_=grouped[:])
+
+        gather_v(1)
+        quantise_wa(0)
+        gather_x(1, 0)
+        gather_x(1, 1)
 
         y_codes = held("y_codes", [P, S2], U32)
         y_sc = held("y_sc", [P, S2], U8)
@@ -143,34 +147,30 @@ def tile_list_repurposing_mechanism_max_kernel(
         y_words = as_words(out_1[0])
 
         def effects(j0, w):
-            per_bank = BANK // w
-            banks = PACK // per_bank
             u, c0 = divmod(j0, HALF)
-            cols = slice(c0, c0 + w)
             rounded = []
             for a in range(PASSES):
-                th = ring.tile([P, banks, w, per_bank], F32, name="th", align_bytes=64, bufs=4)
-                for b in range(banks):
-                    acc = psum_a.tile([P, per_bank, w], F32, name="acc")
+                th = ring.tile([P, w, PACK], F32, name="th", align_bytes=64, bufs=4)
+                for b0 in range(0, w, P):
+                    acc = psum_a.tile([P, PACK, P], F32, name="acc")
                     for k in range(PASSES):
-                        for e in range(per_bank):
-                            i0 = a * PASS + (b * per_bank + e) * P
+                        for t in range(PACK):
+                            i0 = a * PASS + t * P
                             nc.tensor.matmul_mx(
-                                out=acc[:, e, :],
+                                out=acc[:, t, :],
                                 lhsT=v_words[k][:, i0 : i0 + P].bitcast(FP8X4),
                                 lhsT_scale=v_sc[4 * k : P, i0 : i0 + P],
-                                rhs=x_words[k, u][:, cols].bitcast(FP8X4),
-                                rhs_scale=x_sc[4 * k : P, j0 : j0 + w],
-                                start=(k == 0 and e == 0),
-                                stop=(k == PASSES - 1 and e == per_bank - 1),
+                                rhs=x_words[k, u][:, c0 + b0 : c0 + b0 + P].bitcast(FP8X4),
+                                rhs_scale=x_sc[4 * k : P, j0 + b0 : j0 + b0 + P],
+                                start=(k == 0 and t == 0),
+                                stop=(k == PASSES - 1 and t == PACK - 1),
                             )
-                    nc.scalar.activation(th[:, b], acc[:].rearrange("p e n -> p n e"), TANH)
+                    nc.scalar.activation(th[:, b0 : b0 + P, :], acc[:].rearrange("p t n -> p n t"), TANH)
                 h = ring.tile([P, w * PACK], BF16, name="h", align_bytes=64, bufs=4)
-                weight = tw_sb[:, a : a + 1, :].rearrange("p o (b e) -> p o b e", b=banks)
                 nc.vector.tensor_tensor(
-                    h[:].rearrange("p (n b e) -> p n b e", b=banks, e=per_bank),
-                    th[:].rearrange("p b n e -> p n b e"),
-                    weight.broadcast_to([P, w, banks, per_bank]),
+                    h[:].rearrange("p (n t) -> p n t", t=PACK),
+                    th[:],
+                    tw_sb[:, a : a + 1, :].broadcast_to([P, w, PACK]),
                     MULT,
                 )
                 rounded.append(h)
@@ -229,8 +229,7 @@ def tile_list_repurposing_mechanism_max_kernel(
 
         starts = [sum(CHUNKS[:c]) for c in range(len(CHUNKS))]
         made = effects(starts[0], CHUNKS[0])
-        quantise_wa(0, nc.scalar.copy)
-        quantise_wa(1, nc.scalar.copy)
+        quantise_wa(1)
         for c in range(1, len(CHUNKS)):
             ahead = effects(starts[c], CHUNKS[c])
             scores(starts[c - 1], CHUNKS[c - 1], made, nc.scalar.copy)

@@ -46,9 +46,8 @@ def tile_list_repurposing_mechanism_max_kernel(
         list_v = held("list_v", [P, S // 16], U16)
         list_x = held("list_x", [P, S2 // 16], U16)
         v_table = [held("v_table%d" % k, [P, T], U32) for k in range(PASSES)]
-        x_table = [held("x_table%d" % k, [P, T2], U32) for k in range(PASSES)]
-        wb_raw = held("wb_raw", [P, PASSES, 2 * N], U8)
-        wa_raw = [held("wa_raw%d" % a, [P, PACK, N], F32) for a in range(PASSES)]
+        x_table = [held("x_table0", [P, T2], U32)]
+        wa_raw = []
         v_table_sc = held("v_table_sc", [P, T], U8)
         x_table_sc = held("x_table_sc", [P, T2], U8)
         wb_raw_sc = held("wb_raw_sc", [P, PASSES, N], U8)
@@ -65,6 +64,7 @@ def tile_list_repurposing_mechanism_max_kernel(
                 )
 
         def load_wa(a):
+            wa_raw.append(held("wa_raw%d" % a, [P, PACK, N], F32, tag=("v_table_sc", "x_table0")[a]))
             nc.sync.dma_start(wa_raw[a][:], wa[a * PASS : (a + 1) * PASS, :].rearrange("(p i) n -> p i n", i=PACK))
 
         load_scale_rows(nc.gpsimd, x_table_sc, tab2_scales)
@@ -72,12 +72,8 @@ def tile_list_repurposing_mechanism_max_kernel(
         nc.sync.dma_start(list_v[:], offs)
         nc.sync.dma_start(v_table[0][:].bitcast(I32), as_words(tab_words[0]))
         nc.sync.dma_start(list_x[:], offs2)
-        nc.sync.dma_start(x_table[0][:].bitcast(I32), as_words(tab2_words[0]))
-        nc.sync.dma_start(wb_raw[:].bitcast(I32), wb_words.rearrange("a p b -> p a b").bitcast(I32))
-        load_wa(0)
         nc.sync.dma_start(v_table[1][:].bitcast(I32), as_words(tab_words[1]))
-        nc.sync.dma_start(x_table[1][:].bitcast(I32), as_words(tab2_words[1]))
-        load_wa(1)
+        nc.sync.dma_start(x_table[0][:].bitcast(I32), as_words(tab2_words[0]))
         nc.scalar.dma_start(tw_sb[:], tw.rearrange("(a p t) -> p a t", a=PASSES, t=PACK))
         for q in range(4):
             nc.scalar.dma_start(
@@ -100,12 +96,19 @@ def tile_list_repurposing_mechanism_max_kernel(
             return list_x[:, u * (HALF // 16) : (u + 1) * (HALF // 16)]
 
         gather_v(0)
+        wb_raw = held("wb_raw", [P, PASSES, 2 * N], U8, tag="v_table0")
+        nc.sync.dma_start(wb_raw[:].bitcast(I32), wb_words.rearrange("a p b -> p a b").bitcast(I32))
         nc.vector.tensor_copy(v_picked_sc[:], v_table_sc[:].indirect(list_v[:]))
+        load_wa(0)
+        gather_v(1)
         nc.vector.tensor_copy(
             v_sc[:].rearrange("p (a t m) -> p a t m", a=PASSES, t=PACK),
             v_picked_sc[:].rearrange("p (a m t) -> p a t m", a=PASSES, t=PACK),
         )
 
+
+        x_table.append(held("x_table1", [P, T2], U32, tag="v_picked_sc"))
+        nc.sync.dma_start(x_table[1][:].bitcast(I32), as_words(tab2_words[1]))
 
         def gather_x(k, u):
             x_words[k, u] = held("x_words%d_%d" % (k, u), [P, HALF], U32)
@@ -114,18 +117,19 @@ def tile_list_repurposing_mechanism_max_kernel(
         nc.vector.tensor_copy(x_sc[:], x_table_sc[:].indirect(list_x[:]))
         gather_x(0, 0)
         gather_x(0, 1)
+        load_wa(1)
 
-        wb_codes = held("wb_codes", [P, PASSES, 2 * N], U8)
+        wb_codes = held("wb_codes", [P, PASSES, 2 * N], U8, tag="x_table_sc")
         nc.vector.tensor_copy(
             wb_codes[:].bitcast(U16).rearrange("p a (t m) -> p a t m", t=PACK),
             wb_raw[:].bitcast(U16).rearrange("p a (m t) -> p a t m", t=PACK),
         )
-        wb_sc = held("wb_sc", [P, PASSES, N], U8)
+        wb_sc = held("wb_sc", [P, PASSES, N], U8, tag="v_table0")
         nc.vector.tensor_copy(
             wb_sc[:].rearrange("p a (t m) -> p a t m", t=PACK), wb_raw_sc[:].rearrange("p a (m t) -> p a t m", t=PACK)
         )
 
-        wa_codes = [held("wa_codes%d" % a, [P, N], U32) for a in range(PASSES)]
+        wa_codes = []
         wa_sc = [held("wa_sc%d" % a, [P, N], U8) for a in range(PASSES)]
 
         def quantise_wa(a):
@@ -134,12 +138,16 @@ def tile_list_repurposing_mechanism_max_kernel(
             raw = wa_raw[a][:].rearrange("p i (m t) -> p m i t", t=PACK)
             for m0 in (0, P // 2):
                 nc.scalar.copy(dealt[:, m0 : m0 + P // 2], raw[:, m0 : m0 + P // 2])
+            wa_codes.append(held("wa_codes%d" % a, [P, N], U32, tag=("wb_raw_sc", "wa_codes1")[a]))
             nc.vector.quantize_mx(out=wa_codes[a][:].bitcast(FP8X4), scales=wa_sc[a][:], in_=grouped[:])
 
-        gather_v(1)
         quantise_wa(0)
         gather_x(1, 0)
         gather_x(1, 1)
+
+        tw_wide = held("tw_wide", [P, PASSES, max(CHUNKS), PACK], F32)
+        for a in range(PASSES):
+            nc.scalar.copy(tw_wide[:, a], tw_sb[:, a : a + 1, :].broadcast_to([P, max(CHUNKS), PACK]))
 
         y_codes = held("y_codes", [P, S2], U32)
         y_sc = held("y_sc", [P, S2], U8)
@@ -147,30 +155,33 @@ def tile_list_repurposing_mechanism_max_kernel(
         y_words = as_words(out_1[0])
 
         def effects(j0, w):
+            per_bank = BANK // w
+            banks = PACK // per_bank
             u, c0 = divmod(j0, HALF)
+            cols = slice(c0, c0 + w)
             rounded = []
             for a in range(PASSES):
-                th = ring.tile([P, w, PACK], F32, name="th", align_bytes=64, bufs=4)
-                for b0 in range(0, w, P):
-                    acc = psum_a.tile([P, PACK, P], F32, name="acc")
+                th = ring.tile([P, banks, w, per_bank], F32, name="th", align_bytes=64, bufs=4)
+                for b in range(banks):
+                    acc = psum_a.tile([P, per_bank, w], F32, name="acc")
                     for k in range(PASSES):
-                        for t in range(PACK):
-                            i0 = a * PASS + t * P
+                        for e in range(per_bank):
+                            i0 = a * PASS + (b * per_bank + e) * P
                             nc.tensor.matmul_mx(
-                                out=acc[:, t, :],
+                                out=acc[:, e, :],
                                 lhsT=v_words[k][:, i0 : i0 + P].bitcast(FP8X4),
                                 lhsT_scale=v_sc[4 * k : P, i0 : i0 + P],
-                                rhs=x_words[k, u][:, c0 + b0 : c0 + b0 + P].bitcast(FP8X4),
-                                rhs_scale=x_sc[4 * k : P, j0 + b0 : j0 + b0 + P],
-                                start=(k == 0 and t == 0),
-                                stop=(k == PASSES - 1 and t == PACK - 1),
+                                rhs=x_words[k, u][:, cols].bitcast(FP8X4),
+                                rhs_scale=x_sc[4 * k : P, j0 : j0 + w],
+                                start=(k == 0 and e == 0),
+                                stop=(k == PASSES - 1 and e == per_bank - 1),
                             )
-                    nc.scalar.activation(th[:, b0 : b0 + P, :], acc[:].rearrange("p t n -> p n t"), TANH)
+                    nc.scalar.activation(th[:, b], acc[:].rearrange("p e n -> p n e"), TANH)
                 h = ring.tile([P, w * PACK], BF16, name="h", align_bytes=64, bufs=4)
                 nc.vector.tensor_tensor(
-                    h[:].rearrange("p (n t) -> p n t", t=PACK),
-                    th[:],
-                    tw_sb[:, a : a + 1, :].broadcast_to([P, w, PACK]),
+                    h[:].rearrange("p (n b e) -> p n b e", b=banks, e=per_bank),
+                    th[:].rearrange("p b n e -> p n b e"),
+                    tw_wide[:, a, 0:w, :].rearrange("p n (b e) -> p n b e", b=banks),
                     MULT,
                 )
                 rounded.append(h)

@@ -24,7 +24,9 @@ PASSES = 2
 BANK = 512
 HALF = S2 // 2
 FP4_N = 128
-CHUNKS = (256, 256, 256, 128, 128)
+GROUPS = (512, 256, 128, 128)
+WIDE = 256
+X_ROW = 8
 
 
 def tile_list_repurposing_mechanism_max_kernel(
@@ -33,6 +35,7 @@ def tile_list_repurposing_mechanism_max_kernel(
     nc = tc.nc
     with ExitStack() as ctx:
         keep = ctx.enter_context(tc.tile_pool(name="keep", bufs=1))
+        shared = ctx.enter_context(tc.tile_pool(name="shared", bufs=1))
         ring = ctx.enter_context(tc.tile_pool(name="ring", bufs=3))
         psum_a = ctx.enter_context(tc.psum_pool(name="psum_a", bufs=4))
         psum_y = ctx.enter_context(tc.psum_pool(name="psum_y", bufs=2))
@@ -45,30 +48,25 @@ def tile_list_repurposing_mechanism_max_kernel(
 
         list_v = held("list_v", [P, S // 16], U16)
         list_x = held("list_x", [P, S2 // 16], U16)
-        v_table = [held("v_table%d" % k, [P, T], U32) for k in range(PASSES)]
+        v_table = [held("v_table0", [P, T], U32), shared.tile([P, T], U32, name="v_table1", offset=0)]
         x_table = [held("x_table0", [P, T2], U32)]
-        wa_raw = []
         v_table_sc = held("v_table_sc", [P, T], U8)
         x_table_sc = held("x_table_sc", [P, T2], U8)
         wb_raw_sc = held("wb_raw_sc", [P, PASSES, N], U8)
         tw_sb = held("tw_sb", [P, PASSES, PACK], F32)
 
-        nc.vector.memset(v_table_sc[:].bitcast(I32), 0)
         nc.vector.memset(x_table_sc[:].bitcast(I32), 0)
+        nc.vector.memset(v_table_sc[:].bitcast(I32), 0)
         nc.vector.memset(wb_raw_sc[:].rearrange("p a n -> p (a n)").bitcast(I32), 0)
 
-        def load_scale_rows(queue, plane, scales):
+        def load_scale_rows(queue, plane, row, scales):
             for q in range(4):
                 queue.dma_start(
-                    plane[32 * q : 32 * q + 8, :].bitcast(I32), scales[:, 4 * q : 4 * q + 4, :].bitcast(I32)
+                    plane[32 * q + row : 32 * q + row + 8, :].bitcast(I32), scales[:, 4 * q : 4 * q + 4, :].bitcast(I32)
                 )
 
-        def load_wa(a):
-            wa_raw.append(held("wa_raw%d" % a, [P, PACK, N], F32, tag=("v_table_sc", "x_table0")[a]))
-            nc.sync.dma_start(wa_raw[a][:], wa[a * PASS : (a + 1) * PASS, :].rearrange("(p i) n -> p i n", i=PACK))
-
-        load_scale_rows(nc.gpsimd, x_table_sc, tab2_scales)
-        load_scale_rows(nc.scalar, v_table_sc, tab_scales)
+        load_scale_rows(nc.gpsimd, x_table_sc, X_ROW, tab2_scales)
+        load_scale_rows(nc.scalar, v_table_sc, 0, tab_scales)
         nc.sync.dma_start(list_v[:], offs)
         nc.sync.dma_start(v_table[0][:].bitcast(I32), as_words(tab_words[0]))
         nc.sync.dma_start(list_x[:], offs2)
@@ -84,84 +82,92 @@ def tile_list_repurposing_mechanism_max_kernel(
         v_words = [held("v_words%d" % k, [P, S], U32) for k in range(PASSES)]
         v_picked_sc = held("v_picked_sc", [P, S], U8)
         v_sc = held("v_sc", [P, S], U8)
-        x_sc = held("x_sc", [P, S2], U8)
         x_words = {}
+        x_sc = held("x_sc", [P, S2], U8)
+
+        def half_list(u):
+            return list_x[:, u * (HALF // 16) : (u + 1) * (HALF // 16)]
 
         def gather_v(k):
             nc.vector.tensor_copy(
                 v_words[k][:].rearrange("p (a t m) -> p a m t", a=PASSES, t=PACK), v_table[k][:].indirect(list_v[:])
             )
 
-        def half_list(u):
-            return list_x[:, u * (HALF // 16) : (u + 1) * (HALF // 16)]
+        def gather_x(k, tag):
+            x_words[k] = held("x_words%d" % k, [P, S2], U32, tag=tag)
+            for u in range(2):
+                nc.vector.tensor_copy(x_words[k][:, u * HALF : (u + 1) * HALF], x_table[k][:].indirect(half_list(u)))
 
-        gather_v(0)
-        wb_raw = held("wb_raw", [P, PASSES, 2 * N], U8, tag="v_table0")
-        nc.sync.dma_start(wb_raw[:].bitcast(I32), wb_words.rearrange("a p b -> p a b").bitcast(I32))
+
         nc.vector.tensor_copy(v_picked_sc[:], v_table_sc[:].indirect(list_v[:]))
-        load_wa(0)
-        gather_v(1)
+        x_table.append(held("x_table1", [P, T2], U32, tag="v_table_sc"))
+        nc.sync.dma_start(x_table[1][:].bitcast(I32), as_words(tab2_words[1]))
+        gather_v(0)
         nc.vector.tensor_copy(
             v_sc[:].rearrange("p (a t m) -> p a t m", a=PASSES, t=PACK),
             v_picked_sc[:].rearrange("p (a m t) -> p a t m", a=PASSES, t=PACK),
         )
-
-
-        x_table.append(held("x_table1", [P, T2], U32, tag="v_picked_sc"))
-        nc.sync.dma_start(x_table[1][:].bitcast(I32), as_words(tab2_words[1]))
-
-        def gather_x(k, u):
-            x_words[k, u] = held("x_words%d_%d" % (k, u), [P, HALF], U32)
-            nc.vector.tensor_copy(x_words[k, u][:], x_table[k][:].indirect(half_list(u)))
-
+        gather_v(1)
         nc.vector.tensor_copy(x_sc[:], x_table_sc[:].indirect(list_x[:]))
-        gather_x(0, 0)
-        gather_x(0, 1)
-        load_wa(1)
 
-        wb_codes = held("wb_codes", [P, PASSES, 2 * N], U8, tag="x_table_sc")
-        nc.vector.tensor_copy(
-            wb_codes[:].bitcast(U16).rearrange("p a (t m) -> p a t m", t=PACK),
-            wb_raw[:].bitcast(U16).rearrange("p a (m t) -> p a t m", t=PACK),
-        )
-        wb_sc = held("wb_sc", [P, PASSES, N], U8, tag="v_table0")
-        nc.vector.tensor_copy(
-            wb_sc[:].rearrange("p a (t m) -> p a t m", t=PACK), wb_raw_sc[:].rearrange("p a (m t) -> p a t m", t=PACK)
-        )
+        wb_raw = shared.tile([P, PASSES, 2 * N], U8, name="wb_raw", offset=0)
+        wa_raw = [
+            shared.tile([P, PACK, N], F32, name="wa_raw0", offset=PASSES * 2 * N),
+            held("wa_raw1", [P, PACK, N], F32, tag="v_picked_sc"),
+        ]
+        nc.sync.dma_start(wb_raw[:].bitcast(I32), wb_words.rearrange("a p b -> p a b").bitcast(I32))
+        nc.sync.dma_start(wa_raw[0][:], wa[0:PASS, :].rearrange("(p i) n -> p i n", i=PACK))
+        nc.sync.dma_start(wa_raw[1][:], wa[PASS : 2 * PASS, :].rearrange("(p i) n -> p i n", i=PACK))
 
-        wa_codes = []
+        gather_x(0, "x_table_sc")
+        gather_x(1, "x_table0")
+
+        tw_wide = held("tw_wide", [P, PASSES, WIDE, PACK], F32)
+        for a in range(PASSES):
+            nc.scalar.copy(tw_wide[:, a], tw_sb[:, a : a + 1, :].broadcast_to([P, WIDE, PACK]))
+
+        wa_codes = [held("wa_codes%d" % a, [P, N], U32) for a in range(PASSES)]
         wa_sc = [held("wa_sc%d" % a, [P, N], U8) for a in range(PASSES)]
+        wb_codes = held("wb_codes", [P, PASSES, 2 * N], U8)
+        wb_sc = held("wb_sc", [P, PASSES, N], U8)
 
-        def quantise_wa(a):
+        def round_wa(a, copy):
             grouped = held("wa_grouped%d" % a, [P, N * PACK], BF16)
             dealt = grouped[:].rearrange("p (t m i) -> p m i t", t=PACK, i=PACK)
             raw = wa_raw[a][:].rearrange("p i (m t) -> p m i t", t=PACK)
             for m0 in (0, P // 2):
-                nc.scalar.copy(dealt[:, m0 : m0 + P // 2], raw[:, m0 : m0 + P // 2])
-            wa_codes.append(held("wa_codes%d" % a, [P, N], U32, tag=("wb_raw_sc", "wa_codes1")[a]))
+                copy(dealt[:, m0 : m0 + P // 2], raw[:, m0 : m0 + P // 2])
+            return grouped
+
+        def quantise_wa(a, grouped):
             nc.vector.quantize_mx(out=wa_codes[a][:].bitcast(FP8X4), scales=wa_sc[a][:], in_=grouped[:])
 
-        quantise_wa(0)
-        gather_x(1, 0)
-        gather_x(1, 1)
-
-        tw_wide = held("tw_wide", [P, PASSES, max(CHUNKS), PACK], F32)
-        for a in range(PASSES):
-            nc.scalar.copy(tw_wide[:, a], tw_sb[:, a : a + 1, :].broadcast_to([P, max(CHUNKS), PACK]))
+        def deal_wb():
+            nc.vector.tensor_copy(
+                wb_sc[:].rearrange("p a (t m) -> p a t m", t=PACK),
+                wb_raw_sc[:].rearrange("p a (m t) -> p a t m", t=PACK),
+            )
+            nc.vector.tensor_copy(
+                wb_codes[:].bitcast(U16).rearrange("p a (t m) -> p a t m", t=PACK),
+                wb_raw[:].bitcast(U16).rearrange("p a (m t) -> p a t m", t=PACK),
+            )
 
         y_codes = held("y_codes", [P, S2], U32)
         y_sc = held("y_sc", [P, S2], U8)
         y_rows = out_0.rearrange("(p t) j -> p t j", t=PACK)
         y_words = as_words(out_1[0])
+        h = [held("h%d" % a, [P, S2 * PACK], BF16) for a in range(PASSES)]
+        h_codes = [held("h_codes%d" % a, [P, S2], U32) for a in range(PASSES)]
+        h_sc = [held("h_sc%d" % a, [P, S2], U8) for a in range(PASSES)]
+
+        saturated = {}
 
         def effects(j0, w):
             per_bank = BANK // w
             banks = PACK // per_bank
-            u, c0 = divmod(j0, HALF)
-            cols = slice(c0, c0 + w)
-            rounded = []
             for a in range(PASSES):
-                th = ring.tile([P, banks, w, per_bank], F32, name="th", align_bytes=64, bufs=4)
+                th = ring.tile([P, banks, w, per_bank], F32, name="th", align_bytes=64, bufs=10)
+                saturated[j0, a] = th
                 for b in range(banks):
                     acc = psum_a.tile([P, per_bank, w], F32, name="acc")
                     for k in range(PASSES):
@@ -171,35 +177,43 @@ def tile_list_repurposing_mechanism_max_kernel(
                                 out=acc[:, e, :],
                                 lhsT=v_words[k][:, i0 : i0 + P].bitcast(FP8X4),
                                 lhsT_scale=v_sc[4 * k : P, i0 : i0 + P],
-                                rhs=x_words[k, u][:, cols].bitcast(FP8X4),
-                                rhs_scale=x_sc[4 * k : P, j0 : j0 + w],
+                                rhs=x_words[k][:, j0 : j0 + w].bitcast(FP8X4),
+                                rhs_scale=x_sc[X_ROW + 4 * k : P, j0 : j0 + w],
                                 start=(k == 0 and e == 0),
                                 stop=(k == PASSES - 1 and e == per_bank - 1),
                             )
                     nc.scalar.activation(th[:, b], acc[:].rearrange("p e n -> p n e"), TANH)
-                h = ring.tile([P, w * PACK], BF16, name="h", align_bytes=64, bufs=4)
+
+        def weigh(j0, w):
+            per_bank = BANK // w
+            banks = PACK // per_bank
+            for a in range(PASSES):
+                th = saturated[j0, a]
                 nc.vector.tensor_tensor(
-                    h[:].rearrange("p (n b e) -> p n b e", b=banks, e=per_bank),
+                    h[a][:, PACK * j0 : PACK * (j0 + w)].rearrange("p (n b e) -> p n b e", b=banks, e=per_bank),
                     th[:].rearrange("p b n e -> p n b e"),
                     tw_wide[:, a, 0:w, :].rearrange("p n (b e) -> p n b e", b=banks),
                     MULT,
                 )
-                rounded.append(h)
-            made = []
-            for a, h in enumerate(rounded):
-                h_codes = ring.tile([P, w], U32, name="h_codes%d" % a, align_bytes=64)
-                h_sc = ring.tile([P, w], U8, name="h_sc%d" % a, align_bytes=64)
-                nc.vector.quantize_mx(out=h_codes[:].bitcast(FP8X4), scales=h_sc[:], in_=h[:])
-                made.append((h_codes, h_sc))
-            return made
 
-        def scores(j0, w, made, copy):
+        def quantise_h(j0, w):
+            cols = slice(j0, j0 + w)
+            for a in range(PASSES):
+                nc.vector.quantize_mx(
+                    out=h_codes[a][:, cols].bitcast(FP8X4),
+                    scales=h_sc[a][:, cols],
+                    in_=h[a][:, PACK * j0 : PACK * (j0 + w)],
+                )
+
+        def scores(j0, w):
             per_bank = BANK // w
             banks = PACK // per_bank
-            y = ring.tile([P, PACK, w], F32, name="y", align_bytes=64)
+            cols = slice(j0, j0 + w)
+            fp4_n = w if w == BANK else FP4_N
+            y = held("y%d" % j0, [P, PACK, w], F32)
             for b in range(banks):
-                acc_b = psum_y.tile([P, per_bank, w], F32, name="acc_b")
                 acc_a = psum_y.tile([P, per_bank, w], F32, name="acc_a")
+                acc_b = psum_y.tile([P, per_bank, w], F32, name="acc_b")
                 for e in range(per_bank):
                     n0 = (b * per_bank + e) * P
                     for a in range(PASSES):
@@ -207,45 +221,71 @@ def tile_list_repurposing_mechanism_max_kernel(
                             out=acc_a[:, e, :],
                             lhsT=wa_codes[a][:, n0 : n0 + P].bitcast(FP8X4),
                             lhsT_scale=wa_sc[a][:, n0 : n0 + P],
-                            rhs=made[a][0][:].bitcast(FP8X4),
-                            rhs_scale=made[a][1][:],
+                            rhs=h_codes[a][:, cols].bitcast(FP8X4),
+                            rhs_scale=h_sc[a][:, cols],
                             start=(a == 0),
                             stop=(a == PASSES - 1),
                         )
                 for e in range(per_bank):
                     n0 = (b * per_bank + e) * P
-                    for c0 in range(0, w, FP4_N):
+                    for c0 in range(0, w, fp4_n):
                         for a in range(PASSES):
                             nc.tensor.matmul_mx(
-                                out=acc_b[:, e, c0 : c0 + FP4_N],
+                                out=acc_b[:, e, c0 : c0 + fp4_n],
                                 lhsT=wb_codes[:, a, 2 * n0 : 2 * (n0 + P)].bitcast(FP4X4),
                                 lhsT_scale=wb_sc[:, a, n0 : n0 + P],
-                                rhs=made[a][0][:, c0 : c0 + FP4_N].bitcast(FP8X4),
-                                rhs_scale=made[a][1][:, c0 : c0 + FP4_N],
+                                rhs=h_codes[a][:, j0 + c0 : j0 + c0 + fp4_n].bitcast(FP8X4),
+                                rhs_scale=h_sc[a][:, j0 + c0 : j0 + c0 + fp4_n],
                                 start=(a == 0),
                                 stop=(a == PASSES - 1),
                             )
                 ya = ring.tile([P, per_bank, w], F32, name="ya", align_bytes=64)
                 nc.scalar.copy(ya[:], acc_a[:])
-                nc.vector.tensor_tensor(y[:, b * per_bank : (b + 1) * per_bank, :], acc_b[:], ya[:], MAX)
-            nc.sync.dma_start(y_rows[:, :, j0 : j0 + w], y[:])
-            y16 = ring.tile([P, w * PACK], BF16, name="y16", align_bytes=64)
-            copy(
-                y16[:].rearrange("p (c i t) -> p c t i", i=4, t=PACK),
-                y[:].rearrange("p t (c i) -> p c t i", i=4),
-            )
-            cols = slice(j0, j0 + w)
-            nc.vector.quantize_mx(out=y_codes[:, cols].bitcast(FP8X4), scales=y_sc[:, cols], in_=y16[:])
-            nc.sync.dma_start(y_words[:, cols], y_codes[:, cols].bitcast(I32))
+                rows = slice(b * per_bank, (b + 1) * per_bank)
+                nc.vector.tensor_tensor(y[:, rows, :], acc_b[:], ya[:], MAX)
+                if b % 2 == 1 or banks == 1:
+                    done = slice(max(b - 1, 0) * per_bank, (b + 1) * per_bank)
+                    nc.sync.dma_start(y_rows[:, done, cols], y[:, done, :])
+            return y
 
-        starts = [sum(CHUNKS[:c]) for c in range(len(CHUNKS))]
-        made = effects(starts[0], CHUNKS[0])
-        quantise_wa(1)
-        for c in range(1, len(CHUNKS)):
-            ahead = effects(starts[c], CHUNKS[c])
-            scores(starts[c - 1], CHUNKS[c - 1], made, nc.scalar.copy)
-            made = ahead
-        scores(starts[-1], CHUNKS[-1], made, nc.vector.tensor_copy)
+        def planes(j0, w, y, copy):
+            for c0 in range(0, w, WIDE):
+                n = min(w, WIDE)
+                y16 = ring.tile([P, n * PACK], BF16, name="y16", align_bytes=64)
+                copy(
+                    y16[:].rearrange("p (c i t) -> p c t i", i=4, t=PACK),
+                    y[:, :, c0 : c0 + n].rearrange("p t (c i) -> p c t i", i=4),
+                )
+                cols = slice(j0 + c0, j0 + c0 + n)
+                nc.vector.quantize_mx(out=y_codes[:, cols].bitcast(FP8X4), scales=y_sc[:, cols], in_=y16[:])
+            nc.sync.dma_start(y_words[:, j0 : j0 + w], y_codes[:, j0 : j0 + w].bitcast(I32))
+
+        effects(0, 256)
+        effects(256, 256)
+        grouped = [round_wa(0, nc.vector.tensor_copy), round_wa(1, nc.scalar.copy)]
+        deal_wb()
+        effects(512, 256)
+        effects(768, 128)
+        effects(896, 128)
+        weigh(0, 256)
+        quantise_wa(0, grouped[0])
+        weigh(256, 256)
+        quantise_wa(1, grouped[1])
+        quantise_h(0, 512)
+        weigh(512, 256)
+        y0 = scores(0, 512)
+        quantise_h(512, 256)
+        weigh(768, 128)
+        weigh(896, 128)
+        y1 = scores(512, 256)
+        quantise_h(768, 128)
+        quantise_h(896, 128)
+        planes(0, 512, y0, nc.scalar.copy)
+        y2 = scores(768, 128)
+        y3 = scores(896, 128)
+        planes(512, 256, y1, nc.scalar.copy)
+        planes(768, 128, y2, nc.vector.tensor_copy)
+        planes(896, 128, y3, nc.vector.tensor_copy)
         for q in range(4):
             queue = nc.sync if q % 2 == 0 else nc.scalar
             queue.dma_start(out_2[0, 4 * q : 4 * q + 4, :].bitcast(I32), y_sc[32 * q : 32 * q + 4, :].bitcast(I32))

@@ -52,12 +52,13 @@ def tile_list_repurposing_mechanism_max_kernel(
         x_table = [held("x_table0", [P, T2], U32)]
         v_table_sc = held("v_table_sc", [P, T], U8)
         x_table_sc = held("x_table_sc", [P, T2], U8)
-        wb_raw_sc = held("wb_raw_sc", [P, PASSES, N], U8)
+        x_sc = held("x_sc", [P, S2], U8)
         tw_sb = held("tw_sb", [P, PASSES, PACK], F32)
 
-        nc.vector.memset(x_table_sc[:].bitcast(I32), 0)
         nc.vector.memset(v_table_sc[:].bitcast(I32), 0)
-        nc.vector.memset(wb_raw_sc[:].rearrange("p a n -> p (a n)").bitcast(I32), 0)
+        nc.vector.memset(x_table_sc[32:64, :].bitcast(I32), 0)
+        nc.vector.memset(x_table_sc[64:P, :].bitcast(I32), 0)
+        nc.vector.memset(x_sc[:].bitcast(I32), 0)
 
         def load_scale_rows(queue, plane, row, scales):
             for q in range(4):
@@ -65,25 +66,20 @@ def tile_list_repurposing_mechanism_max_kernel(
                     plane[32 * q + row : 32 * q + row + 8, :].bitcast(I32), scales[:, 4 * q : 4 * q + 4, :].bitcast(I32)
                 )
 
-        load_scale_rows(nc.gpsimd, x_table_sc, X_ROW, tab2_scales)
+        nc.gpsimd.dma_start(tw_sb[:], tw.rearrange("(a p t) -> p a t", a=PASSES, t=PACK))
+        nc.sync.dma_start(list_x[:], offs2)
+        nc.sync.dma_start(x_table_sc[0:32, :].bitcast(I32), tab2_scales.rearrange("a q t -> (a q) t").bitcast(I32))
         load_scale_rows(nc.scalar, v_table_sc, 0, tab_scales)
         nc.sync.dma_start(list_v[:], offs)
         nc.sync.dma_start(v_table[0][:].bitcast(I32), as_words(tab_words[0]))
-        nc.sync.dma_start(list_x[:], offs2)
         nc.sync.dma_start(v_table[1][:].bitcast(I32), as_words(tab_words[1]))
         nc.sync.dma_start(x_table[0][:].bitcast(I32), as_words(tab2_words[0]))
-        nc.scalar.dma_start(tw_sb[:], tw.rearrange("(a p t) -> p a t", a=PASSES, t=PACK))
-        for q in range(4):
-            nc.scalar.dma_start(
-                wb_raw_sc[32 * q : 32 * q + 4, :, :].bitcast(I32),
-                wb_scales[:, 4 * q : 4 * q + 4, :].rearrange("a r n -> r a n").bitcast(I32),
-            )
 
         v_words = [held("v_words%d" % k, [P, S], U32) for k in range(PASSES)]
         v_picked_sc = held("v_picked_sc", [P, S], U8)
         v_sc = held("v_sc", [P, S], U8)
         x_words = {}
-        x_sc = held("x_sc", [P, S2], U8)
+        x_picked_sc = held("x_picked_sc", [P, S2], U8)
 
         def half_list(u):
             return list_x[:, u * (HALF // 16) : (u + 1) * (HALF // 16)]
@@ -99,28 +95,42 @@ def tile_list_repurposing_mechanism_max_kernel(
                 nc.vector.tensor_copy(x_words[k][:, u * HALF : (u + 1) * HALF], x_table[k][:].indirect(half_list(u)))
 
 
-        nc.vector.tensor_copy(v_picked_sc[:], v_table_sc[:].indirect(list_v[:]))
-        x_table.append(held("x_table1", [P, T2], U32, tag="v_table_sc"))
-        nc.sync.dma_start(x_table[1][:].bitcast(I32), as_words(tab2_words[1]))
+        nc.vector.tensor_copy(x_picked_sc[:], x_table_sc[:].indirect(list_x[:]))
+        for a in range(PASSES):
+            for q in range(4):
+                row = 32 * q + X_ROW + 4 * a
+                nc.scalar.dma_start(
+                    x_sc[row : row + 4, :].bitcast(I32),
+                    x_picked_sc[16 * a + 4 * q : 16 * a + 4 * q + 4, :].bitcast(I32),
+                )
         gather_v(0)
+        x_table.append(held("x_table1", [P, T2], U32, tag="v_table0"))
+        nc.sync.dma_start(x_table[1][:].bitcast(I32), as_words(tab2_words[1]))
+        nc.vector.tensor_copy(v_picked_sc[:], v_table_sc[:].indirect(list_v[:]))
+        wb_raw_sc = held("wb_raw_sc", [P, PASSES, N], U8, tag="v_table_sc")
+        nc.vector.memset(wb_raw_sc[:].rearrange("p a n -> p (a n)").bitcast(I32), 0)
+        for q in range(4):
+            nc.scalar.dma_start(
+                wb_raw_sc[32 * q : 32 * q + 4, :, :].bitcast(I32),
+                wb_scales[:, 4 * q : 4 * q + 4, :].rearrange("a r n -> r a n").bitcast(I32),
+            )
         nc.vector.tensor_copy(
             v_sc[:].rearrange("p (a t m) -> p a t m", a=PASSES, t=PACK),
             v_picked_sc[:].rearrange("p (a m t) -> p a t m", a=PASSES, t=PACK),
         )
         gather_v(1)
-        nc.vector.tensor_copy(x_sc[:], x_table_sc[:].indirect(list_x[:]))
 
         wb_raw = shared.tile([P, PASSES, 2 * N], U8, name="wb_raw", offset=0)
         wa_raw = [
             shared.tile([P, PACK, N], F32, name="wa_raw0", offset=PASSES * 2 * N),
-            held("wa_raw1", [P, PACK, N], F32, tag="v_picked_sc"),
         ]
         nc.sync.dma_start(wb_raw[:].bitcast(I32), wb_words.rearrange("a p b -> p a b").bitcast(I32))
         nc.sync.dma_start(wa_raw[0][:], wa[0:PASS, :].rearrange("(p i) n -> p i n", i=PACK))
-        nc.sync.dma_start(wa_raw[1][:], wa[PASS : 2 * PASS, :].rearrange("(p i) n -> p i n", i=PACK))
 
-        gather_x(0, "x_table_sc")
-        gather_x(1, "x_table0")
+        gather_x(0, None)
+        wa_raw.append(held("wa_raw1", [P, PACK, N], F32, tag="x_table0"))
+        nc.sync.dma_start(wa_raw[1][:], wa[PASS : 2 * PASS, :].rearrange("(p i) n -> p i n", i=PACK))
+        gather_x(1, None)
 
         tw_wide = held("tw_wide", [P, PASSES, WIDE, PACK], F32)
         for a in range(PASSES):
@@ -131,11 +141,11 @@ def tile_list_repurposing_mechanism_max_kernel(
         wb_codes = held("wb_codes", [P, PASSES, 2 * N], U8)
         wb_sc = held("wb_sc", [P, PASSES, N], U8)
 
-        def round_wa(a, copy):
+        def round_wa(a, copies):
             grouped = held("wa_grouped%d" % a, [P, N * PACK], BF16)
             dealt = grouped[:].rearrange("p (t m i) -> p m i t", t=PACK, i=PACK)
             raw = wa_raw[a][:].rearrange("p i (m t) -> p m i t", t=PACK)
-            for m0 in (0, P // 2):
+            for m0, copy in zip((0, P // 2), copies):
                 copy(dealt[:, m0 : m0 + P // 2], raw[:, m0 : m0 + P // 2])
             return grouped
 
@@ -262,16 +272,16 @@ def tile_list_repurposing_mechanism_max_kernel(
 
         effects(0, 256)
         effects(256, 256)
-        grouped = [round_wa(0, nc.vector.tensor_copy), round_wa(1, nc.scalar.copy)]
         deal_wb()
+        grouped = [round_wa(0, (nc.vector.tensor_copy, nc.vector.tensor_copy)), round_wa(1, (nc.scalar.copy, nc.scalar.copy))]
         effects(512, 256)
         effects(768, 128)
         effects(896, 128)
         weigh(0, 256)
-        quantise_wa(0, grouped[0])
         weigh(256, 256)
-        quantise_wa(1, grouped[1])
+        quantise_wa(0, grouped[0])
         quantise_h(0, 512)
+        quantise_wa(1, grouped[1])
         weigh(512, 256)
         y0 = scores(0, 512)
         quantise_h(512, 256)

@@ -1,6 +1,7 @@
 from contextlib import ExitStack
 
 import concourse.mybir as mybir
+from concourse.masks import make_identity
 
 K, T, S, T2, S2, N = 1024, 2048, 1024, 4096, 1024, 512
 FLOPS = 2 * K * S * S2 + 2 * 2 * S * N * S2
@@ -16,6 +17,7 @@ FP4X4 = mybir.dt.float4_e2m1fn_x4
 TANH = mybir.ActivationFunctionType.Tanh
 MULT = mybir.AluOpType.mult
 MAX = mybir.AluOpType.max
+ADD = mybir.AluOpType.add
 
 P = 128
 PACK = 4
@@ -27,6 +29,7 @@ FP4_N = 128
 GROUPS = (512, 256, 128, 128)
 WIDE = 256
 X_ROW = 8
+GROUPED_AT = 8192
 
 
 def tile_list_repurposing_mechanism_max_kernel(
@@ -37,8 +40,8 @@ def tile_list_repurposing_mechanism_max_kernel(
         keep = ctx.enter_context(tc.tile_pool(name="keep", bufs=1))
         shared = ctx.enter_context(tc.tile_pool(name="shared", bufs=1))
         ring = ctx.enter_context(tc.tile_pool(name="ring", bufs=3))
-        psum_a = ctx.enter_context(tc.psum_pool(name="psum_a", bufs=4))
-        psum_y = ctx.enter_context(tc.psum_pool(name="psum_y", bufs=2))
+        psum_a = ctx.enter_context(tc.psum_pool(name="psum_a", bufs=7))
+        psum_w = ctx.enter_context(tc.psum_pool(name="psum_w", bufs=1))
 
         def held(name, shape, dtype, tag=None):
             return keep.tile(shape, dtype, name=name, tag=tag or name, align_bytes=64)
@@ -48,12 +51,13 @@ def tile_list_repurposing_mechanism_max_kernel(
 
         list_v = held("list_v", [P, S // 16], U16)
         list_x = held("list_x", [P, S2 // 16], U16)
-        v_table = [held("v_table0", [P, T], U32), shared.tile([P, T], U32, name="v_table1", offset=0)]
-        x_table = [held("x_table0", [P, T2], U32)]
+        v_table = [held("v_table%d" % k, [P, T], U32) for k in range(PASSES)]
+        x_table = [shared.tile([P, T2], U32, name="x_table0", offset=0)]
         v_table_sc = held("v_table_sc", [P, T], U8)
         x_table_sc = held("x_table_sc", [P, T2], U8)
         x_sc = held("x_sc", [P, S2], U8)
-        tw_sb = held("tw_sb", [P, PASSES, PACK], F32)
+        tw_rows = held("tw_rows", [P, PASS], F32)
+        identity = held("identity", [P, P], F32)
 
         nc.vector.memset(v_table_sc[:].bitcast(I32), 0)
         nc.vector.memset(x_table_sc[32:64, :].bitcast(I32), 0)
@@ -66,7 +70,11 @@ def tile_list_repurposing_mechanism_max_kernel(
                     plane[32 * q + row : 32 * q + row + 8, :].bitcast(I32), scales[:, 4 * q : 4 * q + 4, :].bitcast(I32)
                 )
 
-        nc.gpsimd.dma_start(tw_sb[:], tw.rearrange("(a p t) -> p a t", a=PASSES, t=PACK))
+        nc.gpsimd.memset(tw_rows[:], 0.0)
+        nc.gpsimd.dma_start(tw_rows[0:PASSES, :], tw.rearrange("(a i) -> a i", a=PASSES))
+        make_identity(nc, identity[:])
+        warm = held("warm", [P, 1], F32)
+        nc.scalar.activation(warm[:], identity[:, 0:1], TANH)
         nc.sync.dma_start(list_x[:], offs2)
         nc.sync.dma_start(x_table_sc[0:32, :].bitcast(I32), tab2_scales.rearrange("a q t -> (a q) t").bitcast(I32))
         load_scale_rows(nc.scalar, v_table_sc, 0, tab_scales)
@@ -103,43 +111,40 @@ def tile_list_repurposing_mechanism_max_kernel(
                     x_sc[row : row + 4, :].bitcast(I32),
                     x_picked_sc[16 * a + 4 * q : 16 * a + 4 * q + 4, :].bitcast(I32),
                 )
-        gather_v(0)
-        x_table.append(held("x_table1", [P, T2], U32, tag="v_table0"))
-        nc.sync.dma_start(x_table[1][:].bitcast(I32), as_words(tab2_words[1]))
         nc.vector.tensor_copy(v_picked_sc[:], v_table_sc[:].indirect(list_v[:]))
-        wb_raw_sc = held("wb_raw_sc", [P, PASSES, N], U8, tag="v_table_sc")
+        x_table.append(held("x_table1", [P, T2], U32, tag="v_table_sc"))
+        nc.sync.dma_start(x_table[1][:].bitcast(I32), as_words(tab2_words[1]))
+        nc.vector.tensor_copy(
+            v_sc[:].rearrange("p (a t m) -> p a t m", a=PASSES, t=PACK),
+            v_picked_sc[:].rearrange("p (a m t) -> p a t m", a=PASSES, t=PACK),
+        )
+        gather_v(0)
+        wb_raw_sc = held("wb_raw_sc", [P, PASSES, N], U8, tag="v_picked_sc")
         nc.vector.memset(wb_raw_sc[:].rearrange("p a n -> p (a n)").bitcast(I32), 0)
         for q in range(4):
             nc.scalar.dma_start(
                 wb_raw_sc[32 * q : 32 * q + 4, :, :].bitcast(I32),
                 wb_scales[:, 4 * q : 4 * q + 4, :].rearrange("a r n -> r a n").bitcast(I32),
             )
-        nc.vector.tensor_copy(
-            v_sc[:].rearrange("p (a t m) -> p a t m", a=PASSES, t=PACK),
-            v_picked_sc[:].rearrange("p (a m t) -> p a t m", a=PASSES, t=PACK),
-        )
         gather_v(1)
 
-        wb_raw = shared.tile([P, PASSES, 2 * N], U8, name="wb_raw", offset=0)
-        wa_raw = [
-            shared.tile([P, PACK, N], F32, name="wa_raw0", offset=PASSES * 2 * N),
-        ]
-        nc.sync.dma_start(wb_raw[:].bitcast(I32), wb_words.rearrange("a p b -> p a b").bitcast(I32))
+        wa_raw = [held("wa_raw0", [P, PACK, N], F32, tag="v_table1")]
         nc.sync.dma_start(wa_raw[0][:], wa[0:PASS, :].rearrange("(p i) n -> p i n", i=PACK))
 
         gather_x(0, None)
-        wa_raw.append(held("wa_raw1", [P, PACK, N], F32, tag="x_table0"))
+        wa_raw.append(shared.tile([P, PACK, N], F32, name="wa_raw1", offset=0))
         nc.sync.dma_start(wa_raw[1][:], wa[PASS : 2 * PASS, :].rearrange("(p i) n -> p i n", i=PACK))
+        wb_raw = shared.tile([P, PASSES, 2 * N], U8, name="wb_raw", offset=GROUPED_AT)
+        nc.sync.dma_start(wb_raw[:].bitcast(I32), wb_words.rearrange("a p b -> p a b").bitcast(I32))
         gather_x(1, None)
 
-        tw_wide = held("tw_wide", [P, PASSES, WIDE, PACK], F32)
-        for a in range(PASSES):
-            nc.scalar.copy(tw_wide[:, a], tw_sb[:, a : a + 1, :].broadcast_to([P, WIDE, PACK]))
+        tw_bank = psum_w.tile([P, PACK, P], F32, name="tw_bank")
+        for t in range(PACK):
+            nc.tensor.transpose(tw_bank[:, t, :], tw_rows[:, t:PASS:PACK], identity[:])
 
         wa_codes = [held("wa_codes%d" % a, [P, N], U32) for a in range(PASSES)]
         wa_sc = [held("wa_sc%d" % a, [P, N], U8) for a in range(PASSES)]
-        wb_codes = held("wb_codes", [P, PASSES, 2 * N], U8)
-        wb_sc = held("wb_sc", [P, PASSES, N], U8)
+        wb_dealt = []
 
         def round_wa(a, copies):
             grouped = held("wa_grouped%d" % a, [P, N * PACK], BF16)
@@ -149,10 +154,21 @@ def tile_list_repurposing_mechanism_max_kernel(
                 copy(dealt[:, m0 : m0 + P // 2], raw[:, m0 : m0 + P // 2])
             return grouped
 
+        def round_wa_pool(a):
+            grouped = held("wa_grouped%d" % a, [P, N * PACK], BF16)
+            dealt = grouped[:].rearrange("p (t m i) -> p m t i", t=PACK, i=PACK)
+            raw = wa_raw[a][:].rearrange("p i (m t) -> p m t i", t=PACK)
+            for m0 in (0, P // 2):
+                nc.gpsimd.tensor_scalar(dealt[:, m0 : m0 + P // 2], raw[:, m0 : m0 + P // 2], 1.0, 0.0, MULT, ADD)
+            return grouped
+
         def quantise_wa(a, grouped):
             nc.vector.quantize_mx(out=wa_codes[a][:].bitcast(FP8X4), scales=wa_sc[a][:], in_=grouped[:])
 
         def deal_wb():
+            wb_codes = shared.tile([P, PASSES, 2 * N], U8, name="wb_codes", offset=0, align_bytes=64)
+            wb_sc = shared.tile([P, PASSES, N], U8, name="wb_sc", offset=PASSES * 2 * N, align_bytes=64)
+            wb_dealt.extend([wb_codes, wb_sc])
             nc.vector.tensor_copy(
                 wb_sc[:].rearrange("p a (t m) -> p a t m", t=PACK),
                 wb_raw_sc[:].rearrange("p a (m t) -> p a t m", t=PACK),
@@ -202,7 +218,9 @@ def tile_list_repurposing_mechanism_max_kernel(
                 nc.vector.tensor_tensor(
                     h[a][:, PACK * j0 : PACK * (j0 + w)].rearrange("p (n b e) -> p n b e", b=banks, e=per_bank),
                     th[:].rearrange("p b n e -> p n b e"),
-                    tw_wide[:, a, 0:w, :].rearrange("p n (b e) -> p n b e", b=banks),
+                    tw_bank[:, :, a : a + 1]
+                    .rearrange("p (b e) n -> p n b e", b=banks)
+                    .broadcast_to([P, w, banks, per_bank]),
                     MULT,
                 )
 
@@ -215,15 +233,15 @@ def tile_list_repurposing_mechanism_max_kernel(
                     in_=h[a][:, PACK * j0 : PACK * (j0 + w)],
                 )
 
-        def scores(j0, w):
+        def scores(j0, w, pool, tags):
             per_bank = BANK // w
             banks = PACK // per_bank
             cols = slice(j0, j0 + w)
             fp4_n = w if w == BANK else FP4_N
             y = held("y%d" % j0, [P, PACK, w], F32)
             for b in range(banks):
-                acc_a = psum_y.tile([P, per_bank, w], F32, name="acc_a")
-                acc_b = psum_y.tile([P, per_bank, w], F32, name="acc_b")
+                acc_a = pool.tile([P, per_bank, w], F32, name="acc_a", tag=tags[0])
+                acc_b = pool.tile([P, per_bank, w], F32, name="acc_b", tag=tags[1])
                 for e in range(per_bank):
                     n0 = (b * per_bank + e) * P
                     for a in range(PASSES):
@@ -242,8 +260,8 @@ def tile_list_repurposing_mechanism_max_kernel(
                         for a in range(PASSES):
                             nc.tensor.matmul_mx(
                                 out=acc_b[:, e, c0 : c0 + fp4_n],
-                                lhsT=wb_codes[:, a, 2 * n0 : 2 * (n0 + P)].bitcast(FP4X4),
-                                lhsT_scale=wb_sc[:, a, n0 : n0 + P],
+                                lhsT=wb_dealt[0][:, a, 2 * n0 : 2 * (n0 + P)].bitcast(FP4X4),
+                                lhsT_scale=wb_dealt[1][:, a, n0 : n0 + P],
                                 rhs=h_codes[a][:, j0 + c0 : j0 + c0 + fp4_n].bitcast(FP8X4),
                                 rhs_scale=h_sc[a][:, j0 + c0 : j0 + c0 + fp4_n],
                                 start=(a == 0),
@@ -272,29 +290,29 @@ def tile_list_repurposing_mechanism_max_kernel(
 
         effects(0, 256)
         effects(256, 256)
-        deal_wb()
-        grouped = [round_wa(0, (nc.vector.tensor_copy, nc.vector.tensor_copy)), round_wa(1, (nc.scalar.copy, nc.scalar.copy))]
+        grouped = [round_wa_pool(0), round_wa_pool(1)]
         effects(512, 256)
         effects(768, 128)
         effects(896, 128)
         weigh(0, 256)
         weigh(256, 256)
+        deal_wb()
         quantise_wa(0, grouped[0])
         quantise_h(0, 512)
         quantise_wa(1, grouped[1])
         weigh(512, 256)
-        y0 = scores(0, 512)
+        y0 = scores(0, 512, psum_a, ("acc", "acc"))
         quantise_h(512, 256)
         weigh(768, 128)
         weigh(896, 128)
-        y1 = scores(512, 256)
         quantise_h(768, 128)
         quantise_h(896, 128)
+        y1 = scores(512, 256, psum_a, ("acc", "acc"))
         planes(0, 512, y0, nc.scalar.copy)
-        y2 = scores(768, 128)
-        y3 = scores(896, 128)
+        y2 = scores(768, 128, psum_a, ("acc", "acc"))
+        y3 = scores(896, 128, psum_a, ("acc", "acc"))
         planes(512, 256, y1, nc.scalar.copy)
-        planes(768, 128, y2, nc.vector.tensor_copy)
+        planes(768, 128, y2, nc.scalar.copy)
         planes(896, 128, y3, nc.vector.tensor_copy)
         for q in range(4):
             queue = nc.sync if q % 2 == 0 else nc.scalar

@@ -56,7 +56,7 @@ def tile_list_repurposing_mechanism_max_kernel(
         v_table_sc = held("v_table_sc", [P, T], U8)
         x_table_sc = held("x_table_sc", [P, T2], U8)
         x_sc = held("x_sc", [P, S2], U8)
-        tw_rows = held("tw_rows", [P, PASS], F32)
+        tw_sb = held("tw_sb", [P, 1, PASSES * PACK], F32)
         identity = held("identity", [P, P], F32)
 
         nc.vector.memset(v_table_sc[:].bitcast(I32), 0)
@@ -70,11 +70,10 @@ def tile_list_repurposing_mechanism_max_kernel(
                     plane[32 * q + row : 32 * q + row + 8, :].bitcast(I32), scales[:, 4 * q : 4 * q + 4, :].bitcast(I32)
                 )
 
-        nc.gpsimd.memset(tw_rows[:], 0.0)
-        nc.gpsimd.dma_start(tw_rows[0:PASSES, :], tw.rearrange("(a i) -> a i", a=PASSES))
+        nc.gpsimd.dma_start(
+            tw_sb[:, 0, :].rearrange("p (a t) -> p a t", a=PASSES), tw.rearrange("(a p t) -> p a t", a=PASSES, t=PACK)
+        )
         make_identity(nc, identity[:])
-        warm = held("warm", [P, 1], F32)
-        nc.scalar.activation(warm[:], identity[:, 0:1], TANH)
         nc.sync.dma_start(list_x[:], offs2)
         nc.sync.dma_start(x_table_sc[0:32, :].bitcast(I32), tab2_scales.rearrange("a q t -> (a q) t").bitcast(I32))
         load_scale_rows(nc.scalar, v_table_sc, 0, tab_scales)
@@ -138,9 +137,17 @@ def tile_list_repurposing_mechanism_max_kernel(
         nc.sync.dma_start(wb_raw[:].bitcast(I32), wb_words.rearrange("a p b -> p a b").bitcast(I32))
         gather_x(1, None)
 
-        tw_bank = psum_w.tile([P, PACK, P], F32, name="tw_bank")
-        for t in range(PACK):
-            nc.tensor.transpose(tw_bank[:, t, :], tw_rows[:, t:PASS:PACK], identity[:])
+        tw_square = held("tw_square", [P, P], F32)
+        tw_turned = held("tw_turned", [P, P], F32)
+        repeats = P // (PASSES * PACK)
+        nc.scalar.copy(
+            tw_square[:].rearrange("p (r c) -> p r c", r=repeats), tw_sb[:].broadcast_to([P, repeats, PASSES * PACK])
+        )
+        turning = psum_w.tile([P, P], F32, name="turning", tag="tw_bank")
+        nc.tensor.transpose(turning[:], tw_square[:], identity[:])
+        nc.scalar.copy(tw_turned[:], turning[:])
+        tw_bank = psum_w.tile([P, P], F32, name="tw_bank")
+        nc.tensor.transpose(tw_bank[:], tw_turned[:], identity[:])
 
         wa_codes = [held("wa_codes%d" % a, [P, N], U32) for a in range(PASSES)]
         wa_sc = [held("wa_sc%d" % a, [P, N], U8) for a in range(PASSES)]
@@ -159,7 +166,10 @@ def tile_list_repurposing_mechanism_max_kernel(
             dealt = grouped[:].rearrange("p (t m i) -> p m t i", t=PACK, i=PACK)
             raw = wa_raw[a][:].rearrange("p i (m t) -> p m t i", t=PACK)
             for m0 in (0, P // 2):
-                nc.gpsimd.tensor_scalar(dealt[:, m0 : m0 + P // 2], raw[:, m0 : m0 + P // 2], 1.0, 0.0, MULT, ADD)
+                if (a, m0) == (0, P // 2):
+                    nc.scalar.copy(dealt[:, m0 : m0 + P // 2], raw[:, m0 : m0 + P // 2])
+                else:
+                    nc.gpsimd.tensor_scalar(dealt[:, m0 : m0 + P // 2], raw[:, m0 : m0 + P // 2], 1.0, 0.0, MULT, ADD)
             return grouped
 
         def quantise_wa(a, grouped):
@@ -218,8 +228,8 @@ def tile_list_repurposing_mechanism_max_kernel(
                 nc.vector.tensor_tensor(
                     h[a][:, PACK * j0 : PACK * (j0 + w)].rearrange("p (n b e) -> p n b e", b=banks, e=per_bank),
                     th[:].rearrange("p b n e -> p n b e"),
-                    tw_bank[:, :, a : a + 1]
-                    .rearrange("p (b e) n -> p n b e", b=banks)
+                    tw_bank[:, PACK * a : PACK * (a + 1)]
+                    .rearrange("p (n b e) -> p n b e", n=1, b=banks)
                     .broadcast_to([P, w, banks, per_bank]),
                     MULT,
                 )
@@ -297,8 +307,8 @@ def tile_list_repurposing_mechanism_max_kernel(
         weigh(0, 256)
         weigh(256, 256)
         deal_wb()
-        quantise_wa(0, grouped[0])
         quantise_h(0, 512)
+        quantise_wa(0, grouped[0])
         quantise_wa(1, grouped[1])
         weigh(512, 256)
         y0 = scores(0, 512, psum_a, ("acc", "acc"))

@@ -28,8 +28,8 @@ HALF = S2 // 2
 FP4_N = 128
 GROUPS = (512, 256, 128, 128)
 WIDE = 256
-X_ROW = 8
-GROUPED_AT = 8192
+TABLE_ROW = 4
+WHOLE_AT = 96
 
 
 def tile_list_repurposing_mechanism_max_kernel(
@@ -38,7 +38,6 @@ def tile_list_repurposing_mechanism_max_kernel(
     nc = tc.nc
     with ExitStack() as ctx:
         keep = ctx.enter_context(tc.tile_pool(name="keep", bufs=1))
-        shared = ctx.enter_context(tc.tile_pool(name="shared", bufs=1))
         ring = ctx.enter_context(tc.tile_pool(name="ring", bufs=3))
         psum_a = ctx.enter_context(tc.psum_pool(name="psum_a", bufs=7))
         psum_w = ctx.enter_context(tc.psum_pool(name="psum_w", bufs=1))
@@ -52,41 +51,41 @@ def tile_list_repurposing_mechanism_max_kernel(
         list_v = held("list_v", [P, S // 16], U16)
         list_x = held("list_x", [P, S2 // 16], U16)
         v_table = [held("v_table%d" % k, [P, T], U32) for k in range(PASSES)]
-        x_table = [shared.tile([P, T2], U32, name="x_table0", offset=0)]
+        x_table = [held("x_table%d" % k, [P, T2], U32) for k in range(PASSES)]
         v_table_sc = held("v_table_sc", [P, T], U8)
         x_table_sc = held("x_table_sc", [P, T2], U8)
-        x_sc = held("x_sc", [P, S2], U8)
+        picked_sc = held("picked_sc", [P, S2 + S], U8)
+        placed_sc = held("placed_sc", [P, S2 + S], U8)
+        dealt_sc = held("dealt_sc", [P, S], U8)
         tw_sb = held("tw_sb", [P, 1, PASSES * PACK], F32)
         identity = held("identity", [P, P], F32)
 
-        nc.vector.memset(v_table_sc[:].bitcast(I32), 0)
-        nc.vector.memset(x_table_sc[32:64, :].bitcast(I32), 0)
-        nc.vector.memset(x_table_sc[64:P, :].bitcast(I32), 0)
-        nc.vector.memset(x_sc[:].bitcast(I32), 0)
+        nc.gpsimd.memset(placed_sc[:].bitcast(I32), 0)
+        for plane in (x_table_sc, v_table_sc):
+            nc.vector.memset(plane[0:WHOLE_AT, :].bitcast(I32), 0)
 
-        def load_scale_rows(queue, plane, row, scales):
-            for q in range(4):
-                queue.dma_start(
-                    plane[32 * q + row : 32 * q + row + 8, :].bitcast(I32), scales[:, 4 * q : 4 * q + 4, :].bitcast(I32)
-                )
-
+        for q in range(4):
+            nc.gpsimd.dma_start(
+                placed_sc[32 * q : 32 * q + 4, S2:].rearrange("r (a n) -> r a n", a=PASSES).bitcast(I32),
+                wb_scales[:, 4 * q : 4 * q + 4, :].rearrange("a r n -> r a n").bitcast(I32),
+            )
         nc.gpsimd.dma_start(
             tw_sb[:, 0, :].rearrange("p (a t) -> p a t", a=PASSES), tw.rearrange("(a p t) -> p a t", a=PASSES, t=PACK)
         )
         make_identity(nc, identity[:])
         nc.sync.dma_start(list_x[:], offs2)
-        nc.sync.dma_start(x_table_sc[0:32, :].bitcast(I32), tab2_scales.rearrange("a q t -> (a q) t").bitcast(I32))
-        load_scale_rows(nc.scalar, v_table_sc, 0, tab_scales)
+        nc.sync.dma_start(x_table_sc[WHOLE_AT:P, :].bitcast(I32), tab2_scales.rearrange("a q t -> (a q) t").bitcast(I32))
         nc.sync.dma_start(list_v[:], offs)
+        nc.sync.dma_start(v_table_sc[WHOLE_AT:P, :].bitcast(I32), tab_scales.rearrange("a q t -> (a q) t").bitcast(I32))
+        nc.sync.dma_start(x_table[0][:].bitcast(I32), as_words(tab2_words[0]))
         nc.sync.dma_start(v_table[0][:].bitcast(I32), as_words(tab_words[0]))
         nc.sync.dma_start(v_table[1][:].bitcast(I32), as_words(tab_words[1]))
-        nc.sync.dma_start(x_table[0][:].bitcast(I32), as_words(tab2_words[0]))
+        nc.sync.dma_start(x_table[1][:].bitcast(I32), as_words(tab2_words[1]))
+        wb_raw = held("wb_raw", [P, PASSES, 2 * N], U8)
+        nc.sync.dma_start(wb_raw[:].bitcast(I32), wb_words.rearrange("a p b -> p a b").bitcast(I32))
 
         v_words = [held("v_words%d" % k, [P, S], U32) for k in range(PASSES)]
-        v_picked_sc = held("v_picked_sc", [P, S], U8)
-        v_sc = held("v_sc", [P, S], U8)
         x_words = {}
-        x_picked_sc = held("x_picked_sc", [P, S2], U8)
 
         def half_list(u):
             return list_x[:, u * (HALF // 16) : (u + 1) * (HALF // 16)]
@@ -101,40 +100,27 @@ def tile_list_repurposing_mechanism_max_kernel(
             for u in range(2):
                 nc.vector.tensor_copy(x_words[k][:, u * HALF : (u + 1) * HALF], x_table[k][:].indirect(half_list(u)))
 
+        def place_rows(queue, a, q):
+            row = 32 * q + TABLE_ROW + 4 * a
+            src = WHOLE_AT + 16 * a + 4 * q
+            queue.dma_start(placed_sc[row : row + 4, :].bitcast(I32), picked_sc[src : src + 4, :].bitcast(I32))
 
-        nc.vector.tensor_copy(x_picked_sc[:], x_table_sc[:].indirect(list_x[:]))
+        nc.vector.tensor_copy(picked_sc[:, 0:S2], x_table_sc[:].indirect(list_x[:]))
+        nc.vector.tensor_copy(picked_sc[:, S2:], v_table_sc[:].indirect(list_v[:]))
         for a in range(PASSES):
             for q in range(4):
-                row = 32 * q + X_ROW + 4 * a
-                nc.scalar.dma_start(
-                    x_sc[row : row + 4, :].bitcast(I32),
-                    x_picked_sc[16 * a + 4 * q : 16 * a + 4 * q + 4, :].bitcast(I32),
-                )
-        nc.vector.tensor_copy(v_picked_sc[:], v_table_sc[:].indirect(list_v[:]))
-        x_table.append(held("x_table1", [P, T2], U32, tag="v_table_sc"))
-        nc.sync.dma_start(x_table[1][:].bitcast(I32), as_words(tab2_words[1]))
-        nc.vector.tensor_copy(
-            v_sc[:].rearrange("p (a t m) -> p a t m", a=PASSES, t=PACK),
-            v_picked_sc[:].rearrange("p (a m t) -> p a t m", a=PASSES, t=PACK),
-        )
-        gather_v(0)
-        wb_raw_sc = held("wb_raw_sc", [P, PASSES, N], U8, tag="v_picked_sc")
-        nc.vector.memset(wb_raw_sc[:].rearrange("p a n -> p (a n)").bitcast(I32), 0)
-        for q in range(4):
-            nc.scalar.dma_start(
-                wb_raw_sc[32 * q : 32 * q + 4, :, :].bitcast(I32),
-                wb_scales[:, 4 * q : 4 * q + 4, :].rearrange("a r n -> r a n").bitcast(I32),
-            )
-        gather_v(1)
-
-        wa_raw = [held("wa_raw0", [P, PACK, N], F32, tag="v_table1")]
-        nc.sync.dma_start(wa_raw[0][:], wa[0:PASS, :].rearrange("(p i) n -> p i n", i=PACK))
-
+                place_rows(nc.scalar, a, q)
         gather_x(0, None)
-        wa_raw.append(shared.tile([P, PACK, N], F32, name="wa_raw1", offset=0))
+        wa_raw = [held("wa_raw0", [P, PACK, N], F32, tag="x_table0")]
+        nc.sync.dma_start(wa_raw[0][:], wa[0:PASS, :].rearrange("(p i) n -> p i n", i=PACK))
+        gather_v(0)
+        wa_raw.append(held("wa_raw1", [P, PACK, N], F32, tag="v_table0"))
         nc.sync.dma_start(wa_raw[1][:], wa[PASS : 2 * PASS, :].rearrange("(p i) n -> p i n", i=PACK))
-        wb_raw = shared.tile([P, PASSES, 2 * N], U8, name="wb_raw", offset=GROUPED_AT)
-        nc.sync.dma_start(wb_raw[:].bitcast(I32), wb_words.rearrange("a p b -> p a b").bitcast(I32))
+        nc.vector.tensor_copy(
+            dealt_sc[:].rearrange("p (a t m) -> p a t m", a=PASSES, t=PACK),
+            placed_sc[:, S2:].rearrange("p (a m t) -> p a t m", a=PASSES, t=PACK),
+        )
+        gather_v(1)
         gather_x(1, None)
 
         tw_square = held("tw_square", [P, P], F32)
@@ -151,38 +137,21 @@ def tile_list_repurposing_mechanism_max_kernel(
 
         wa_codes = [held("wa_codes%d" % a, [P, N], U32) for a in range(PASSES)]
         wa_sc = [held("wa_sc%d" % a, [P, N], U8) for a in range(PASSES)]
-        wb_dealt = []
-
-        def round_wa(a, copies):
-            grouped = held("wa_grouped%d" % a, [P, N * PACK], BF16)
-            dealt = grouped[:].rearrange("p (t m i) -> p m i t", t=PACK, i=PACK)
-            raw = wa_raw[a][:].rearrange("p i (m t) -> p m i t", t=PACK)
-            for m0, copy in zip((0, P // 2), copies):
-                copy(dealt[:, m0 : m0 + P // 2], raw[:, m0 : m0 + P // 2])
-            return grouped
 
         def round_wa_pool(a):
             grouped = held("wa_grouped%d" % a, [P, N * PACK], BF16)
             dealt = grouped[:].rearrange("p (t m i) -> p m t i", t=PACK, i=PACK)
             raw = wa_raw[a][:].rearrange("p i (m t) -> p m t i", t=PACK)
             for m0 in (0, P // 2):
-                if (a, m0) == (0, P // 2):
-                    nc.scalar.copy(dealt[:, m0 : m0 + P // 2], raw[:, m0 : m0 + P // 2])
-                else:
-                    nc.gpsimd.tensor_scalar(dealt[:, m0 : m0 + P // 2], raw[:, m0 : m0 + P // 2], 1.0, 0.0, MULT, ADD)
+                nc.gpsimd.tensor_scalar(dealt[:, m0 : m0 + P // 2], raw[:, m0 : m0 + P // 2], 1.0, 0.0, MULT, ADD)
             return grouped
 
         def quantise_wa(a, grouped):
             nc.vector.quantize_mx(out=wa_codes[a][:].bitcast(FP8X4), scales=wa_sc[a][:], in_=grouped[:])
 
+        wb_codes = held("wb_codes", [P, PASSES, 2 * N], U8)
+
         def deal_wb():
-            wb_codes = shared.tile([P, PASSES, 2 * N], U8, name="wb_codes", offset=0, align_bytes=64)
-            wb_sc = shared.tile([P, PASSES, N], U8, name="wb_sc", offset=PASSES * 2 * N, align_bytes=64)
-            wb_dealt.extend([wb_codes, wb_sc])
-            nc.vector.tensor_copy(
-                wb_sc[:].rearrange("p a (t m) -> p a t m", t=PACK),
-                wb_raw_sc[:].rearrange("p a (m t) -> p a t m", t=PACK),
-            )
             nc.vector.tensor_copy(
                 wb_codes[:].bitcast(U16).rearrange("p a (t m) -> p a t m", t=PACK),
                 wb_raw[:].bitcast(U16).rearrange("p a (m t) -> p a t m", t=PACK),
@@ -212,9 +181,9 @@ def tile_list_repurposing_mechanism_max_kernel(
                             nc.tensor.matmul_mx(
                                 out=acc[:, e, :],
                                 lhsT=v_words[k][:, i0 : i0 + P].bitcast(FP8X4),
-                                lhsT_scale=v_sc[4 * k : P, i0 : i0 + P],
+                                lhsT_scale=dealt_sc[TABLE_ROW + 4 * k : P, i0 : i0 + P],
                                 rhs=x_words[k][:, j0 : j0 + w].bitcast(FP8X4),
-                                rhs_scale=x_sc[X_ROW + 4 * k : P, j0 : j0 + w],
+                                rhs_scale=placed_sc[TABLE_ROW + 4 * k : P, j0 : j0 + w],
                                 start=(k == 0 and e == 0),
                                 stop=(k == PASSES - 1 and e == per_bank - 1),
                             )
@@ -249,9 +218,27 @@ def tile_list_repurposing_mechanism_max_kernel(
             cols = slice(j0, j0 + w)
             fp4_n = w if w == BANK else FP4_N
             y = held("y%d" % j0, [P, PACK, w], F32)
+            from_wb = []
+            for b in range(banks):
+                acc_b = pool.tile([P, per_bank, w], F32, name="acc_b", tag=tags[1])
+                for e in range(per_bank):
+                    n0 = (b * per_bank + e) * P
+                    for c0 in range(0, w, fp4_n):
+                        for a in range(PASSES):
+                            nc.tensor.matmul_mx(
+                                out=acc_b[:, e, c0 : c0 + fp4_n],
+                                lhsT=wb_codes[:, a, 2 * n0 : 2 * (n0 + P)].bitcast(FP4X4),
+                                lhsT_scale=dealt_sc[:, a * N + n0 : a * N + n0 + P],
+                                rhs=h_codes[a][:, j0 + c0 : j0 + c0 + fp4_n].bitcast(FP8X4),
+                                rhs_scale=h_sc[a][:, j0 + c0 : j0 + c0 + fp4_n],
+                                start=(a == 0),
+                                stop=(a == PASSES - 1),
+                            )
+                yb = ring.tile([P, per_bank, w], F32, name="yb", align_bytes=64, bufs=4)
+                nc.scalar.copy(yb[:], acc_b[:])
+                from_wb.append(yb)
             for b in range(banks):
                 acc_a = pool.tile([P, per_bank, w], F32, name="acc_a", tag=tags[0])
-                acc_b = pool.tile([P, per_bank, w], F32, name="acc_b", tag=tags[1])
                 for e in range(per_bank):
                     n0 = (b * per_bank + e) * P
                     for a in range(PASSES):
@@ -264,23 +251,8 @@ def tile_list_repurposing_mechanism_max_kernel(
                             start=(a == 0),
                             stop=(a == PASSES - 1),
                         )
-                for e in range(per_bank):
-                    n0 = (b * per_bank + e) * P
-                    for c0 in range(0, w, fp4_n):
-                        for a in range(PASSES):
-                            nc.tensor.matmul_mx(
-                                out=acc_b[:, e, c0 : c0 + fp4_n],
-                                lhsT=wb_dealt[0][:, a, 2 * n0 : 2 * (n0 + P)].bitcast(FP4X4),
-                                lhsT_scale=wb_dealt[1][:, a, n0 : n0 + P],
-                                rhs=h_codes[a][:, j0 + c0 : j0 + c0 + fp4_n].bitcast(FP8X4),
-                                rhs_scale=h_sc[a][:, j0 + c0 : j0 + c0 + fp4_n],
-                                start=(a == 0),
-                                stop=(a == PASSES - 1),
-                            )
-                ya = ring.tile([P, per_bank, w], F32, name="ya", align_bytes=64)
-                nc.scalar.copy(ya[:], acc_a[:])
                 rows = slice(b * per_bank, (b + 1) * per_bank)
-                nc.vector.tensor_tensor(y[:, rows, :], acc_b[:], ya[:], MAX)
+                nc.vector.tensor_tensor(y[:, rows, :], acc_a[:], from_wb[b][:], MAX)
                 if b % 2 == 1 or banks == 1:
                     done = slice(max(b - 1, 0) * per_bank, (b + 1) * per_bank)
                     nc.sync.dma_start(y_rows[:, done, cols], y[:, done, :])
@@ -304,9 +276,9 @@ def tile_list_repurposing_mechanism_max_kernel(
         effects(512, 256)
         effects(768, 128)
         effects(896, 128)
+        deal_wb()
         weigh(0, 256)
         weigh(256, 256)
-        deal_wb()
         quantise_h(0, 512)
         quantise_wa(0, grouped[0])
         quantise_wa(1, grouped[1])

@@ -80,9 +80,20 @@ def tile_list_repurposing_mechanism_max_kernel(
         nc.sync.dma_start(x_table[0][:].bitcast(I32), as_words(tab2_words[0]))
         nc.sync.dma_start(v_table[0][:].bitcast(I32), as_words(tab_words[0]))
         nc.sync.dma_start(v_table[1][:].bitcast(I32), as_words(tab_words[1]))
+        wa_raw = {}
+
+        def load_wa(a, u, tag):
+            wa_raw[a, u] = held("wa_raw%d%d" % (a, u), [P, PACK, N // 2], F32, tag=tag)
+            rows = wa[a * PASS : (a + 1) * PASS, u * (N // 2) : (u + 1) * (N // 2)]
+            nc.sync.dma_start(wa_raw[a, u][:], rows.rearrange("(p i) n -> p i n", i=PACK))
+
         nc.sync.dma_start(x_table[1][:].bitcast(I32), as_words(tab2_words[1]))
         wb_raw = held("wb_raw", [P, PASSES, 2 * N], U8)
         nc.sync.dma_start(wb_raw[:].bitcast(I32), wb_words.rearrange("a p b -> p a b").bitcast(I32))
+        load_wa(0, 0, None)
+        load_wa(0, 1, None)
+        load_wa(1, 0, None)
+        load_wa(1, 1, None)
 
         v_words = [held("v_words%d" % k, [P, S], U32) for k in range(PASSES)]
         x_words = {}
@@ -95,10 +106,9 @@ def tile_list_repurposing_mechanism_max_kernel(
                 v_words[k][:].rearrange("p (a t m) -> p a m t", a=PASSES, t=PACK), v_table[k][:].indirect(list_v[:])
             )
 
-        def gather_x(k, tag):
-            x_words[k] = held("x_words%d" % k, [P, S2], U32, tag=tag)
-            for u in range(2):
-                nc.vector.tensor_copy(x_words[k][:, u * HALF : (u + 1) * HALF], x_table[k][:].indirect(half_list(u)))
+        def gather_x(k, u, tag):
+            x_words[k, u] = held("x_words%d%d" % (k, u), [P, HALF], U32, tag=tag)
+            nc.vector.tensor_copy(x_words[k, u][:], x_table[k][:].indirect(half_list(u)))
 
         def place_rows(queue, a, q):
             row = 32 * q + TABLE_ROW + 4 * a
@@ -110,18 +120,21 @@ def tile_list_repurposing_mechanism_max_kernel(
         for a in range(PASSES):
             for q in range(4):
                 place_rows(nc.scalar, a, q)
-        gather_x(0, None)
-        wa_raw = [held("wa_raw0", [P, PACK, N], F32, tag="x_table0")]
-        nc.sync.dma_start(wa_raw[0][:], wa[0:PASS, :].rearrange("(p i) n -> p i n", i=PACK))
+        gather_x(0, 0, None)
+        gather_x(0, 1, None)
         gather_v(0)
-        wa_raw.append(held("wa_raw1", [P, PACK, N], F32, tag="v_table0"))
-        nc.sync.dma_start(wa_raw[1][:], wa[PASS : 2 * PASS, :].rearrange("(p i) n -> p i n", i=PACK))
         nc.vector.tensor_copy(
             dealt_sc[:].rearrange("p (a t m) -> p a t m", a=PASSES, t=PACK),
             placed_sc[:, S2:].rearrange("p (a m t) -> p a t m", a=PASSES, t=PACK),
         )
         gather_v(1)
-        gather_x(1, None)
+        gather_x(1, 0, None)
+        wb_codes = held("wb_codes", [P, PASSES, 2 * N], U8)
+        nc.vector.tensor_copy(
+            wb_codes[:].bitcast(U16).rearrange("p a (t m) -> p a t m", t=PACK),
+            wb_raw[:].bitcast(U16).rearrange("p a (m t) -> p a t m", t=PACK),
+        )
+        gather_x(1, 1, "wb_raw")
 
         tw_square = held("tw_square", [P, P], F32)
         tw_turned = held("tw_turned", [P, P], F32)
@@ -135,27 +148,15 @@ def tile_list_repurposing_mechanism_max_kernel(
         tw_bank = psum_w.tile([P, P], F32, name="tw_bank")
         nc.tensor.transpose(tw_bank[:], tw_turned[:], identity[:])
 
-        wa_codes = [held("wa_codes%d" % a, [P, N], U32) for a in range(PASSES)]
-        wa_sc = [held("wa_sc%d" % a, [P, N], U8) for a in range(PASSES)]
+        wa_codes = held("wa_codes", [P, PASSES * N], U32)
+        wa_sc = held("wa_sc", [P, PASSES * N], U8)
+        grouped = held("wa_grouped", [P, PASSES * N * PACK], BF16)
 
-        def round_wa_pool(a):
-            grouped = held("wa_grouped%d" % a, [P, N * PACK], BF16)
-            dealt = grouped[:].rearrange("p (t m i) -> p m t i", t=PACK, i=PACK)
-            raw = wa_raw[a][:].rearrange("p i (m t) -> p m t i", t=PACK)
-            for m0 in (0, P // 2):
-                nc.gpsimd.tensor_scalar(dealt[:, m0 : m0 + P // 2], raw[:, m0 : m0 + P // 2], 1.0, 0.0, MULT, ADD)
-            return grouped
-
-        def quantise_wa(a, grouped):
-            nc.vector.quantize_mx(out=wa_codes[a][:].bitcast(FP8X4), scales=wa_sc[a][:], in_=grouped[:])
-
-        wb_codes = held("wb_codes", [P, PASSES, 2 * N], U8)
-
-        def deal_wb():
-            nc.vector.tensor_copy(
-                wb_codes[:].bitcast(U16).rearrange("p a (t m) -> p a t m", t=PACK),
-                wb_raw[:].bitcast(U16).rearrange("p a (m t) -> p a t m", t=PACK),
-            )
+        def round_wa(a, u):
+            dealt = grouped[:].rearrange("p (a t m i) -> p a m t i", a=PASSES, t=PACK, i=PACK)
+            out = dealt[:, a, u * (P // 2) : (u + 1) * (P // 2)]
+            raw = wa_raw[a, u][:].rearrange("p i (m t) -> p m t i", t=PACK)
+            nc.gpsimd.tensor_scalar(out, raw, 1.0, 0.0, MULT, ADD)
 
         y_codes = held("y_codes", [P, S2], U32)
         y_sc = held("y_sc", [P, S2], U8)
@@ -182,22 +183,22 @@ def tile_list_repurposing_mechanism_max_kernel(
                                 out=acc[:, e, :],
                                 lhsT=v_words[k][:, i0 : i0 + P].bitcast(FP8X4),
                                 lhsT_scale=dealt_sc[TABLE_ROW + 4 * k : P, i0 : i0 + P],
-                                rhs=x_words[k][:, j0 : j0 + w].bitcast(FP8X4),
+                                rhs=x_words[k, j0 // HALF][:, j0 % HALF : j0 % HALF + w].bitcast(FP8X4),
                                 rhs_scale=placed_sc[TABLE_ROW + 4 * k : P, j0 : j0 + w],
                                 start=(k == 0 and e == 0),
                                 stop=(k == PASSES - 1 and e == per_bank - 1),
                             )
                     nc.scalar.activation(th[:, b], acc[:].rearrange("p e n -> p n e"), TANH)
 
-        def weigh(j0, w):
+        def weigh(j0, w, engine, weights):
             per_bank = BANK // w
             banks = PACK // per_bank
             for a in range(PASSES):
                 th = saturated[j0, a]
-                nc.vector.tensor_tensor(
+                engine.tensor_tensor(
                     h[a][:, PACK * j0 : PACK * (j0 + w)].rearrange("p (n b e) -> p n b e", b=banks, e=per_bank),
                     th[:].rearrange("p b n e -> p n b e"),
-                    tw_bank[:, PACK * a : PACK * (a + 1)]
+                    weights[:, PACK * a : PACK * (a + 1)]
                     .rearrange("p (n b e) -> p n b e", n=1, b=banks)
                     .broadcast_to([P, w, banks, per_bank]),
                     MULT,
@@ -244,8 +245,8 @@ def tile_list_repurposing_mechanism_max_kernel(
                     for a in range(PASSES):
                         nc.tensor.matmul_mx(
                             out=acc_a[:, e, :],
-                            lhsT=wa_codes[a][:, n0 : n0 + P].bitcast(FP8X4),
-                            lhsT_scale=wa_sc[a][:, n0 : n0 + P],
+                            lhsT=wa_codes[:, a * N + n0 : a * N + n0 + P].bitcast(FP8X4),
+                            lhsT_scale=wa_sc[:, a * N + n0 : a * N + n0 + P],
                             rhs=h_codes[a][:, cols].bitcast(FP8X4),
                             rhs_scale=h_sc[a][:, cols],
                             start=(a == 0),
@@ -270,31 +271,31 @@ def tile_list_repurposing_mechanism_max_kernel(
                 nc.vector.quantize_mx(out=y_codes[:, cols].bitcast(FP8X4), scales=y_sc[:, cols], in_=y16[:])
             nc.sync.dma_start(y_words[:, j0 : j0 + w], y_codes[:, j0 : j0 + w].bitcast(I32))
 
+        for a in range(PASSES):
+            for u in range(2):
+                round_wa(a, u)
         effects(0, 256)
         effects(256, 256)
-        grouped = [round_wa_pool(0), round_wa_pool(1)]
         effects(512, 256)
         effects(768, 128)
         effects(896, 128)
-        deal_wb()
-        weigh(0, 256)
-        weigh(256, 256)
+        weigh(0, 256, nc.vector, tw_bank)
+        weigh(256, 256, nc.vector, tw_bank)
         quantise_h(0, 512)
-        quantise_wa(0, grouped[0])
-        quantise_wa(1, grouped[1])
-        weigh(512, 256)
-        y0 = scores(0, 512, psum_a, ("acc", "acc"))
+        nc.vector.quantize_mx(out=wa_codes[:].bitcast(FP8X4), scales=wa_sc[:], in_=grouped[:])
+        weigh(768, 128, nc.gpsimd, tw_sb[:, 0, :])
+        weigh(896, 128, nc.gpsimd, tw_sb[:, 0, :])
+        weigh(512, 256, nc.vector, tw_bank)
         quantise_h(512, 256)
-        weigh(768, 128)
-        weigh(896, 128)
+        y0 = scores(0, 512, psum_a, ("acc", "acc"))
         quantise_h(768, 128)
         quantise_h(896, 128)
         y1 = scores(512, 256, psum_a, ("acc", "acc"))
-        planes(0, 512, y0, nc.scalar.copy)
         y2 = scores(768, 128, psum_a, ("acc", "acc"))
         y3 = scores(896, 128, psum_a, ("acc", "acc"))
+        planes(0, 512, y0, nc.scalar.copy)
         planes(512, 256, y1, nc.scalar.copy)
-        planes(768, 128, y2, nc.scalar.copy)
+        planes(768, 128, y2, nc.vector.tensor_copy)
         planes(896, 128, y3, nc.vector.tensor_copy)
         for q in range(4):
             queue = nc.sync if q % 2 == 0 else nc.scalar

@@ -79,29 +79,15 @@ def tile_list_repurposing_mechanism_max_kernel(
         nc.sync.dma_start(v_table_sc[WHOLE_AT:P, :].bitcast(I32), tab_scales.rearrange("a q t -> (a q) t").bitcast(I32))
         nc.sync.dma_start(x_table[0][:].bitcast(I32), as_words(tab2_words[0]))
         nc.sync.dma_start(v_table[0][:].bitcast(I32), as_words(tab_words[0]))
-        nc.sync.dma_start(v_table[1][:].bitcast(I32), as_words(tab_words[1]))
-        wa_raw = {}
 
-        def load_wa(a, u, tag):
-            wa_raw[a, u] = held("wa_raw%d%d" % (a, u), [P, PACK, N // 2], F32, tag=tag)
-            rows = wa[a * PASS : (a + 1) * PASS, u * (N // 2) : (u + 1) * (N // 2)]
-            nc.sync.dma_start(wa_raw[a, u][:], rows.rearrange("(p i) n -> p i n", i=PACK))
-
-        nc.sync.dma_start(x_table[1][:].bitcast(I32), as_words(tab2_words[1]))
-        wb_raw = held("wb_raw", [P, PASSES, 2 * N], U8)
-        nc.sync.dma_start(wb_raw[:].bitcast(I32), wb_words.rearrange("a p b -> p a b").bitcast(I32))
-        load_wa(0, 0, None)
-        load_wa(0, 1, None)
-        load_wa(1, 0, None)
-        load_wa(1, 1, None)
-
-        v_words = [held("v_words%d" % k, [P, S], U32) for k in range(PASSES)]
+        v_words = {}
         x_words = {}
 
         def half_list(u):
             return list_x[:, u * (HALF // 16) : (u + 1) * (HALF // 16)]
 
-        def gather_v(k):
+        def gather_v(k, tag):
+            v_words[k] = held("v_words%d" % k, [P, S], U32, tag=tag)
             nc.vector.tensor_copy(
                 v_words[k][:].rearrange("p (a t m) -> p a m t", a=PASSES, t=PACK), v_table[k][:].indirect(list_v[:])
             )
@@ -117,17 +103,35 @@ def tile_list_repurposing_mechanism_max_kernel(
 
         nc.vector.tensor_copy(picked_sc[:, 0:S2], x_table_sc[:].indirect(list_x[:]))
         nc.vector.tensor_copy(picked_sc[:, S2:], v_table_sc[:].indirect(list_v[:]))
-        for a in range(PASSES):
-            for q in range(4):
-                place_rows(nc.scalar, a, q)
+        blocks = [(a, q) for a in range(PASSES) for q in range(4)]
+        for a, q in blocks[:2]:
+            place_rows(nc.sync, a, q)
+        nc.sync.dma_start(v_table[1][:].bitcast(I32), as_words(tab_words[1]))
+        for a, q in blocks[2:]:
+            place_rows(nc.sync, a, q)
+        wa_raw = {}
+
+        def load_wa(a, u, tag):
+            wa_raw[a, u] = held("wa_raw%d%d" % (a, u), [P, PACK, N // 2], F32, tag=tag)
+            rows = wa[a * PASS : (a + 1) * PASS, u * (N // 2) : (u + 1) * (N // 2)]
+            nc.sync.dma_start(wa_raw[a, u][:], rows.rearrange("(p i) n -> p i n", i=PACK))
+
+        nc.sync.dma_start(x_table[1][:].bitcast(I32), as_words(tab2_words[1]))
+        wb_raw = held("wb_raw", [P, PASSES, 2 * N], U8)
+        nc.sync.dma_start(wb_raw[:].bitcast(I32), wb_words.rearrange("a p b -> p a b").bitcast(I32))
+        load_wa(0, 0, None)
+        load_wa(0, 1, None)
+        load_wa(1, 0, None)
+        load_wa(1, 1, None)
+
         gather_x(0, 0, None)
         gather_x(0, 1, None)
-        gather_v(0)
+        gather_v(0, None)
         nc.vector.tensor_copy(
             dealt_sc[:].rearrange("p (a t m) -> p a t m", a=PASSES, t=PACK),
             placed_sc[:, S2:].rearrange("p (a m t) -> p a t m", a=PASSES, t=PACK),
         )
-        gather_v(1)
+        gather_v(1, "picked_sc")
         gather_x(1, 0, None)
         wb_codes = held("wb_codes", [P, PASSES, 2 * N], U8)
         nc.vector.tensor_copy(

@@ -64,11 +64,6 @@ def tile_list_repurposing_mechanism_max_kernel(
         for plane in (x_table_sc, v_table_sc):
             nc.vector.memset(plane[0:WHOLE_AT, :].bitcast(I32), 0)
 
-        for q in range(4):
-            nc.gpsimd.dma_start(
-                placed_sc[32 * q : 32 * q + 4, S2:].rearrange("r (a n) -> r a n", a=PASSES).bitcast(I32),
-                wb_scales[:, 4 * q : 4 * q + 4, :].rearrange("a r n -> r a n").bitcast(I32),
-            )
         nc.gpsimd.dma_start(
             tw_sb[:, 0, :].rearrange("p (a t) -> p a t", a=PASSES), tw.rearrange("(a p t) -> p a t", a=PASSES, t=PACK)
         )
@@ -79,6 +74,11 @@ def tile_list_repurposing_mechanism_max_kernel(
         nc.sync.dma_start(v_table_sc[WHOLE_AT:P, :].bitcast(I32), tab_scales.rearrange("a q t -> (a q) t").bitcast(I32))
         nc.sync.dma_start(x_table[0][:].bitcast(I32), as_words(tab2_words[0]))
         nc.sync.dma_start(v_table[0][:].bitcast(I32), as_words(tab_words[0]))
+        for q in range(4):
+            nc.sync.dma_start(
+                placed_sc[32 * q : 32 * q + 4, S2:].rearrange("r (a n) -> r a n", a=PASSES).bitcast(I32),
+                wb_scales[:, 4 * q : 4 * q + 4, :].rearrange("a r n -> r a n").bitcast(I32),
+            )
 
         v_words = {}
         x_words = {}
@@ -162,7 +162,6 @@ def tile_list_repurposing_mechanism_max_kernel(
             raw = wa_raw[a, u][:].rearrange("p i (m t) -> p m t i", t=PACK)
             nc.gpsimd.tensor_scalar(out, raw, 1.0, 0.0, MULT, ADD)
 
-        y_codes = held("y_codes", [P, S2], U32)
         y_sc = held("y_sc", [P, S2], U8)
         y_rows = out_0.rearrange("(p t) j -> p t j", t=PACK)
         y_words = as_words(out_1[0])
@@ -176,7 +175,7 @@ def tile_list_repurposing_mechanism_max_kernel(
             per_bank = BANK // w
             banks = PACK // per_bank
             for a in range(PASSES):
-                th = ring.tile([P, banks, w, per_bank], F32, name="th", align_bytes=64, bufs=10)
+                th = ring.tile([P, banks, w, per_bank], F32, name="th", align_bytes=64, bufs=8)
                 saturated[j0, a] = th
                 for b in range(banks):
                     acc = psum_a.tile([P, per_bank, w], F32, name="acc")
@@ -194,19 +193,26 @@ def tile_list_repurposing_mechanism_max_kernel(
                             )
                     nc.scalar.activation(th[:, b], acc[:].rearrange("p e n -> p n e"), TANH)
 
-        def weigh(j0, w, engine, weights):
+        def weigh(j0, w, a, first, last, engine, weights):
             per_bank = BANK // w
             banks = PACK // per_bank
-            for a in range(PASSES):
-                th = saturated[j0, a]
-                engine.tensor_tensor(
-                    h[a][:, PACK * j0 : PACK * (j0 + w)].rearrange("p (n b e) -> p n b e", b=banks, e=per_bank),
-                    th[:].rearrange("p b n e -> p n b e"),
-                    weights[:, PACK * a : PACK * (a + 1)]
-                    .rearrange("p (n b e) -> p n b e", n=1, b=banks)
-                    .broadcast_to([P, w, banks, per_bank]),
-                    MULT,
-                )
+            th = saturated[j0, a]
+            engine.tensor_tensor(
+                h[a][:, PACK * (j0 + first) : PACK * (j0 + last)].rearrange(
+                    "p (n b e) -> p n b e", b=banks, e=per_bank
+                ),
+                th[:, :, first:last, :].rearrange("p b n e -> p n b e"),
+                weights[:, PACK * a : PACK * (a + 1)]
+                .rearrange("p (n b e) -> p n b e", n=1, b=banks)
+                .broadcast_to([P, last - first, banks, per_bank]),
+                MULT,
+            )
+
+        def weigh_vector(j0, w, a, first, last):
+            weigh(j0, w, a, first, last, nc.vector, tw_bank)
+
+        def weigh_pool(j0, w, a, first, last):
+            weigh(j0, w, a, first, last, nc.gpsimd, tw_sb[:, 0, :])
 
         def quantise_h(j0, w):
             cols = slice(j0, j0 + w)
@@ -239,7 +245,7 @@ def tile_list_repurposing_mechanism_max_kernel(
                                 start=(a == 0),
                                 stop=(a == PASSES - 1),
                             )
-                yb = ring.tile([P, per_bank, w], F32, name="yb", align_bytes=64, bufs=4)
+                yb = held("yb%d_%d" % (j0, b), [P, per_bank, w], F32)
                 nc.scalar.copy(yb[:], acc_b[:])
                 from_wb.append(yb)
             for b in range(banks):
@@ -263,10 +269,14 @@ def tile_list_repurposing_mechanism_max_kernel(
                     nc.sync.dma_start(y_rows[:, done, cols], y[:, done, :])
             return y
 
-        def planes(j0, w, y, copy):
-            for c0 in range(0, w, WIDE):
+        def pool_copy(out, in_):
+            order = "p c t i -> p c i t"
+            nc.gpsimd.tensor_scalar(out.rearrange(order), in_.rearrange(order), 1.0, 0.0, MULT, ADD)
+
+        def planes(j0, w, y, copies):
+            for c0, copy in zip(range(0, w, WIDE), copies):
                 n = min(w, WIDE)
-                y16 = ring.tile([P, n * PACK], BF16, name="y16", align_bytes=64)
+                y16 = ring.tile([P, n * PACK], BF16, name="y16", align_bytes=64, bufs=5)
                 copy(
                     y16[:].rearrange("p (c i t) -> p c t i", i=4, t=PACK),
                     y[:, :, c0 : c0 + n].rearrange("p t (c i) -> p c t i", i=4),
@@ -283,13 +293,16 @@ def tile_list_repurposing_mechanism_max_kernel(
         effects(512, 256)
         effects(768, 128)
         effects(896, 128)
-        weigh(0, 256, nc.vector, tw_bank)
-        weigh(256, 256, nc.vector, tw_bank)
+        for j0 in (0, 256):
+            for a in range(PASSES):
+                weigh_vector(j0, 256, a, 0, 256)
         quantise_h(0, 512)
         nc.vector.quantize_mx(out=wa_codes[:].bitcast(FP8X4), scales=wa_sc[:], in_=grouped[:])
-        weigh(768, 128, nc.gpsimd, tw_sb[:, 0, :])
-        weigh(896, 128, nc.gpsimd, tw_sb[:, 0, :])
-        weigh(512, 256, nc.vector, tw_bank)
+        for j0 in (768, 896):
+            for a in range(PASSES):
+                weigh_pool(j0, 128, a, 0, 128)
+        weigh_vector(512, 256, 0, 0, 256)
+        weigh_vector(512, 256, 1, 0, 256)
         quantise_h(512, 256)
         y0 = scores(0, 512, psum_a, ("acc", "acc"))
         quantise_h(768, 128)
@@ -297,10 +310,11 @@ def tile_list_repurposing_mechanism_max_kernel(
         y1 = scores(512, 256, psum_a, ("acc", "acc"))
         y2 = scores(768, 128, psum_a, ("acc", "acc"))
         y3 = scores(896, 128, psum_a, ("acc", "acc"))
-        planes(0, 512, y0, nc.scalar.copy)
-        planes(512, 256, y1, nc.scalar.copy)
-        planes(768, 128, y2, nc.vector.tensor_copy)
-        planes(896, 128, y3, nc.vector.tensor_copy)
+        y_codes = held("y_codes", [P, S2], U32, tag="yb768_0")
+        planes(0, 512, y0, [nc.scalar.copy, pool_copy])
+        planes(512, 256, y1, [nc.scalar.copy])
+        planes(768, 128, y2, [nc.scalar.copy])
+        planes(896, 128, y3, [nc.vector.tensor_copy])
         for q in range(4):
             queue = nc.sync if q % 2 == 0 else nc.scalar
             queue.dma_start(out_2[0, 4 * q : 4 * q + 4, :].bitcast(I32), y_sc[32 * q : 32 * q + 4, :].bitcast(I32))

@@ -87,9 +87,12 @@ def tile_list_repurposing_mechanism_max_kernel(
             return list_x[:, u * (HALF // 16) : (u + 1) * (HALF // 16)]
 
         def gather_v(k, tag):
-            v_words[k] = held("v_words%d" % k, [P, S], U32, tag=tag)
+            v_words[k] = held("v_words%d" % k, [P, S], U32)
+            picked = held("v_picked%d" % k, [P, S], U32, tag=tag)
+            nc.vector.tensor_copy(picked[:], v_table[k][:].indirect(list_v[:]))
             nc.vector.tensor_copy(
-                v_words[k][:].rearrange("p (a t m) -> p a m t", a=PASSES, t=PACK), v_table[k][:].indirect(list_v[:])
+                v_words[k][:].rearrange("p (a t c i) -> p a c t i", a=PASSES, t=PACK, i=4),
+                picked[:].rearrange("p (a c i t) -> p a c t i", a=PASSES, t=PACK, i=4),
             )
 
         def gather_x(k, u, tag):
@@ -291,16 +294,15 @@ def tile_list_repurposing_mechanism_max_kernel(
         effects(0, 256)
         effects(256, 256)
         effects(512, 256)
-        effects(768, 128)
-        effects(896, 128)
+        effects(768, 256)
         for j0 in (0, 256):
             for a in range(PASSES):
                 weigh_vector(j0, 256, a, 0, 256)
         quantise_h(0, 512)
         nc.vector.quantize_mx(out=wa_codes[:].bitcast(FP8X4), scales=wa_sc[:], in_=grouped[:])
-        for j0 in (768, 896):
+        for first in (0, 128):
             for a in range(PASSES):
-                weigh_pool(j0, 128, a, 0, 128)
+                weigh_pool(768, 256, a, first, first + 128)
         weigh_vector(512, 256, 0, 0, 256)
         weigh_vector(512, 256, 1, 0, 256)
         quantise_h(512, 256)

@@ -24,12 +24,11 @@ PACK = 4
 PASS = P * PACK
 PASSES = 2
 BANK = 512
-HALF = S2 // 2
-FP4_N = 128
-GROUPS = (512, 256, 128, 128)
-WIDE = 256
+CHUNK = 256
 TABLE_ROW = 4
 WHOLE_AT = 96
+POOL_SHARE = 192
+QUADRANTS = (0, 2, 1, 3)
 
 
 def tile_list_repurposing_mechanism_max_kernel(
@@ -38,8 +37,7 @@ def tile_list_repurposing_mechanism_max_kernel(
     nc = tc.nc
     with ExitStack() as ctx:
         keep = ctx.enter_context(tc.tile_pool(name="keep", bufs=1))
-        ring = ctx.enter_context(tc.tile_pool(name="ring", bufs=3))
-        psum_a = ctx.enter_context(tc.psum_pool(name="psum_a", bufs=7))
+        psum = ctx.enter_context(tc.psum_pool(name="psum", bufs=7))
         psum_w = ctx.enter_context(tc.psum_pool(name="psum_w", bufs=1))
 
         def held(name, shape, dtype, tag=None):
@@ -60,88 +58,86 @@ def tile_list_repurposing_mechanism_max_kernel(
         tw_sb = held("tw_sb", [P, 1, PASSES * PACK], F32)
         identity = held("identity", [P, P], F32)
 
-        nc.gpsimd.memset(placed_sc[:].bitcast(I32), 0)
-        for plane in (x_table_sc, v_table_sc):
+        make_identity(nc, identity[:])
+        nc.vector.memset(placed_sc[:].bitcast(I32), 0)
+        for plane in (v_table_sc, x_table_sc):
             nc.vector.memset(plane[0:WHOLE_AT, :].bitcast(I32), 0)
 
         nc.gpsimd.dma_start(
             tw_sb[:, 0, :].rearrange("p (a t) -> p a t", a=PASSES), tw.rearrange("(a p t) -> p a t", a=PASSES, t=PACK)
         )
-        make_identity(nc, identity[:])
-        nc.sync.dma_start(list_x[:], offs2)
-        nc.sync.dma_start(x_table_sc[WHOLE_AT:P, :].bitcast(I32), tab2_scales.rearrange("a q t -> (a q) t").bitcast(I32))
         nc.sync.dma_start(list_v[:], offs)
         nc.sync.dma_start(v_table_sc[WHOLE_AT:P, :].bitcast(I32), tab_scales.rearrange("a q t -> (a q) t").bitcast(I32))
-        nc.sync.dma_start(x_table[0][:].bitcast(I32), as_words(tab2_words[0]))
+        nc.sync.dma_start(list_x[:], offs2)
+        nc.sync.dma_start(x_table_sc[WHOLE_AT:P, :].bitcast(I32), tab2_scales.rearrange("a q t -> (a q) t").bitcast(I32))
         nc.sync.dma_start(v_table[0][:].bitcast(I32), as_words(tab_words[0]))
-        for q in range(4):
+        nc.sync.dma_start(x_table[0][:].bitcast(I32), as_words(tab2_words[0]))
+        for q in QUADRANTS:
             nc.sync.dma_start(
                 placed_sc[32 * q : 32 * q + 4, S2:].rearrange("r (a n) -> r a n", a=PASSES).bitcast(I32),
                 wb_scales[:, 4 * q : 4 * q + 4, :].rearrange("a r n -> r a n").bitcast(I32),
             )
 
-        v_words = {}
-        x_words = {}
+        def entries(lst, j0, n):
+            return lst[:, j0 // 16 : (j0 + n) // 16]
 
-        def half_list(u):
-            return list_x[:, u * (HALF // 16) : (u + 1) * (HALF // 16)]
+        v_words = [held("v_words%d" % k, [P, S], U32) for k in range(PASSES)]
+        x_words = [held("x_words%d" % k, [P, S2], U32) for k in range(PASSES)]
 
         def gather_v(k, tag):
-            v_words[k] = held("v_words%d" % k, [P, S], U32)
             picked = held("v_picked%d" % k, [P, S], U32, tag=tag)
-            nc.vector.tensor_copy(picked[:], v_table[k][:].indirect(list_v[:]))
-            nc.vector.tensor_copy(
-                v_words[k][:].rearrange("p (a t c i) -> p a c t i", a=PASSES, t=PACK, i=4),
-                picked[:].rearrange("p (a c i t) -> p a c t i", a=PASSES, t=PACK, i=4),
-            )
+            for a in range(PASSES):
+                nc.vector.tensor_copy(
+                    picked[:, a * PASS : (a + 1) * PASS], v_table[k][:].indirect(entries(list_v, a * PASS, PASS))
+                )
+            for a in range(PASSES):
+                nc.vector.tensor_copy(
+                    v_words[k][:, a * PASS : (a + 1) * PASS].rearrange("p (t c i) -> p c t i", t=PACK, i=4),
+                    picked[:, a * PASS : (a + 1) * PASS].rearrange("p (c i t) -> p c t i", t=PACK, i=4),
+                )
 
-        def gather_x(k, u, tag):
-            x_words[k, u] = held("x_words%d%d" % (k, u), [P, HALF], U32, tag=tag)
-            nc.vector.tensor_copy(x_words[k, u][:], x_table[k][:].indirect(half_list(u)))
+        def gather_x(k, j0, n):
+            nc.vector.tensor_copy(x_words[k][:, j0 : j0 + n], x_table[k][:].indirect(entries(list_x, j0, n)))
 
-        def place_rows(queue, a, q):
+        def place_rows(a, q):
             row = 32 * q + TABLE_ROW + 4 * a
             src = WHOLE_AT + 16 * a + 4 * q
-            queue.dma_start(placed_sc[row : row + 4, :].bitcast(I32), picked_sc[src : src + 4, :].bitcast(I32))
+            nc.sync.dma_start(placed_sc[row : row + 4, :].bitcast(I32), picked_sc[src : src + 4, :].bitcast(I32))
 
-        nc.vector.tensor_copy(picked_sc[:, 0:S2], x_table_sc[:].indirect(list_x[:]))
         nc.vector.tensor_copy(picked_sc[:, S2:], v_table_sc[:].indirect(list_v[:]))
-        blocks = [(a, q) for a in range(PASSES) for q in range(4)]
+        nc.vector.tensor_copy(picked_sc[:, 0:S2], x_table_sc[:].indirect(list_x[:]))
+        blocks = [(a, q + 2 * half) for q in range(2) for a in range(PASSES) for half in range(2)]
         for a, q in blocks[:2]:
-            place_rows(nc.sync, a, q)
+            place_rows(a, q)
         nc.sync.dma_start(v_table[1][:].bitcast(I32), as_words(tab_words[1]))
         for a, q in blocks[2:]:
-            place_rows(nc.sync, a, q)
-        wa_raw = {}
-
-        def load_wa(a, u, tag):
-            wa_raw[a, u] = held("wa_raw%d%d" % (a, u), [P, PACK, N // 2], F32, tag=tag)
-            rows = wa[a * PASS : (a + 1) * PASS, u * (N // 2) : (u + 1) * (N // 2)]
-            nc.sync.dma_start(wa_raw[a, u][:], rows.rearrange("(p i) n -> p i n", i=PACK))
-
+            place_rows(a, q)
         nc.sync.dma_start(x_table[1][:].bitcast(I32), as_words(tab2_words[1]))
-        wb_raw = held("wb_raw", [P, PASSES, 2 * N], U8)
-        nc.sync.dma_start(wb_raw[:].bitcast(I32), wb_words.rearrange("a p b -> p a b").bitcast(I32))
-        load_wa(0, 0, None)
-        load_wa(0, 1, None)
-        load_wa(1, 0, None)
-        load_wa(1, 1, None)
+        wide = PACK * CHUNK
+        corner = PACK * P // 2
+        wa_at = wide + PACK * (CHUNK - POOL_SHARE)
+        wa_end = wa_at + PASSES * N * PACK
+        wb_raw = [held("wb_raw%d" % a, [P, 2 * N], U8) for a in range(PASSES)]
+        for a in range(PASSES):
+            nc.sync.dma_start(wb_raw[a][:].bitcast(I32), wb_words[a].bitcast(I32))
+        wa_raw = {}
+        for a in range(PASSES):
+            for u in range(2):
+                wa_raw[a, u] = held("wa_raw%d%d" % (a, u), [P, PACK, N // 2], F32)
+                rows = wa[a * PASS : (a + 1) * PASS, u * (N // 2) : (u + 1) * (N // 2)]
+                nc.sync.dma_start(wa_raw[a, u][:], rows.rearrange("(p i) n -> p i n", i=PACK))
 
-        gather_x(0, 0, None)
-        gather_x(0, 1, None)
         gather_v(0, None)
+        gather_x(0, 0, S2 // 2)
+        gather_x(0, S2 // 2, S2 // 2)
         nc.vector.tensor_copy(
             dealt_sc[:].rearrange("p (a t m) -> p a t m", a=PASSES, t=PACK),
             placed_sc[:, S2:].rearrange("p (a m t) -> p a t m", a=PASSES, t=PACK),
         )
         gather_v(1, "picked_sc")
-        gather_x(1, 0, None)
-        wb_codes = held("wb_codes", [P, PASSES, 2 * N], U8)
-        nc.vector.tensor_copy(
-            wb_codes[:].bitcast(U16).rearrange("p a (t m) -> p a t m", t=PACK),
-            wb_raw[:].bitcast(U16).rearrange("p a (m t) -> p a t m", t=PACK),
-        )
-        gather_x(1, 1, "wb_raw")
+        gather_x(1, 0, CHUNK)
+        gather_x(1, CHUNK, CHUNK)
+        gather_x(1, 2 * CHUNK, 2 * CHUNK)
 
         tw_square = held("tw_square", [P, P], F32)
         tw_turned = held("tw_turned", [P, P], F32)
@@ -155,168 +151,191 @@ def tile_list_repurposing_mechanism_max_kernel(
         tw_bank = psum_w.tile([P, P], F32, name="tw_bank")
         nc.tensor.transpose(tw_bank[:], tw_turned[:], identity[:])
 
+        wb_codes = held("wb_codes", [P, PASSES, 2 * N], U8)
+
+        def deal_wb(a, copy):
+            copy(
+                wb_codes[:, a, :].bitcast(U16).rearrange("p (t m) -> p t m", t=PACK),
+                wb_raw[a][:].bitcast(U16).rearrange("p (m t) -> p t m", t=PACK),
+            )
+
+        deal_wb(0, nc.scalar.copy)
+        deal_wb(1, nc.vector.tensor_copy)
+        stage = held("stage", [P, wa_end - corner + 2 * wide], BF16, tag="wb_raw1")
+        wa16 = stage[:, wa_at:wa_end]
+        h_first = held("h_first", [P, 2 * wide], BF16)
+        h_front = [h_first[:], stage[:, wa_end - corner :]]
+        h_mid = held("h_mid", [P, 2 * wide], BF16)
+        h_back = stage[:, 0 : 2 * wide]
+        h16 = {}
+        for a in range(PASSES):
+            h16[0, a] = h_front[a][:, 0:wide]
+            h16[1, a] = h_front[a][:, wide:]
+            h16[2, a] = h_mid[:, a * wide : (a + 1) * wide]
+            h16[3, a] = h_back[:, a * wide : (a + 1) * wide]
+        h_codes = held("h_codes", [P, PASSES * S2], U32)
+        h_sc = held("h_sc", [P, PASSES * S2], U8)
         wa_codes = held("wa_codes", [P, PASSES * N], U32)
         wa_sc = held("wa_sc", [P, PASSES * N], U8)
-        grouped = held("wa_grouped", [P, PASSES * N * PACK], BF16)
+
+        def code_at(a, j):
+            if j < 2 * CHUNK:
+                return a * 2 * CHUNK + j
+            return PASSES * (j // CHUNK) * CHUNK + a * CHUNK + j % CHUNK
 
         def round_wa(a, u):
-            dealt = grouped[:].rearrange("p (a t m i) -> p a m t i", a=PASSES, t=PACK, i=PACK)
+            dealt = wa16.rearrange("p (a t m i) -> p a m t i", a=PASSES, t=PACK, i=PACK)
             out = dealt[:, a, u * (P // 2) : (u + 1) * (P // 2)]
             raw = wa_raw[a, u][:].rearrange("p i (m t) -> p m t i", t=PACK)
             nc.gpsimd.tensor_scalar(out, raw, 1.0, 0.0, MULT, ADD)
 
-        y_sc = held("y_sc", [P, S2], U8)
-        y_rows = out_0.rearrange("(p t) j -> p t j", t=PACK)
-        y_words = as_words(out_1[0])
-        h = [held("h%d" % a, [P, S2 * PACK], BF16) for a in range(PASSES)]
-        h_codes = [held("h_codes%d" % a, [P, S2], U32) for a in range(PASSES)]
-        h_sc = [held("h_sc%d" % a, [P, S2], U8) for a in range(PASSES)]
-
         saturated = {}
 
-        def effects(j0, w):
-            per_bank = BANK // w
-            banks = PACK // per_bank
+        def effects(c):
+            j0 = c * CHUNK
+            both = held("th%d" % c, [P, PASSES, 2, CHUNK, 2], F32, tag="wb_raw0" if c == 0 else None)
             for a in range(PASSES):
-                th = ring.tile([P, banks, w, per_bank], F32, name="th", align_bytes=64, bufs=8)
-                saturated[j0, a] = th
-                for b in range(banks):
-                    acc = psum_a.tile([P, per_bank, w], F32, name="acc")
+                th = both[:, a]
+                saturated[c, a] = th
+                for b in range(2):
+                    acc = psum.tile([P, 2, CHUNK], F32, name="acc")
                     for k in range(PASSES):
-                        for e in range(per_bank):
-                            i0 = a * PASS + (b * per_bank + e) * P
+                        for e in range(2):
+                            i0 = a * PASS + (2 * b + e) * P
                             nc.tensor.matmul_mx(
                                 out=acc[:, e, :],
                                 lhsT=v_words[k][:, i0 : i0 + P].bitcast(FP8X4),
                                 lhsT_scale=dealt_sc[TABLE_ROW + 4 * k : P, i0 : i0 + P],
-                                rhs=x_words[k, j0 // HALF][:, j0 % HALF : j0 % HALF + w].bitcast(FP8X4),
-                                rhs_scale=placed_sc[TABLE_ROW + 4 * k : P, j0 : j0 + w],
+                                rhs=x_words[k][:, j0 : j0 + CHUNK].bitcast(FP8X4),
+                                rhs_scale=placed_sc[TABLE_ROW + 4 * k : P, j0 : j0 + CHUNK],
                                 start=(k == 0 and e == 0),
-                                stop=(k == PASSES - 1 and e == per_bank - 1),
+                                stop=(k == PASSES - 1 and e == 1),
                             )
                     nc.scalar.activation(th[:, b], acc[:].rearrange("p e n -> p n e"), TANH)
 
-        def weigh(j0, w, a, first, last, engine, weights):
-            per_bank = BANK // w
-            banks = PACK // per_bank
-            th = saturated[j0, a]
+        def weigh(c, a, first, last, engine, weights):
             engine.tensor_tensor(
-                h[a][:, PACK * (j0 + first) : PACK * (j0 + last)].rearrange(
-                    "p (n b e) -> p n b e", b=banks, e=per_bank
-                ),
-                th[:, :, first:last, :].rearrange("p b n e -> p n b e"),
+                h16[c, a][:, PACK * first : PACK * last].rearrange("p (n b e) -> p n b e", b=2, e=2),
+                saturated[c, a][:, :, first:last, :].rearrange("p b n e -> p n b e"),
                 weights[:, PACK * a : PACK * (a + 1)]
-                .rearrange("p (n b e) -> p n b e", n=1, b=banks)
-                .broadcast_to([P, last - first, banks, per_bank]),
+                .rearrange("p (n b e) -> p n b e", n=1, b=2)
+                .broadcast_to([P, last - first, 2, 2]),
                 MULT,
             )
 
-        def weigh_vector(j0, w, a, first, last):
-            weigh(j0, w, a, first, last, nc.vector, tw_bank)
+        def quantise(codes, scales, values):
+            nc.vector.quantize_mx(out=codes.bitcast(FP8X4), scales=scales, in_=values)
 
-        def weigh_pool(j0, w, a, first, last):
-            weigh(j0, w, a, first, last, nc.gpsimd, tw_sb[:, 0, :])
+        def quantise_h(at, values, n):
+            quantise(h_codes[:, at : at + n], h_sc[:, at : at + n], values)
 
-        def quantise_h(j0, w):
-            cols = slice(j0, j0 + w)
-            for a in range(PASSES):
-                nc.vector.quantize_mx(
-                    out=h_codes[a][:, cols].bitcast(FP8X4),
-                    scales=h_sc[a][:, cols],
-                    in_=h[a][:, PACK * j0 : PACK * (j0 + w)],
-                )
+        yb = held("yb", [P, PACK, S2], F32)
+        y = {}
+        y_rows = out_0.rearrange("(p t) j -> p t j", t=PACK)
+        y_words = as_words(out_1[0])
 
-        def scores(j0, w, pool, tags):
+        def sums_wb(j0, w):
             per_bank = BANK // w
-            banks = PACK // per_bank
-            cols = slice(j0, j0 + w)
-            fp4_n = w if w == BANK else FP4_N
-            y = held("y%d" % j0, [P, PACK, w], F32)
-            from_wb = []
-            for b in range(banks):
-                acc_b = pool.tile([P, per_bank, w], F32, name="acc_b", tag=tags[1])
-                for e in range(per_bank):
-                    n0 = (b * per_bank + e) * P
-                    for c0 in range(0, w, fp4_n):
-                        for a in range(PASSES):
-                            nc.tensor.matmul_mx(
-                                out=acc_b[:, e, c0 : c0 + fp4_n],
-                                lhsT=wb_codes[:, a, 2 * n0 : 2 * (n0 + P)].bitcast(FP4X4),
-                                lhsT_scale=dealt_sc[:, a * N + n0 : a * N + n0 + P],
-                                rhs=h_codes[a][:, j0 + c0 : j0 + c0 + fp4_n].bitcast(FP8X4),
-                                rhs_scale=h_sc[a][:, j0 + c0 : j0 + c0 + fp4_n],
-                                start=(a == 0),
-                                stop=(a == PASSES - 1),
-                            )
-                yb = held("yb%d_%d" % (j0, b), [P, per_bank, w], F32)
-                nc.scalar.copy(yb[:], acc_b[:])
-                from_wb.append(yb)
-            for b in range(banks):
-                acc_a = pool.tile([P, per_bank, w], F32, name="acc_a", tag=tags[0])
+            for b in range(PACK // per_bank):
+                acc = psum.tile([P, per_bank, w], F32, name="acc")
                 for e in range(per_bank):
                     n0 = (b * per_bank + e) * P
                     for a in range(PASSES):
+                        at = code_at(a, j0)
                         nc.tensor.matmul_mx(
-                            out=acc_a[:, e, :],
+                            out=acc[:, e, :],
+                            lhsT=wb_codes[:, a, 2 * n0 : 2 * (n0 + P)].bitcast(FP4X4),
+                            lhsT_scale=dealt_sc[:, a * N + n0 : a * N + n0 + P],
+                            rhs=h_codes[:, at : at + w].bitcast(FP8X4),
+                            rhs_scale=h_sc[:, at : at + w],
+                            start=(a == 0),
+                            stop=(a == PASSES - 1),
+                        )
+                nc.scalar.copy(yb[:, b * per_bank : (b + 1) * per_bank, j0 : j0 + w], acc[:])
+
+        def sums_wa(j0, w):
+            per_bank = BANK // w
+            y[j0] = held("y%d" % j0, [P, PACK, w], F32)
+            for b in range(PACK // per_bank):
+                acc = psum.tile([P, per_bank, w], F32, name="acc")
+                for e in range(per_bank):
+                    n0 = (b * per_bank + e) * P
+                    for a in range(PASSES):
+                        at = code_at(a, j0)
+                        nc.tensor.matmul_mx(
+                            out=acc[:, e, :],
                             lhsT=wa_codes[:, a * N + n0 : a * N + n0 + P].bitcast(FP8X4),
                             lhsT_scale=wa_sc[:, a * N + n0 : a * N + n0 + P],
-                            rhs=h_codes[a][:, cols].bitcast(FP8X4),
-                            rhs_scale=h_sc[a][:, cols],
+                            rhs=h_codes[:, at : at + w].bitcast(FP8X4),
+                            rhs_scale=h_sc[:, at : at + w],
                             start=(a == 0),
                             stop=(a == PASSES - 1),
                         )
                 rows = slice(b * per_bank, (b + 1) * per_bank)
-                nc.vector.tensor_tensor(y[:, rows, :], acc_a[:], from_wb[b][:], MAX)
-                if b % 2 == 1 or banks == 1:
-                    done = slice(max(b - 1, 0) * per_bank, (b + 1) * per_bank)
-                    nc.sync.dma_start(y_rows[:, done, cols], y[:, done, :])
-            return y
+                nc.vector.tensor_tensor(y[j0][:, rows, :], acc[:], yb[:, rows, j0 : j0 + w], MAX)
+            nc.sync.dma_start(y_rows[:, :, j0 : j0 + w], y[j0][:])
+
+        y_codes = held("y_codes", [P, S2], U32)
+        y_sc = held("y_sc", [P, S2], U8)
+        y16 = [held("y16_0", [P, wide], BF16)]
+
+        def round_y(j0, out, copy):
+            copy(
+                out.rearrange("p (c i t) -> p c t i", i=4, t=PACK), y[j0][:].rearrange("p t (c i) -> p c t i", i=4)
+            )
 
         def pool_copy(out, in_):
             order = "p c t i -> p c i t"
             nc.gpsimd.tensor_scalar(out.rearrange(order), in_.rearrange(order), 1.0, 0.0, MULT, ADD)
 
-        def planes(j0, w, y, copies):
-            for c0, copy in zip(range(0, w, WIDE), copies):
-                n = min(w, WIDE)
-                y16 = ring.tile([P, n * PACK], BF16, name="y16", align_bytes=64, bufs=5)
-                copy(
-                    y16[:].rearrange("p (c i t) -> p c t i", i=4, t=PACK),
-                    y[:, :, c0 : c0 + n].rearrange("p t (c i) -> p c t i", i=4),
-                )
-                cols = slice(j0 + c0, j0 + c0 + n)
-                nc.vector.quantize_mx(out=y_codes[:, cols].bitcast(FP8X4), scales=y_sc[:, cols], in_=y16[:])
+        def quantise_y(j0, w, values):
+            quantise(y_codes[:, j0 : j0 + w], y_sc[:, j0 : j0 + w], values)
+
+        def store_words(j0, w):
             nc.sync.dma_start(y_words[:, j0 : j0 + w], y_codes[:, j0 : j0 + w].bitcast(I32))
 
+        for c in range(4):
+            effects(c)
+        round_wa(0, 0)
+        round_wa(0, 1)
+        round_wa(1, 0)
+        for c in range(2):
+            for a in range(PASSES):
+                weigh(c, a, 0, CHUNK, nc.vector, tw_bank)
         for a in range(PASSES):
-            for u in range(2):
-                round_wa(a, u)
-        effects(0, 256)
-        effects(256, 256)
-        effects(512, 256)
-        effects(768, 256)
-        for j0 in (0, 256):
-            for a in range(PASSES):
-                weigh_vector(j0, 256, a, 0, 256)
-        quantise_h(0, 512)
-        nc.vector.quantize_mx(out=wa_codes[:].bitcast(FP8X4), scales=wa_sc[:], in_=grouped[:])
-        for first in (0, 128):
-            for a in range(PASSES):
-                weigh_pool(768, 256, a, first, first + 128)
-        weigh_vector(512, 256, 0, 0, 256)
-        weigh_vector(512, 256, 1, 0, 256)
-        quantise_h(512, 256)
-        y0 = scores(0, 512, psum_a, ("acc", "acc"))
-        quantise_h(768, 128)
-        quantise_h(896, 128)
-        y1 = scores(512, 256, psum_a, ("acc", "acc"))
-        y2 = scores(768, 128, psum_a, ("acc", "acc"))
-        y3 = scores(896, 128, psum_a, ("acc", "acc"))
-        y_codes = held("y_codes", [P, S2], U32, tag="yb768_0")
-        planes(0, 512, y0, [nc.scalar.copy, pool_copy])
-        planes(512, 256, y1, [nc.scalar.copy])
-        planes(768, 128, y2, [nc.scalar.copy])
-        planes(896, 128, y3, [nc.vector.tensor_copy])
+            quantise_h(a * 2 * CHUNK, h_front[a], 2 * CHUNK)
+        round_wa(1, 1)
+        for a in range(PASSES):
+            weigh(2, a, 0, CHUNK, nc.vector, tw_bank)
+        for a in range(PASSES):
+            quantise_h(code_at(a, 2 * CHUNK), h16[2, a], CHUNK)
+        quantise(wa_codes[:], wa_sc[:], wa16)
+        weigh(3, 0, 0, CHUNK, nc.vector, tw_bank)
+        weigh(3, 1, CHUNK - POOL_SHARE, CHUNK, nc.gpsimd, tw_sb[:, 0, :])
+        weigh(3, 1, 0, CHUNK - POOL_SHARE, nc.vector, tw_bank)
+        sums_wb(0, 2 * CHUNK)
+        sums_wb(2 * CHUNK, CHUNK)
+        sums_wa(0, CHUNK)
+        quantise_h(code_at(0, 3 * CHUNK), h_back, 2 * CHUNK)
+        sums_wa(CHUNK, CHUNK)
+        sums_wa(2 * CHUNK, CHUNK)
+        round_y(0, y16[0][:], nc.scalar.copy)
+        sums_wb(3 * CHUNK, CHUNK)
+        quantise_y(0, CHUNK, y16[0][:])
+        sums_wa(3 * CHUNK, CHUNK // 2)
+        sums_wa(3 * CHUNK + CHUNK // 2, CHUNK // 2)
+        y16.append(held("y16_1", [P, wide], BF16, tag="wb_codes"))
+        round_y(CHUNK, y16[1][:], nc.scalar.copy)
+        y16.append(held("y16_2", [P, wide], BF16, tag="y16_0"))
+        y16.append(held("y16_3", [P, wide], BF16))
+        round_y(2 * CHUNK, y16[2][:], pool_copy)
+        round_y(3 * CHUNK, y16[3][:, 0 : wide // 2], nc.scalar.copy)
+        quantise_y(CHUNK, CHUNK, y16[1][:])
+        store_words(0, 2 * CHUNK)
+        round_y(3 * CHUNK + CHUNK // 2, y16[3][:, wide // 2 :], nc.vector.tensor_copy)
+        quantise_y(2 * CHUNK, CHUNK, y16[2][:])
+        quantise_y(3 * CHUNK, CHUNK, y16[3][:])
+        store_words(2 * CHUNK, 2 * CHUNK)
         for q in range(4):
             queue = nc.sync if q % 2 == 0 else nc.scalar
             queue.dma_start(out_2[0, 4 * q : 4 * q + 4, :].bitcast(I32), y_sc[32 * q : 32 * q + 4, :].bitcast(I32))

@@ -37,6 +37,7 @@ def tile_list_repurposing_mechanism_max_kernel(
     nc = tc.nc
     with ExitStack() as ctx:
         keep = ctx.enter_context(tc.tile_pool(name="keep", bufs=1))
+        laid = ctx.enter_context(tc.tile_pool(name="laid", bufs=1))
         psum = ctx.enter_context(tc.psum_pool(name="psum", bufs=7))
         psum_w = ctx.enter_context(tc.psum_pool(name="psum_w", bufs=1))
 
@@ -82,7 +83,7 @@ def tile_list_repurposing_mechanism_max_kernel(
             return lst[:, j0 // 16 : (j0 + n) // 16]
 
         v_words = [held("v_words%d" % k, [P, S], U32) for k in range(PASSES)]
-        x_words = [held("x_words%d" % k, [P, S2], U32) for k in range(PASSES)]
+        x_words = {}
 
         def gather_v(k, tag):
             picked = held("v_picked%d" % k, [P, S], U32, tag=tag)
@@ -96,8 +97,11 @@ def tile_list_repurposing_mechanism_max_kernel(
                     picked[:, a * PASS : (a + 1) * PASS].rearrange("p (c i t) -> p c t i", t=PACK, i=4),
                 )
 
-        def gather_x(k, j0, n):
-            nc.vector.tensor_copy(x_words[k][:, j0 : j0 + n], x_table[k][:].indirect(entries(list_x, j0, n)))
+        def gather_x(k, j0, n, at=None):
+            picked = keep.tile([P, n], U32, name="x_words%d_%d" % (k, j0), align_bytes=64) if at is None else at
+            nc.vector.tensor_copy(picked[:], x_table[k][:].indirect(entries(list_x, j0, n)))
+            for c0 in range(0, n, CHUNK):
+                x_words[k, (j0 + c0) // CHUNK] = picked[:, c0 : c0 + CHUNK]
 
         def place_rows(a, q):
             row = 32 * q + TABLE_ROW + 4 * a
@@ -117,7 +121,11 @@ def tile_list_repurposing_mechanism_max_kernel(
         corner = PACK * P // 2
         wa_at = wide + PACK * (CHUNK - POOL_SHARE)
         wa_end = wa_at + PASSES * N * PACK
-        wb_raw = [held("wb_raw%d" % a, [P, 2 * N], U8) for a in range(PASSES)]
+        th_bytes = PASSES * wide * 4
+        wb_raw = [
+            laid.tile([P, 2 * N], U8, name="wb_raw0", align_bytes=64, offset=th_bytes - N),
+            held("wb_raw1", [P, 2 * N], U8),
+        ]
         for a in range(PASSES):
             nc.sync.dma_start(wb_raw[a][:].bitcast(I32), wb_words[a].bitcast(I32))
         wa_raw = {}
@@ -137,7 +145,6 @@ def tile_list_repurposing_mechanism_max_kernel(
         gather_v(1, "picked_sc")
         gather_x(1, 0, CHUNK)
         gather_x(1, CHUNK, CHUNK)
-        gather_x(1, 2 * CHUNK, 2 * CHUNK)
 
         tw_square = held("tw_square", [P, P], F32)
         tw_turned = held("tw_turned", [P, P], F32)
@@ -161,7 +168,9 @@ def tile_list_repurposing_mechanism_max_kernel(
 
         deal_wb(0, nc.scalar.copy)
         deal_wb(1, nc.vector.tensor_copy)
-        stage = held("stage", [P, wa_end - corner + 2 * wide], BF16, tag="wb_raw1")
+        late = laid.tile([P, 2 * CHUNK], U32, name="x_words_late", align_bytes=64, offset=th_bytes)
+        gather_x(1, 2 * CHUNK, 2 * CHUNK, late)
+        stage = held("stage", [P, wa_end - corner + 2 * wide], BF16)
         wa16 = stage[:, wa_at:wa_end]
         h_first = held("h_first", [P, 2 * wide], BF16)
         h_front = [h_first[:], stage[:, wa_end - corner :]]
@@ -193,7 +202,10 @@ def tile_list_repurposing_mechanism_max_kernel(
 
         def effects(c):
             j0 = c * CHUNK
-            both = held("th%d" % c, [P, PASSES, 2, CHUNK, 2], F32, tag="wb_raw0" if c == 0 else None)
+            if c == 0:
+                both = laid.tile([P, PASSES, 2, CHUNK, 2], F32, name="th0", align_bytes=64, offset=0)
+            else:
+                both = held("th%d" % c, [P, PASSES, 2, CHUNK, 2], F32)
             for a in range(PASSES):
                 th = both[:, a]
                 saturated[c, a] = th
@@ -206,7 +218,7 @@ def tile_list_repurposing_mechanism_max_kernel(
                                 out=acc[:, e, :],
                                 lhsT=v_words[k][:, i0 : i0 + P].bitcast(FP8X4),
                                 lhsT_scale=dealt_sc[TABLE_ROW + 4 * k : P, i0 : i0 + P],
-                                rhs=x_words[k][:, j0 : j0 + CHUNK].bitcast(FP8X4),
+                                rhs=x_words[k, c].bitcast(FP8X4),
                                 rhs_scale=placed_sc[TABLE_ROW + 4 * k : P, j0 : j0 + CHUNK],
                                 start=(k == 0 and e == 0),
                                 stop=(k == PASSES - 1 and e == 1),

@@ -85,12 +85,12 @@ def tile_list_repurposing_mechanism_max_kernel(
         v_words = [held("v_words%d" % k, [P, S], U32) for k in range(PASSES)]
         x_words = {}
 
-        def gather_v(k, tag):
-            picked = held("v_picked%d" % k, [P, S], U32, tag=tag)
-            for a in range(PASSES):
-                nc.vector.tensor_copy(
-                    picked[:, a * PASS : (a + 1) * PASS], v_table[k][:].indirect(entries(list_v, a * PASS, PASS))
-                )
+        def gather_v(k, picked, a):
+            nc.vector.tensor_copy(
+                picked[:, a * PASS : (a + 1) * PASS], v_table[k][:].indirect(entries(list_v, a * PASS, PASS))
+            )
+
+        def deal_v(k, picked):
             for a in range(PASSES):
                 nc.vector.tensor_copy(
                     v_words[k][:, a * PASS : (a + 1) * PASS].rearrange("p (t c i) -> p c t i", t=PACK, i=4),
@@ -135,14 +135,20 @@ def tile_list_repurposing_mechanism_max_kernel(
                 rows = wa[a * PASS : (a + 1) * PASS, u * (N // 2) : (u + 1) * (N // 2)]
                 nc.sync.dma_start(wa_raw[a, u][:], rows.rearrange("(p i) n -> p i n", i=PACK))
 
-        gather_v(0, None)
+        v_first = held("v_picked0", [P, S], U32)
+        for a in range(PASSES):
+            gather_v(0, v_first, a)
+        deal_v(0, v_first)
         gather_x(0, 0, S2 // 2)
         gather_x(0, S2 // 2, S2 // 2)
+        v_second = held("v_picked1", [P, S], U32, tag="picked_sc")
+        gather_v(1, v_second, 0)
         nc.vector.tensor_copy(
             dealt_sc[:].rearrange("p (a t m) -> p a t m", a=PASSES, t=PACK),
             placed_sc[:, S2:].rearrange("p (a m t) -> p a t m", a=PASSES, t=PACK),
         )
-        gather_v(1, "picked_sc")
+        gather_v(1, v_second, 1)
+        deal_v(1, v_second)
         gather_x(1, 0, CHUNK)
         gather_x(1, CHUNK, CHUNK)
 
@@ -330,20 +336,21 @@ def tile_list_repurposing_mechanism_max_kernel(
         sums_wa(0, CHUNK)
         quantise_h(code_at(0, 3 * CHUNK), h_back, 2 * CHUNK)
         sums_wa(CHUNK, CHUNK)
-        sums_wa(2 * CHUNK, CHUNK)
         round_y(0, y16[0][:], nc.scalar.copy)
-        sums_wb(3 * CHUNK, CHUNK)
         quantise_y(0, CHUNK, y16[0][:])
+        store_words(0, CHUNK)
+        y16.append(held("y16_1", [P, wide], BF16, tag="y16_0"))
+        round_y(CHUNK, y16[1][:], pool_copy)
+        sums_wa(2 * CHUNK, CHUNK)
+        sums_wb(3 * CHUNK, CHUNK)
         sums_wa(3 * CHUNK, CHUNK // 2)
         sums_wa(3 * CHUNK + CHUNK // 2, CHUNK // 2)
-        y16.append(held("y16_1", [P, wide], BF16, tag="wb_codes"))
-        round_y(CHUNK, y16[1][:], nc.scalar.copy)
-        y16.append(held("y16_2", [P, wide], BF16, tag="y16_0"))
+        y16.append(held("y16_2", [P, wide], BF16, tag="wb_codes"))
         y16.append(held("y16_3", [P, wide], BF16))
-        round_y(2 * CHUNK, y16[2][:], pool_copy)
+        round_y(2 * CHUNK, y16[2][:], nc.scalar.copy)
         round_y(3 * CHUNK, y16[3][:, 0 : wide // 2], nc.scalar.copy)
         quantise_y(CHUNK, CHUNK, y16[1][:])
-        store_words(0, 2 * CHUNK)
+        store_words(CHUNK, CHUNK)
         round_y(3 * CHUNK + CHUNK // 2, y16[3][:, wide // 2 :], nc.vector.tensor_copy)
         quantise_y(2 * CHUNK, CHUNK, y16[2][:])
         quantise_y(3 * CHUNK, CHUNK, y16[3][:])

@@ -28,6 +28,7 @@ CHUNK = 256
 TABLE_ROW = 4
 WHOLE_AT = 96
 POOL_SHARE = 192
+POOL_PART = (3, 1)
 QUADRANTS = (0, 2, 1, 3)
 
 
@@ -139,15 +140,14 @@ def tile_list_repurposing_mechanism_max_kernel(
         for a in range(PASSES):
             gather_v(0, v_first, a)
         deal_v(0, v_first)
-        gather_x(0, 0, S2 // 2)
-        gather_x(0, S2 // 2, S2 // 2)
-        v_second = held("v_picked1", [P, S], U32, tag="picked_sc")
-        gather_v(1, v_second, 0)
+        gather_x(0, 0, S2)
         nc.vector.tensor_copy(
             dealt_sc[:].rearrange("p (a t m) -> p a t m", a=PASSES, t=PACK),
             placed_sc[:, S2:].rearrange("p (a m t) -> p a t m", a=PASSES, t=PACK),
         )
-        gather_v(1, v_second, 1)
+        v_second = held("v_picked1", [P, S], U32, tag="picked_sc")
+        for a in range(PASSES):
+            gather_v(1, v_second, a)
         deal_v(1, v_second)
         gather_x(1, 0, CHUNK)
         gather_x(1, CHUNK, CHUNK)
@@ -163,6 +163,9 @@ def tile_list_repurposing_mechanism_max_kernel(
         nc.scalar.copy(tw_turned[:], turning[:])
         tw_bank = psum_w.tile([P, P], F32, name="tw_bank")
         nc.tensor.transpose(tw_bank[:], tw_turned[:], identity[:])
+
+        tw_long = held("tw_long", [P, POOL_SHARE, PACK], F32)
+        nc.scalar.copy(tw_long[:], tw_sb[:, :, PACK:].broadcast_to([P, POOL_SHARE, PACK]))
 
         wb_codes = held("wb_codes", [P, PASSES, 2 * N], U8)
 
@@ -215,21 +218,25 @@ def tile_list_repurposing_mechanism_max_kernel(
             for a in range(PASSES):
                 th = both[:, a]
                 saturated[c, a] = th
+                slots = PACK if (c, a) == POOL_PART else 2
+                w = BANK // slots
                 for b in range(2):
-                    acc = psum.tile([P, 2, CHUNK], F32, name="acc")
+                    acc = psum.tile([P, slots, w], F32, name="acc")
+                    col = b * w % CHUNK
                     for k in range(PASSES):
-                        for e in range(2):
-                            i0 = a * PASS + (2 * b + e) * P
+                        for e in range(slots):
+                            i0 = a * PASS + (slots * b + e) % PACK * P
                             nc.tensor.matmul_mx(
                                 out=acc[:, e, :],
                                 lhsT=v_words[k][:, i0 : i0 + P].bitcast(FP8X4),
                                 lhsT_scale=dealt_sc[TABLE_ROW + 4 * k : P, i0 : i0 + P],
-                                rhs=x_words[k, c].bitcast(FP8X4),
-                                rhs_scale=placed_sc[TABLE_ROW + 4 * k : P, j0 : j0 + CHUNK],
+                                rhs=x_words[k, c][:, col : col + w].bitcast(FP8X4),
+                                rhs_scale=placed_sc[TABLE_ROW + 4 * k : P, j0 + col : j0 + col + w],
                                 start=(k == 0 and e == 0),
-                                stop=(k == PASSES - 1 and e == 1),
+                                stop=(k == PASSES - 1 and e == slots - 1),
                             )
-                    nc.scalar.activation(th[:, b], acc[:].rearrange("p e n -> p n e"), TANH)
+                    out = th[:, b].rearrange("p n e -> p (n e)").rearrange("p (n e) -> p n e", e=slots)
+                    nc.scalar.activation(out, acc[:].rearrange("p e n -> p n e"), TANH)
 
         def weigh(c, a, first, last, engine, weights):
             engine.tensor_tensor(
@@ -239,6 +246,14 @@ def tile_list_repurposing_mechanism_max_kernel(
                 .rearrange("p (n b e) -> p n b e", n=1, b=2)
                 .broadcast_to([P, last - first, 2, 2]),
                 MULT,
+            )
+
+        def weigh_last(first, last, engine, weights):
+            cols = slice(PACK * first, PACK * last)
+            values = saturated[POOL_PART].rearrange("p b n e -> p (b n e)")[:, cols]
+            by_column = "p (n t) -> p n t"
+            engine.tensor_tensor(
+                h16[POOL_PART][:, cols].rearrange(by_column, t=PACK), values.rearrange(by_column, t=PACK), weights, MULT
             )
 
         def quantise(codes, scales, values):
@@ -329,8 +344,9 @@ def tile_list_repurposing_mechanism_max_kernel(
             quantise_h(code_at(a, 2 * CHUNK), h16[2, a], CHUNK)
         quantise(wa_codes[:], wa_sc[:], wa16)
         weigh(3, 0, 0, CHUNK, nc.vector, tw_bank)
-        weigh(3, 1, CHUNK - POOL_SHARE, CHUNK, nc.gpsimd, tw_sb[:, 0, :])
-        weigh(3, 1, 0, CHUNK - POOL_SHARE, nc.vector, tw_bank)
+        weigh_last(CHUNK - POOL_SHARE, CHUNK, nc.gpsimd, tw_long[:])
+        rest = CHUNK - POOL_SHARE
+        weigh_last(0, rest, nc.vector, tw_bank[:, PACK : 2 * PACK].unsqueeze(1).broadcast_to([P, rest, PACK]))
         sums_wb(0, 2 * CHUNK)
         sums_wb(2 * CHUNK, CHUNK)
         sums_wa(0, CHUNK)
@@ -350,11 +366,11 @@ def tile_list_repurposing_mechanism_max_kernel(
         round_y(2 * CHUNK, y16[2][:], nc.scalar.copy)
         round_y(3 * CHUNK, y16[3][:, 0 : wide // 2], nc.scalar.copy)
         quantise_y(CHUNK, CHUNK, y16[1][:])
-        store_words(CHUNK, CHUNK)
         round_y(3 * CHUNK + CHUNK // 2, y16[3][:, wide // 2 :], nc.vector.tensor_copy)
         quantise_y(2 * CHUNK, CHUNK, y16[2][:])
+        store_words(CHUNK, 2 * CHUNK)
         quantise_y(3 * CHUNK, CHUNK, y16[3][:])
-        store_words(2 * CHUNK, 2 * CHUNK)
+        store_words(3 * CHUNK, CHUNK)
         for q in range(4):
             queue = nc.sync if q % 2 == 0 else nc.scalar
             queue.dma_start(out_2[0, 4 * q : 4 * q + 4, :].bitcast(I32), y_sc[32 * q : 32 * q + 4, :].bitcast(I32))

@@ -29,7 +29,6 @@ TABLE_ROW = 4
 WHOLE_AT = 96
 POOL_SHARE = 192
 POOL_PART = (3, 1)
-QUADRANTS = (0, 2, 1, 3)
 
 
 def tile_list_repurposing_mechanism_max_kernel(
@@ -74,10 +73,10 @@ def tile_list_repurposing_mechanism_max_kernel(
         nc.sync.dma_start(x_table_sc[WHOLE_AT:P, :].bitcast(I32), tab2_scales.rearrange("a q t -> (a q) t").bitcast(I32))
         nc.sync.dma_start(v_table[0][:].bitcast(I32), as_words(tab_words[0]))
         nc.sync.dma_start(x_table[0][:].bitcast(I32), as_words(tab2_words[0]))
-        for q in QUADRANTS:
+        for r in range(4):
             nc.sync.dma_start(
-                placed_sc[32 * q : 32 * q + 4, S2:].rearrange("r (a n) -> r a n", a=PASSES).bitcast(I32),
-                wb_scales[:, 4 * q : 4 * q + 4, :].rearrange("a r n -> r a n").bitcast(I32),
+                placed_sc[r:P:32, S2:].rearrange("q (a n) -> q a n", a=PASSES).bitcast(I32),
+                wb_scales[:, r:16:4, :].rearrange("a q n -> q a n").bitcast(I32),
             )
 
         def entries(lst, j0, n):
@@ -104,24 +103,24 @@ def tile_list_repurposing_mechanism_max_kernel(
             for c0 in range(0, n, CHUNK):
                 x_words[k, (j0 + c0) // CHUNK] = picked[:, c0 : c0 + CHUNK]
 
-        def place_rows(a, q):
-            row = 32 * q + TABLE_ROW + 4 * a
-            src = WHOLE_AT + 16 * a + 4 * q
-            nc.sync.dma_start(placed_sc[row : row + 4, :].bitcast(I32), picked_sc[src : src + 4, :].bitcast(I32))
+        def place_rows(a, r):
+            row = TABLE_ROW + 4 * a + r
+            src = WHOLE_AT + 16 * a + r
+            nc.sync.dma_start(placed_sc[row:P:32, :].bitcast(I32), picked_sc[src : src + 13 : 4, :].bitcast(I32))
 
         nc.vector.tensor_copy(picked_sc[:, S2:], v_table_sc[:].indirect(list_v[:]))
         nc.vector.tensor_copy(picked_sc[:, 0:S2], x_table_sc[:].indirect(list_x[:]))
-        blocks = [(a, q + 2 * half) for q in range(2) for a in range(PASSES) for half in range(2)]
-        for a, q in blocks[:2]:
-            place_rows(a, q)
+        blocks = [(a, r) for r in range(4) for a in range(PASSES)]
+        for a, r in blocks[:2]:
+            place_rows(a, r)
         nc.sync.dma_start(v_table[1][:].bitcast(I32), as_words(tab_words[1]))
-        for a, q in blocks[2:]:
-            place_rows(a, q)
+        for a, r in blocks[2:]:
+            place_rows(a, r)
         nc.sync.dma_start(x_table[1][:].bitcast(I32), as_words(tab2_words[1]))
         wide = PACK * CHUNK
         corner = PACK * P // 2
         wa_at = wide + PACK * (CHUNK - POOL_SHARE)
-        wa_end = wa_at + PASSES * N * PACK
+        wa_end = wa_at + N * PACK
         th_bytes = PASSES * wide * 4
         wb_raw = [
             laid.tile([P, 2 * N], U8, name="wb_raw0", align_bytes=64, offset=th_bytes - N),
@@ -180,7 +179,8 @@ def tile_list_repurposing_mechanism_max_kernel(
         late = laid.tile([P, 2 * CHUNK], U32, name="x_words_late", align_bytes=64, offset=th_bytes)
         gather_x(1, 2 * CHUNK, 2 * CHUNK, late)
         stage = held("stage", [P, wa_end - corner + 2 * wide], BF16)
-        wa16 = stage[:, wa_at:wa_end]
+        wa_first = held("wa_first", [P, N * PACK], BF16)
+        wa16 = [wa_first[:], stage[:, wa_at:wa_end]]
         h_first = held("h_first", [P, 2 * wide], BF16)
         h_front = [h_first[:], stage[:, wa_end - corner :]]
         h_mid = held("h_mid", [P, 2 * wide], BF16)
@@ -193,7 +193,7 @@ def tile_list_repurposing_mechanism_max_kernel(
             h16[3, a] = h_back[:, a * wide : (a + 1) * wide]
         h_codes = held("h_codes", [P, PASSES * S2], U32)
         h_sc = held("h_sc", [P, PASSES * S2], U8)
-        wa_codes = held("wa_codes", [P, PASSES * N], U32)
+        wa_codes = {}
         wa_sc = held("wa_sc", [P, PASSES * N], U8)
 
         def code_at(a, j):
@@ -202,8 +202,8 @@ def tile_list_repurposing_mechanism_max_kernel(
             return PASSES * (j // CHUNK) * CHUNK + a * CHUNK + j % CHUNK
 
         def round_wa(a, u):
-            dealt = wa16.rearrange("p (a t m i) -> p a m t i", a=PASSES, t=PACK, i=PACK)
-            out = dealt[:, a, u * (P // 2) : (u + 1) * (P // 2)]
+            dealt = wa16[a].rearrange("p (t m i) -> p m t i", t=PACK, i=PACK)
+            out = dealt[:, u * (P // 2) : (u + 1) * (P // 2)]
             raw = wa_raw[a, u][:].rearrange("p i (m t) -> p m t i", t=PACK)
             nc.gpsimd.tensor_scalar(out, raw, 1.0, 0.0, MULT, ADD)
 
@@ -262,6 +262,10 @@ def tile_list_repurposing_mechanism_max_kernel(
         def quantise_h(at, values, n):
             quantise(h_codes[:, at : at + n], h_sc[:, at : at + n], values)
 
+        def quantise_wa(a, tag):
+            wa_codes[a] = held("wa_codes%d" % a, [P, N], U32, tag=tag)
+            quantise(wa_codes[a][:], wa_sc[:, a * N : (a + 1) * N], wa16[a])
+
         yb = held("yb", [P, PACK, S2], F32)
         y = {}
         y_rows = out_0.rearrange("(p t) j -> p t j", t=PACK)
@@ -286,27 +290,46 @@ def tile_list_repurposing_mechanism_max_kernel(
                         )
                 nc.scalar.copy(yb[:, b * per_bank : (b + 1) * per_bank, j0 : j0 + w], acc[:])
 
-        def sums_wa(j0, w):
+        def passes_wa(acc, b, a, j0, w):
+            per_bank = BANK // w
+            at = code_at(a, j0)
+            for e in range(per_bank):
+                n0 = (b * per_bank + e) * P
+                nc.tensor.matmul_mx(
+                    out=acc[:, e, :],
+                    lhsT=wa_codes[a][:, n0 : n0 + P].bitcast(FP8X4),
+                    lhsT_scale=wa_sc[:, a * N + n0 : a * N + n0 + P],
+                    rhs=h_codes[:, at : at + w].bitcast(FP8X4),
+                    rhs_scale=h_sc[:, at : at + w],
+                    start=(a == 0 and e == 0),
+                    stop=(a == PASSES - 1 and e == per_bank - 1),
+                )
+
+        def open_wa(j0, w):
+            per_bank = BANK // w
+            banks = [psum.tile([P, per_bank, w], F32, name="acc") for b in range(PACK // per_bank)]
+            for b, acc in enumerate(banks):
+                passes_wa(acc, b, 0, j0, w)
+            return banks
+
+        def close_wa(j0, w, banks, between=None):
             per_bank = BANK // w
             y[j0] = held("y%d" % j0, [P, PACK, w], F32)
             for b in range(PACK // per_bank):
-                acc = psum.tile([P, per_bank, w], F32, name="acc")
-                for e in range(per_bank):
-                    n0 = (b * per_bank + e) * P
-                    for a in range(PASSES):
-                        at = code_at(a, j0)
-                        nc.tensor.matmul_mx(
-                            out=acc[:, e, :],
-                            lhsT=wa_codes[:, a * N + n0 : a * N + n0 + P].bitcast(FP8X4),
-                            lhsT_scale=wa_sc[:, a * N + n0 : a * N + n0 + P],
-                            rhs=h_codes[:, at : at + w].bitcast(FP8X4),
-                            rhs_scale=h_sc[:, at : at + w],
-                            start=(a == 0),
-                            stop=(a == PASSES - 1),
-                        )
+                if banks:
+                    acc = banks[b]
+                else:
+                    acc = psum.tile([P, per_bank, w], F32, name="acc")
+                    passes_wa(acc, b, 0, j0, w)
+                passes_wa(acc, b, 1, j0, w)
                 rows = slice(b * per_bank, (b + 1) * per_bank)
                 nc.vector.tensor_tensor(y[j0][:, rows, :], acc[:], yb[:, rows, j0 : j0 + w], MAX)
-            nc.sync.dma_start(y_rows[:, :, j0 : j0 + w], y[j0][:])
+                nc.sync.dma_start(y_rows[:, rows, j0 : j0 + w], y[j0][:, rows, :])
+                if between and b == 0:
+                    between()
+
+        def sums_wa(j0, w):
+            close_wa(j0, w, None)
 
         y_codes = held("y_codes", [P, S2], U32)
         y_sc = held("y_sc", [P, S2], U8)
@@ -335,21 +358,23 @@ def tile_list_repurposing_mechanism_max_kernel(
         for c in range(2):
             for a in range(PASSES):
                 weigh(c, a, 0, CHUNK, nc.vector, tw_bank)
-        for a in range(PASSES):
-            quantise_h(a * 2 * CHUNK, h_front[a], 2 * CHUNK)
+        quantise_h(0, h_front[0], 2 * CHUNK)
+        quantise_wa(0, "th1")
+        quantise_h(2 * CHUNK, h_front[1], 2 * CHUNK)
         round_wa(1, 1)
         for a in range(PASSES):
             weigh(2, a, 0, CHUNK, nc.vector, tw_bank)
         for a in range(PASSES):
             quantise_h(code_at(a, 2 * CHUNK), h16[2, a], CHUNK)
-        quantise(wa_codes[:], wa_sc[:], wa16)
+        quantise_wa(1, None)
         weigh(3, 0, 0, CHUNK, nc.vector, tw_bank)
         weigh_last(CHUNK - POOL_SHARE, CHUNK, nc.gpsimd, tw_long[:])
         rest = CHUNK - POOL_SHARE
         weigh_last(0, rest, nc.vector, tw_bank[:, PACK : 2 * PACK].unsqueeze(1).broadcast_to([P, rest, PACK]))
         sums_wb(0, 2 * CHUNK)
+        opened = open_wa(0, CHUNK)
         sums_wb(2 * CHUNK, CHUNK)
-        sums_wa(0, CHUNK)
+        close_wa(0, CHUNK, opened)
         quantise_h(code_at(0, 3 * CHUNK), h_back, 2 * CHUNK)
         sums_wa(CHUNK, CHUNK)
         round_y(0, y16[0][:], nc.scalar.copy)

@@ -54,15 +54,16 @@ def tile_list_repurposing_mechanism_max_kernel(
         v_table_sc = held("v_table_sc", [P, T], U8)
         x_table_sc = held("x_table_sc", [P, T2], U8)
         picked_sc = held("picked_sc", [P, S2 + S], U8)
-        placed_sc = held("placed_sc", [P, S2 + S], U8)
-        dealt_sc = held("dealt_sc", [P, S], U8)
+        placed_sc = [held("placed_sc%d" % k, [P, S2 + S], U8) for k in range(PASSES)]
+        dealt_sc = [held("dealt_sc%d" % k, [P, S], U8) for k in range(PASSES)]
         tw_sb = held("tw_sb", [P, 1, PASSES * PACK], F32)
         identity = held("identity", [P, P], F32)
 
+        nc.gpsimd.memset(placed_sc[0][:].bitcast(I32), 0)
         make_identity(nc, identity[:])
-        nc.vector.memset(placed_sc[:].bitcast(I32), 0)
         for plane in (v_table_sc, x_table_sc):
             nc.vector.memset(plane[0:WHOLE_AT, :].bitcast(I32), 0)
+        nc.gpsimd.memset(placed_sc[1][:].bitcast(I32), 0)
 
         nc.gpsimd.dma_start(
             tw_sb[:, 0, :].rearrange("p (a t) -> p a t", a=PASSES), tw.rearrange("(a p t) -> p a t", a=PASSES, t=PACK)
@@ -72,12 +73,12 @@ def tile_list_repurposing_mechanism_max_kernel(
         nc.sync.dma_start(list_x[:], offs2)
         nc.sync.dma_start(x_table_sc[WHOLE_AT:P, :].bitcast(I32), tab2_scales.rearrange("a q t -> (a q) t").bitcast(I32))
         nc.sync.dma_start(v_table[0][:].bitcast(I32), as_words(tab_words[0]))
-        nc.sync.dma_start(x_table[0][:].bitcast(I32), as_words(tab2_words[0]))
         for r in range(4):
             nc.sync.dma_start(
-                placed_sc[r:P:32, S2:].rearrange("q (a n) -> q a n", a=PASSES).bitcast(I32),
+                placed_sc[0][r:P:32, S2:].rearrange("q (a n) -> q a n", a=PASSES).bitcast(I32),
                 wb_scales[:, r:16:4, :].rearrange("a q n -> q a n").bitcast(I32),
             )
+        nc.sync.dma_start(x_table[0][:].bitcast(I32), as_words(tab2_words[0]))
 
         def entries(lst, j0, n):
             return lst[:, j0 // 16 : (j0 + n) // 16]
@@ -103,19 +104,26 @@ def tile_list_repurposing_mechanism_max_kernel(
             for c0 in range(0, n, CHUNK):
                 x_words[k, (j0 + c0) // CHUNK] = picked[:, c0 : c0 + CHUNK]
 
+        def deal_scales(k):
+            nc.vector.tensor_copy(
+                dealt_sc[k][:].rearrange("p (a t m) -> p a t m", a=PASSES, t=PACK),
+                placed_sc[k][:, S2:].rearrange("p (a m t) -> p a t m", a=PASSES, t=PACK),
+            )
+
         def place_rows(a, r):
             row = TABLE_ROW + 4 * a + r
             src = WHOLE_AT + 16 * a + r
-            nc.sync.dma_start(placed_sc[row:P:32, :].bitcast(I32), picked_sc[src : src + 13 : 4, :].bitcast(I32))
+            nc.sync.dma_start(placed_sc[a][row:P:32, :].bitcast(I32), picked_sc[src : src + 13 : 4, :].bitcast(I32))
 
         nc.vector.tensor_copy(picked_sc[:, S2:], v_table_sc[:].indirect(list_v[:]))
         nc.vector.tensor_copy(picked_sc[:, 0:S2], x_table_sc[:].indirect(list_x[:]))
-        blocks = [(a, r) for r in range(4) for a in range(PASSES)]
-        for a, r in blocks[:2]:
-            place_rows(a, r)
+        for r in range(4):
+            place_rows(0, r)
+            if r < 2:
+                place_rows(1, r)
         nc.sync.dma_start(v_table[1][:].bitcast(I32), as_words(tab_words[1]))
-        for a, r in blocks[2:]:
-            place_rows(a, r)
+        for r in range(2, 4):
+            place_rows(1, r)
         nc.sync.dma_start(x_table[1][:].bitcast(I32), as_words(tab2_words[1]))
         wide = PACK * CHUNK
         corner = PACK * P // 2
@@ -140,13 +148,11 @@ def tile_list_repurposing_mechanism_max_kernel(
             gather_v(0, v_first, a)
         deal_v(0, v_first)
         gather_x(0, 0, S2)
-        nc.vector.tensor_copy(
-            dealt_sc[:].rearrange("p (a t m) -> p a t m", a=PASSES, t=PACK),
-            placed_sc[:, S2:].rearrange("p (a m t) -> p a t m", a=PASSES, t=PACK),
-        )
-        v_second = held("v_picked1", [P, S], U32, tag="picked_sc")
+        deal_scales(0)
+        v_second = held("v_picked1", [P, S], U32)
         for a in range(PASSES):
             gather_v(1, v_second, a)
+        deal_scales(1)
         deal_v(1, v_second)
         gather_x(1, 0, CHUNK)
         gather_x(1, CHUNK, CHUNK)
@@ -229,9 +235,9 @@ def tile_list_repurposing_mechanism_max_kernel(
                             nc.tensor.matmul_mx(
                                 out=acc[:, e, :],
                                 lhsT=v_words[k][:, i0 : i0 + P].bitcast(FP8X4),
-                                lhsT_scale=dealt_sc[TABLE_ROW + 4 * k : P, i0 : i0 + P],
+                                lhsT_scale=dealt_sc[k][TABLE_ROW + 4 * k : P, i0 : i0 + P],
                                 rhs=x_words[k, c][:, col : col + w].bitcast(FP8X4),
-                                rhs_scale=placed_sc[TABLE_ROW + 4 * k : P, j0 + col : j0 + col + w],
+                                rhs_scale=placed_sc[k][TABLE_ROW + 4 * k : P, j0 + col : j0 + col + w],
                                 start=(k == 0 and e == 0),
                                 stop=(k == PASSES - 1 and e == slots - 1),
                             )
@@ -282,7 +288,7 @@ def tile_list_repurposing_mechanism_max_kernel(
                         nc.tensor.matmul_mx(
                             out=acc[:, e, :],
                             lhsT=wb_codes[:, a, 2 * n0 : 2 * (n0 + P)].bitcast(FP4X4),
-                            lhsT_scale=dealt_sc[:, a * N + n0 : a * N + n0 + P],
+                            lhsT_scale=dealt_sc[0][:, a * N + n0 : a * N + n0 + P],
                             rhs=h_codes[:, at : at + w].bitcast(FP8X4),
                             rhs_scale=h_sc[:, at : at + w],
                             start=(a == 0),
@@ -370,11 +376,11 @@ def tile_list_repurposing_mechanism_max_kernel(
         weigh(3, 0, 0, CHUNK, nc.vector, tw_bank)
         weigh_last(CHUNK - POOL_SHARE, CHUNK, nc.gpsimd, tw_long[:])
         rest = CHUNK - POOL_SHARE
-        weigh_last(0, rest, nc.vector, tw_bank[:, PACK : 2 * PACK].unsqueeze(1).broadcast_to([P, rest, PACK]))
+        rest_weights = tw_bank[:, PACK : 2 * PACK].unsqueeze(1).broadcast_to([P, rest, PACK])
         sums_wb(0, 2 * CHUNK)
         opened = open_wa(0, CHUNK)
         sums_wb(2 * CHUNK, CHUNK)
-        close_wa(0, CHUNK, opened)
+        close_wa(0, CHUNK, opened, lambda: weigh_last(0, rest, nc.vector, rest_weights))
         quantise_h(code_at(0, 3 * CHUNK), h_back, 2 * CHUNK)
         sums_wa(CHUNK, CHUNK)
         round_y(0, y16[0][:], nc.scalar.copy)

@@ -207,11 +207,13 @@ def tile_list_repurposing_mechanism_max_kernel(
                 return a * 2 * CHUNK + j
             return PASSES * (j // CHUNK) * CHUNK + a * CHUNK + j % CHUNK
 
-        def round_wa(a, u):
+        def wa_views(a, u, first, last):
             dealt = wa16[a].rearrange("p (t m i) -> p m t i", t=PACK, i=PACK)
-            out = dealt[:, u * (P // 2) : (u + 1) * (P // 2)]
-            raw = wa_raw[a, u][:].rearrange("p i (m t) -> p m t i", t=PACK)
-            nc.gpsimd.tensor_scalar(out, raw, 1.0, 0.0, MULT, ADD)
+            out = dealt[:, u * (P // 2) + first : u * (P // 2) + last]
+            return out, wa_raw[a, u][:].rearrange("p i (m t) -> p m t i", t=PACK)[:, first:last]
+
+        def round_wa(a, u, last=P // 2):
+            nc.gpsimd.tensor_scalar(*wa_views(a, u, 0, last), 1.0, 0.0, MULT, ADD)
 
         saturated = {}
 
@@ -356,11 +358,14 @@ def tile_list_repurposing_mechanism_max_kernel(
         def store_words(j0, w):
             nc.sync.dma_start(y_words[:, j0 : j0 + w], y_codes[:, j0 : j0 + w].bitcast(I32))
 
-        for c in range(4):
-            effects(c)
+        effects(0)
+        effects(1)
+        nc.scalar.copy(*wa_views(1, 0, P // 4, P // 2))
+        effects(2)
+        effects(3)
         round_wa(0, 0)
         round_wa(0, 1)
-        round_wa(1, 0)
+        round_wa(1, 0, P // 4)
         for c in range(2):
             for a in range(PASSES):
                 weigh(c, a, 0, CHUNK, nc.vector, tw_bank)

@@ -147,12 +147,14 @@ def tile_list_repurposing_mechanism_max_kernel(
         for a in range(PASSES):
             gather_v(0, v_first, a)
         deal_v(0, v_first)
-        gather_x(0, 0, S2)
+        gather_x(0, 0, CHUNK)
+        gather_x(0, 2 * CHUNK, 2 * CHUNK)
         deal_scales(0)
         v_second = held("v_picked1", [P, S], U32)
         for a in range(PASSES):
             gather_v(1, v_second, a)
         deal_scales(1)
+        gather_x(0, CHUNK, CHUNK, held("x_words0_second", [P, CHUNK], U32, tag="v_table1"))
         deal_v(1, v_second)
         gather_x(1, 0, CHUNK)
         gather_x(1, CHUNK, CHUNK)

@@ -63,11 +63,8 @@ def tile_list_repurposing_mechanism_max_kernel(
         make_identity(nc, identity[:])
         for plane in (v_table_sc, x_table_sc):
             nc.vector.memset(plane[0:WHOLE_AT, :].bitcast(I32), 0)
-        nc.gpsimd.memset(placed_sc[1][:].bitcast(I32), 0)
+        nc.vector.memset(placed_sc[1][:].bitcast(I32), 0)
 
-        nc.gpsimd.dma_start(
-            tw_sb[:, 0, :].rearrange("p (a t) -> p a t", a=PASSES), tw.rearrange("(a p t) -> p a t", a=PASSES, t=PACK)
-        )
         nc.sync.dma_start(list_v[:], offs)
         nc.sync.dma_start(v_table_sc[WHOLE_AT:P, :].bitcast(I32), tab_scales.rearrange("a q t -> (a q) t").bitcast(I32))
         nc.sync.dma_start(list_x[:], offs2)
@@ -78,6 +75,9 @@ def tile_list_repurposing_mechanism_max_kernel(
                 placed_sc[0][r:P:32, S2:].rearrange("q (a n) -> q a n", a=PASSES).bitcast(I32),
                 wb_scales[:, r:16:4, :].rearrange("a q n -> q a n").bitcast(I32),
             )
+        nc.sync.dma_start(
+            tw_sb[:, 0, :].rearrange("p (a t) -> p a t", a=PASSES), tw.rearrange("(a p t) -> p a t", a=PASSES, t=PACK)
+        )
         nc.sync.dma_start(x_table[0][:].bitcast(I32), as_words(tab2_words[0]))
 
         def entries(lst, j0, n):

@@ -27,7 +27,7 @@ BANK = 512
 CHUNK = 256
 TABLE_ROW = 4
 WHOLE_AT = 96
-POOL_SHARE = 192
+POOL_SHARE = 224
 POOL_PART = (3, 1)
 
 
@@ -186,11 +186,9 @@ def tile_list_repurposing_mechanism_max_kernel(
         deal_wb(1, nc.vector.tensor_copy)
         late = laid.tile([P, 2 * CHUNK], U32, name="x_words_late", align_bytes=64, offset=th_bytes)
         gather_x(1, 2 * CHUNK, 2 * CHUNK, late)
-        stage = held("stage", [P, wa_end - corner + 2 * wide], BF16)
-        wa_first = held("wa_first", [P, N * PACK], BF16)
-        wa16 = [wa_first[:], stage[:, wa_at:wa_end]]
-        h_first = held("h_first", [P, 2 * wide], BF16)
-        h_front = [h_first[:], stage[:, wa_end - corner :]]
+        stage = held("stage", [P, wa_end - corner + N * PACK], BF16)
+        wa16 = [stage[:, wa_end - corner :], stage[:, wa_at:wa_end]]
+        h_front = [held("h_front%d" % a, [P, 2 * wide], BF16)[:] for a in range(PASSES)]
         h_mid = held("h_mid", [P, 2 * wide], BF16)
         h_back = stage[:, 0 : 2 * wide]
         h16 = {}
@@ -372,8 +370,8 @@ def tile_list_repurposing_mechanism_max_kernel(
             for a in range(PASSES):
                 weigh(c, a, 0, CHUNK, nc.vector, tw_bank)
         quantise_h(0, h_front[0], 2 * CHUNK)
-        quantise_wa(0, "th1")
         quantise_h(2 * CHUNK, h_front[1], 2 * CHUNK)
+        quantise_wa(0, "th1")
         round_wa(1, 1)
         for a in range(PASSES):
             weigh(2, a, 0, CHUNK, nc.vector, tw_bank)

@@ -384,8 +384,8 @@ def tile_list_repurposing_mechanism_max_kernel(
         rest_weights = tw_bank[:, PACK : 2 * PACK].unsqueeze(1).broadcast_to([P, rest, PACK])
         sums_wb(0, 2 * CHUNK)
         opened = open_wa(0, CHUNK)
-        sums_wb(2 * CHUNK, CHUNK)
         close_wa(0, CHUNK, opened, lambda: weigh_last(0, rest, nc.vector, rest_weights))
+        sums_wb(2 * CHUNK, CHUNK)
         quantise_h(code_at(0, 3 * CHUNK), h_back, 2 * CHUNK)
         sums_wa(CHUNK, CHUNK)
         round_y(0, y16[0][:], nc.scalar.copy)

from contextlib import ExitStack

import concourse.mybir as mybir
from concourse.masks import make_identity

K, T, S, T2, S2, N = 1024, 2048, 1024, 4096, 1024, 512
FLOPS = 2 * K * S * S2 + 2 * 2 * S * N * S2

F32 = mybir.dt.float32
BF16 = mybir.dt.bfloat16
I32 = mybir.dt.int32
U32 = mybir.dt.uint32
U16 = mybir.dt.uint16
U8 = mybir.dt.uint8
FP8X4 = mybir.dt.float8_e4m3fn_x4
FP4X4 = mybir.dt.float4_e2m1fn_x4
TANH = mybir.ActivationFunctionType.Tanh
MULT = mybir.AluOpType.mult
MAX = mybir.AluOpType.max
ADD = mybir.AluOpType.add

P = 128
PACK = 4
PASS = P * PACK
PASSES = 2
BANK = 512
CHUNK = 256
TABLE_ROW = 4
WHOLE_AT = 96
POOL_SHARE = 224
POOL_PART = (3, 1)


def tile_list_repurposing_mechanism_max_kernel(
    tc, tab_words, tab_scales, tab2_words, tab2_scales, offs, offs2, tw, wa, wb_words, wb_scales, out_0, out_1, out_2
):
    nc = tc.nc
    with ExitStack() as ctx:
        keep = ctx.enter_context(tc.tile_pool(name="keep", bufs=1))
        laid = ctx.enter_context(tc.tile_pool(name="laid", bufs=1))
        psum = ctx.enter_context(tc.psum_pool(name="psum", bufs=7))
        psum_w = ctx.enter_context(tc.psum_pool(name="psum_w", bufs=1))

        def held(name, shape, dtype, tag=None):
            return keep.tile(shape, dtype, name=name, tag=tag or name, align_bytes=64)

        def as_words(packed):
            return packed.rearrange("p t i -> p (t i)").bitcast(I32)

        list_v = held("list_v", [P, S // 16], U16)
        list_x = held("list_x", [P, S2 // 16], U16)
        v_table = [held("v_table%d" % k, [P, T], U32) for k in range(PASSES)]
        x_table = [held("x_table%d" % k, [P, T2], U32) for k in range(PASSES)]
        v_table_sc = held("v_table_sc", [P, T], U8)
        x_table_sc = held("x_table_sc", [P, T2], U8)
        picked_sc = held("picked_sc", [P, S2 + S], U8)
        placed_sc = [held("placed_sc%d" % k, [P, S2 + S], U8) for k in range(PASSES)]
        dealt_sc = [held("dealt_sc%d" % k, [P, S], U8) for k in range(PASSES)]
        tw_sb = held("tw_sb", [P, 1, PASSES * PACK], F32)
        identity = held("identity", [P, P], F32)

        nc.gpsimd.memset(placed_sc[0][:].bitcast(I32), 0)
        make_identity(nc, identity[:])
        for plane in (v_table_sc, x_table_sc):
            nc.vector.memset(plane[0:WHOLE_AT, :].bitcast(I32), 0)
        nc.vector.memset(placed_sc[1][:].bitcast(I32), 0)

        nc.sync.dma_start(list_v[:], offs)
        nc.sync.dma_start(v_table_sc[WHOLE_AT:P, :].bitcast(I32), tab_scales.rearrange("a q t -> (a q) t").bitcast(I32))
        nc.sync.dma_start(list_x[:], offs2)
        nc.sync.dma_start(x_table_sc[WHOLE_AT:P, :].bitcast(I32), tab2_scales.rearrange("a q t -> (a q) t").bitcast(I32))
        nc.sync.dma_start(v_table[0][:].bitcast(I32), as_words(tab_words[0]))
        for r in range(4):
            nc.sync.dma_start(
                placed_sc[0][r:P:32, S2:].rearrange("q (a n) -> q a n", a=PASSES).bitcast(I32),
                wb_scales[:, r:16:4, :].rearrange("a q n -> q a n").bitcast(I32),
            )
        nc.sync.dma_start(
            tw_sb[:, 0, :].rearrange("p (a t) -> p a t", a=PASSES), tw.rearrange("(a p t) -> p a t", a=PASSES, t=PACK)
        )
        nc.sync.dma_start(x_table[0][:].bitcast(I32), as_words(tab2_words[0]))

        def entries(lst, j0, n):
            return lst[:, j0 // 16 : (j0 + n) // 16]

        v_words = [held("v_words%d" % k, [P, S], U32) for k in range(PASSES)]
        x_words = {}

        def gather_v(k, picked, a):
            nc.vector.tensor_copy(
                picked[:, a * PASS : (a + 1) * PASS], v_table[k][:].indirect(entries(list_v, a * PASS, PASS))
            )

        def deal_v(k, picked):
            for a in range(PASSES):
                nc.vector.tensor_copy(
                    v_words[k][:, a * PASS : (a + 1) * PASS].rearrange("p (t c i) -> p c t i", t=PACK, i=4),
                    picked[:, a * PASS : (a + 1) * PASS].rearrange("p (c i t) -> p c t i", t=PACK, i=4),
                )

        def gather_x(k, j0, n, at=None):
            picked = keep.tile([P, n], U32, name="x_words%d_%d" % (k, j0), align_bytes=64) if at is None else at
            nc.vector.tensor_copy(picked[:], x_table[k][:].indirect(entries(list_x, j0, n)))
            for c0 in range(0, n, CHUNK):
                x_words[k, (j0 + c0) // CHUNK] = picked[:, c0 : c0 + CHUNK]

        def deal_scales(k):
            nc.vector.tensor_copy(
                dealt_sc[k][:].rearrange("p (a t m) -> p a t m", a=PASSES, t=PACK),
                placed_sc[k][:, S2:].rearrange("p (a m t) -> p a t m", a=PASSES, t=PACK),
            )

        def place_rows(a, r):
            row = TABLE_ROW + 4 * a + r
            src = WHOLE_AT + 16 * a + r
            nc.sync.dma_start(placed_sc[a][row:P:32, :].bitcast(I32), picked_sc[src : src + 13 : 4, :].bitcast(I32))

        nc.vector.tensor_copy(picked_sc[:, S2:], v_table_sc[:].indirect(list_v[:]))
        nc.vector.tensor_copy(picked_sc[:, 0:S2], x_table_sc[:].indirect(list_x[:]))
        for r in range(4):
            place_rows(0, r)
            if r < 2:
                place_rows(1, r)
        nc.sync.dma_start(v_table[1][:].bitcast(I32), as_words(tab_words[1]))
        for r in range(2, 4):
            place_rows(1, r)
        nc.sync.dma_start(x_table[1][:].bitcast(I32), as_words(tab2_words[1]))
        wide = PACK * CHUNK
        corner = PACK * P // 2
        wa_at = wide + PACK * (CHUNK - POOL_SHARE)
        wa_end = wa_at + N * PACK
        th_bytes = PASSES * wide * 4
        wb_raw = [
            laid.tile([P, 2 * N], U8, name="wb_raw0", align_bytes=64, offset=th_bytes - N),
            held("wb_raw1", [P, 2 * N], U8),
        ]
        for a in range(PASSES):
            nc.sync.dma_start(wb_raw[a][:].bitcast(I32), wb_words[a].bitcast(I32))
        wa_raw = {}
        for a in range(PASSES):
            for u in range(2):
                wa_raw[a, u] = held("wa_raw%d%d" % (a, u), [P, PACK, N // 2], F32)
                rows = wa[a * PASS : (a + 1) * PASS, u * (N // 2) : (u + 1) * (N // 2)]
                nc.sync.dma_start(wa_raw[a, u][:], rows.rearrange("(p i) n -> p i n", i=PACK))

        v_first = held("v_picked0", [P, S], U32)
        for a in range(PASSES):
            gather_v(0, v_first, a)
        deal_v(0, v_first)
        gather_x(0, 0, CHUNK)
        gather_x(0, 2 * CHUNK, 2 * CHUNK)
        deal_scales(0)
        v_second = held("v_picked1", [P, S], U32)
        for a in range(PASSES):
            gather_v(1, v_second, a)
        deal_scales(1)
        gather_x(0, CHUNK, CHUNK, held("x_words0_second", [P, CHUNK], U32, tag="v_table1"))
        deal_v(1, v_second)
        gather_x(1, 0, CHUNK)
        gather_x(1, CHUNK, CHUNK)

        tw_square = held("tw_square", [P, P], F32)
        tw_turned = held("tw_turned", [P, P], F32)
        repeats = P // (PASSES * PACK)
        nc.scalar.copy(
            tw_square[:].rearrange("p (r c) -> p r c", r=repeats), tw_sb[:].broadcast_to([P, repeats, PASSES * PACK])
        )
        turning = psum_w.tile([P, P], F32, name="turning", tag="tw_bank")
        nc.tensor.transpose(turning[:], tw_square[:], identity[:])
        nc.scalar.copy(tw_turned[:], turning[:])
        tw_bank = psum_w.tile([P, P], F32, name="tw_bank")
        nc.tensor.transpose(tw_bank[:], tw_turned[:], identity[:])

        tw_long = held("tw_long", [P, POOL_SHARE, PACK], F32)
        nc.scalar.copy(tw_long[:], tw_sb[:, :, PACK:].broadcast_to([P, POOL_SHARE, PACK]))

        wb_codes = held("wb_codes", [P, PASSES, 2 * N], U8)

        def deal_wb(a, copy):
            copy(
                wb_codes[:, a, :].bitcast(U16).rearrange("p (t m) -> p t m", t=PACK),
                wb_raw[a][:].bitcast(U16).rearrange("p (m t) -> p t m", t=PACK),
            )

        deal_wb(0, nc.scalar.copy)
        deal_wb(1, nc.vector.tensor_copy)
        late = laid.tile([P, 2 * CHUNK], U32, name="x_words_late", align_bytes=64, offset=th_bytes)
        gather_x(1, 2 * CHUNK, 2 * CHUNK, late)
        stage = held("stage", [P, wa_end - corner + N * PACK], BF16)
        wa16 = [stage[:, wa_end - corner :], stage[:, wa_at:wa_end]]
        h_front = [held("h_front%d" % a, [P, 2 * wide], BF16)[:] for a in range(PASSES)]
        h_mid = held("h_mid", [P, 2 * wide], BF16)
        h_back = stage[:, 0 : 2 * wide]
        h16 = {}
        for a in range(PASSES):
            h16[0, a] = h_front[a][:, 0:wide]
            h16[1, a] = h_front[a][:, wide:]
            h16[2, a] = h_mid[:, a * wide : (a + 1) * wide]
            h16[3, a] = h_back[:, a * wide : (a + 1) * wide]
        h_codes = held("h_codes", [P, PASSES * S2], U32)
        h_sc = held("h_sc", [P, PASSES * S2], U8)
        wa_codes = {}
        wa_sc = held("wa_sc", [P, PASSES * N], U8)

        def code_at(a, j):
            if j < 2 * CHUNK:
                return a * 2 * CHUNK + j
            return PASSES * (j // CHUNK) * CHUNK + a * CHUNK + j % CHUNK

        def wa_views(a, u, first, last):
            dealt = wa16[a].rearrange("p (t m i) -> p m t i", t=PACK, i=PACK)
            out = dealt[:, u * (P // 2) + first : u * (P // 2) + last]
            return out, wa_raw[a, u][:].rearrange("p i (m t) -> p m t i", t=PACK)[:, first:last]

        def round_wa(a, u, last=P // 2):
            nc.gpsimd.tensor_scalar(*wa_views(a, u, 0, last), 1.0, 0.0, MULT, ADD)

        saturated = {}

        def effects(c):
            j0 = c * CHUNK
            if c == 0:
                both = laid.tile([P, PASSES, 2, CHUNK, 2], F32, name="th0", align_bytes=64, offset=0)
            else:
                both = held("th%d" % c, [P, PASSES, 2, CHUNK, 2], F32)
            for a in range(PASSES):
                th = both[:, a]
                saturated[c, a] = th
                slots = PACK if (c, a) == POOL_PART else 2
                w = BANK // slots
                for b in range(2):
                    acc = psum.tile([P, slots, w], F32, name="acc")
                    col = b * w % CHUNK
                    for k in range(PASSES):
                        for e in range(slots):
                            i0 = a * PASS + (slots * b + e) % PACK * P
                            nc.tensor.matmul_mx(
                                out=acc[:, e, :],
                                lhsT=v_words[k][:, i0 : i0 + P].bitcast(FP8X4),
                                lhsT_scale=dealt_sc[k][TABLE_ROW + 4 * k : P, i0 : i0 + P],
                                rhs=x_words[k, c][:, col : col + w].bitcast(FP8X4),
                                rhs_scale=placed_sc[k][TABLE_ROW + 4 * k : P, j0 + col : j0 + col + w],
                                start=(k == 0 and e == 0),
                                stop=(k == PASSES - 1 and e == slots - 1),
                            )
                    out = th[:, b].rearrange("p n e -> p (n e)").rearrange("p (n e) -> p n e", e=slots)
                    nc.scalar.activation(out, acc[:].rearrange("p e n -> p n e"), TANH)

        def weigh(c, a, first, last, engine, weights):
            engine.tensor_tensor(
                h16[c, a][:, PACK * first : PACK * last].rearrange("p (n b e) -> p n b e", b=2, e=2),
                saturated[c, a][:, :, first:last, :].rearrange("p b n e -> p n b e"),
                weights[:, PACK * a : PACK * (a + 1)]
                .rearrange("p (n b e) -> p n b e", n=1, b=2)
                .broadcast_to([P, last - first, 2, 2]),
                MULT,
            )

        def weigh_last(first, last, engine, weights):
            cols = slice(PACK * first, PACK * last)
            values = saturated[POOL_PART].rearrange("p b n e -> p (b n e)")[:, cols]
            by_column = "p (n t) -> p n t"
            engine.tensor_tensor(
                h16[POOL_PART][:, cols].rearrange(by_column, t=PACK), values.rearrange(by_column, t=PACK), weights, MULT
            )

        def quantise(codes, scales, values):
            nc.vector.quantize_mx(out=codes.bitcast(FP8X4), scales=scales, in_=values)

        def quantise_h(at, values, n):
            quantise(h_codes[:, at : at + n], h_sc[:, at : at + n], values)

        def quantise_wa(a, tag):
            wa_codes[a] = held("wa_codes%d" % a, [P, N], U32, tag=tag)
            quantise(wa_codes[a][:], wa_sc[:, a * N : (a + 1) * N], wa16[a])

        yb = held("yb", [P, PACK, S2], F32)
        y = {}
        y_rows = out_0.rearrange("(p t) j -> p t j", t=PACK)
        y_words = as_words(out_1[0])

        def sums_wb(j0, w):
            per_bank = BANK // w
            for b in range(PACK // per_bank):
                acc = psum.tile([P, per_bank, w], F32, name="acc")
                for e in range(per_bank):
                    n0 = (b * per_bank + e) * P
                    for a in range(PASSES):
                        at = code_at(a, j0)
                        nc.tensor.matmul_mx(
                            out=acc[:, e, :],
                            lhsT=wb_codes[:, a, 2 * n0 : 2 * (n0 + P)].bitcast(FP4X4),
                            lhsT_scale=dealt_sc[0][:, a * N + n0 : a * N + n0 + P],
                            rhs=h_codes[:, at : at + w].bitcast(FP8X4),
                            rhs_scale=h_sc[:, at : at + w],
                            start=(a == 0),
                            stop=(a == PASSES - 1),
                        )
                nc.scalar.copy(yb[:, b * per_bank : (b + 1) * per_bank, j0 : j0 + w], acc[:])

        def passes_wa(acc, b, a, j0, w):
            per_bank = BANK // w
            at = code_at(a, j0)
            for e in range(per_bank):
                n0 = (b * per_bank + e) * P
                nc.tensor.matmul_mx(
                    out=acc[:, e, :],
                    lhsT=wa_codes[a][:, n0 : n0 + P].bitcast(FP8X4),
                    lhsT_scale=wa_sc[:, a * N + n0 : a * N + n0 + P],
                    rhs=h_codes[:, at : at + w].bitcast(FP8X4),
                    rhs_scale=h_sc[:, at : at + w],
                    start=(a == 0 and e == 0),
                    stop=(a == PASSES - 1 and e == per_bank - 1),
                )

        def open_wa(j0, w):
            per_bank = BANK // w
            banks = [psum.tile([P, per_bank, w], F32, name="acc") for b in range(PACK // per_bank)]
            for b, acc in enumerate(banks):
                passes_wa(acc, b, 0, j0, w)
            return banks

        def close_wa(j0, w, banks, between=None):
            per_bank = BANK // w
            y[j0] = held("y%d" % j0, [P, PACK, w], F32)
            for b in range(PACK // per_bank):
                if banks:
                    acc = banks[b]
                else:
                    acc = psum.tile([P, per_bank, w], F32, name="acc")
                    passes_wa(acc, b, 0, j0, w)
                passes_wa(acc, b, 1, j0, w)
                rows = slice(b * per_bank, (b + 1) * per_bank)
                nc.vector.tensor_tensor(y[j0][:, rows, :], acc[:], yb[:, rows, j0 : j0 + w], MAX)
                nc.sync.dma_start(y_rows[:, rows, j0 : j0 + w], y[j0][:, rows, :])
                if between and b == 0:
                    between()

        def sums_wa(j0, w):
            close_wa(j0, w, None)

        y_codes = held("y_codes", [P, S2], U32)
        y_sc = held("y_sc", [P, S2], U8)
        y16 = [held("y16_0", [P, wide], BF16)]

        def round_y(j0, out, copy):
            copy(
                out.rearrange("p (c i t) -> p c t i", i=4, t=PACK), y[j0][:].rearrange("p t (c i) -> p c t i", i=4)
            )

        def pool_copy(out, in_):
            order = "p c t i -> p c i t"
            nc.gpsimd.tensor_scalar(out.rearrange(order), in_.rearrange(order), 1.0, 0.0, MULT, ADD)

        def quantise_y(j0, w, values):
            quantise(y_codes[:, j0 : j0 + w], y_sc[:, j0 : j0 + w], values)

        def store_words(j0, w):
            nc.sync.dma_start(y_words[:, j0 : j0 + w], y_codes[:, j0 : j0 + w].bitcast(I32))

        effects(0)
        effects(1)
        nc.scalar.copy(*wa_views(1, 0, P // 4, P // 2))
        effects(2)
        effects(3)
        round_wa(0, 0)
        round_wa(0, 1)
        round_wa(1, 0, P // 4)
        for c in range(2):
            for a in range(PASSES):
                weigh(c, a, 0, CHUNK, nc.vector, tw_bank)
        quantise_h(0, h_front[0], 2 * CHUNK)
        quantise_h(2 * CHUNK, h_front[1], 2 * CHUNK)
        quantise_wa(0, "th1")
        round_wa(1, 1)
        for a in range(PASSES):
            weigh(2, a, 0, CHUNK, nc.vector, tw_bank)
        for a in range(PASSES):
            quantise_h(code_at(a, 2 * CHUNK), h16[2, a], CHUNK)
        quantise_wa(1, None)
        weigh(3, 0, 0, CHUNK, nc.vector, tw_bank)
        weigh_last(CHUNK - POOL_SHARE, CHUNK, nc.gpsimd, tw_long[:])
        rest = CHUNK - POOL_SHARE
        rest_weights = tw_bank[:, PACK : 2 * PACK].unsqueeze(1).broadcast_to([P, rest, PACK])
        sums_wb(0, 2 * CHUNK)
        opened = open_wa(0, CHUNK)
        close_wa(0, CHUNK, opened, lambda: weigh_last(0, rest, nc.vector, rest_weights))
        sums_wb(2 * CHUNK, CHUNK)
        quantise_h(code_at(0, 3 * CHUNK), h_back, 2 * CHUNK)
        sums_wa(CHUNK, CHUNK)
        round_y(0, y16[0][:], nc.scalar.copy)
        quantise_y(0, CHUNK, y16[0][:])
        store_words(0, CHUNK)
        y16.append(held("y16_1", [P, wide], BF16, tag="y16_0"))
        round_y(CHUNK, y16[1][:], pool_copy)
        sums_wa(2 * CHUNK, CHUNK)
        sums_wb(3 * CHUNK, CHUNK)
        sums_wa(3 * CHUNK, CHUNK // 2)
        sums_wa(3 * CHUNK + CHUNK // 2, CHUNK // 2)
        y16.append(held("y16_2", [P, wide], BF16, tag="wb_codes"))
        y16.append(held("y16_3", [P, wide], BF16))
        round_y(2 * CHUNK, y16[2][:], nc.scalar.copy)
        round_y(3 * CHUNK, y16[3][:, 0 : wide // 2], nc.scalar.copy)
        quantise_y(CHUNK, CHUNK, y16[1][:])
        round_y(3 * CHUNK + CHUNK // 2, y16[3][:, wide // 2 :], nc.vector.tensor_copy)
        quantise_y(2 * CHUNK, CHUNK, y16[2][:])
        store_words(CHUNK, 2 * CHUNK)
        quantise_y(3 * CHUNK, CHUNK, y16[3][:])
        store_words(3 * CHUNK, CHUNK)
        for q in range(4):
            queue = nc.sync if q % 2 == 0 else nc.scalar
            queue.dma_start(out_2[0, 4 * q : 4 * q + 4, :].bitcast(I32), y_sc[32 * q : 32 * q + 4, :].bitcast(I32))
